import numpy as np
import ml_dtypes


def mxq(x, axis, fmt="e4m3"):
    dtype, down = {"e4m3": (ml_dtypes.float8_e4m3fn, 7), "e5m2": (ml_dtypes.float8_e5m2, 14)}[fmt]
    v = np.moveaxis(np.asarray(x, np.float32).astype(ml_dtypes.bfloat16).astype(np.float64), axis, -1)
    blocks = v.reshape(v.shape[:-1] + (-1, 32))
    amax = np.abs(blocks).max(-1, keepdims=True)
    byte = np.maximum(np.where(amax > 0, np.frexp(amax)[1] - 1 + 127, 0) - down, 1)
    scale = np.exp2(byte - 127.0)
    codes = (blocks / scale).astype(np.float32).astype(dtype).astype(np.float64)
    return np.moveaxis((codes * scale).reshape(v.shape), -1, axis)


WIDE = False


def mx_kscale(k):
    if not WIDE:
        return np.ones(k)
    levels = np.array([10, -10, 5, -5, 0])
    if k % 512:
        return np.exp2(np.random.permutation(np.resize(levels, k // 32))).repeat(32)
    a = np.empty((k // 512, 16))
    for p in range(k // 512):
        a[p, :8] = np.random.permutation(np.resize(levels, 8))
        for g in range(8):
            far = levels[np.abs(levels - a[p, g]) >= 10]
            a[p, g + 8] = far[np.random.randint(len(far))]
    return np.exp2(a.ravel()).repeat(32)


BF16 = ml_dtypes.bfloat16


def bf(x):
    return np.asarray(x, np.float32).astype(BF16)


def f64(x):
    return np.asarray(x).astype(np.float64)


E2M1 = np.array([0.0, 0.5, 1.0, 1.5, 2.0, 3.0, 4.0, 6.0, -0.0, -0.5, -1.0, -1.5, -2.0, -3.0, -4.0, -6.0])


def pack_weight(w, fmt):
    k, n = w.shape
    w = f64(bf(w)).reshape(k // 32, 32, n)
    amax = np.abs(w).max(1)
    if fmt == "e4m3":
        byte = np.frexp(amax)[1] - 1 + 127 - 7
    else:
        mant, ex = np.frexp(amax / 6.0)
        byte = np.where(mant > 0.5, ex, ex - 1) + 127
    byte = np.clip(np.where(amax > 0, byte, 1), 1, 254)
    scaled = (w * np.exp2(127.0 - byte)[:, None, :]).reshape(k, n).astype(np.float32)
    by_word = np.ascontiguousarray(scaled.reshape(k // 512, 128, 4, n).transpose(0, 1, 3, 2))
    if fmt == "e4m3":
        words = by_word.astype(ml_dtypes.float8_e4m3fn).view(np.uint8)
    else:
        c = by_word.astype(ml_dtypes.float4_e2m1fn).view(np.uint8) & 0xF
        words = c[..., 0::2] | (c[..., 1::2] << 4)
    return np.ascontiguousarray(words), np.ascontiguousarray(byte.astype(np.uint8).reshape(k // 512, 16, n))


def unpack_weight(words, scales, fmt):
    g, p, n, _ = words.shape
    if fmt == "e4m3":
        vals = np.ascontiguousarray(words).view(ml_dtypes.float8_e4m3fn).astype(np.float64)
    else:
        nib = np.empty((g, p, n, 4), np.uint8)
        nib[..., 0::2] = words & 0xF
        nib[..., 1::2] = words >> 4
        vals = E2M1[nib]
    vals = vals * np.repeat(np.exp2(scales.astype(np.float64) - 127.0), 8, axis=1)[..., None]
    return vals.transpose(0, 1, 3, 2).reshape(g * 512, n)
def pack4(w):
    words, scales = pack_weight(w, "e2m1")
    return words.reshape(words.shape[0], 128, -1), scales


def unpack4(words, scales):
    return unpack_weight(words.reshape(words.shape[0], 128, -1, 2), scales, "e2m1")


T, A, B = 1536, 1024, 1024

SUM_GAIN, DIFF_GAIN = 0.8, 0.3


def draw0():
    s = mx_kscale(A)
    u = mx_kscale(T)
    wd = DIFF_GAIN * np.random.standard_normal((A, B)) / np.sqrt(A) / s[:, None]
    wd_words, wd_scales = pack4(wd)
    return {"x": bf(np.random.standard_normal((T, A)) * s * u[:, None]),
            "ws": bf(SUM_GAIN * np.random.standard_normal((A, B)) / np.sqrt(A) / s[:, None]),
            "wd_words": wd_words,
            "wd_scales": wd_scales,
            "noise": bf((1.0 + 0.5 * np.random.random(T)) * u ** 2)}


def core(x, ws, wd_words, wd_scales, noise):
    xq = mxq(f64(x), 1, "e4m3")
    total = xq @ mxq(f64(ws), 0, "e4m3")
    diff = xq @ unpack4(wd_words, wd_scales)
    r = diff / (total ** 2 + f64(noise)[:, None])
    return mxq(r, 0, "e4m3").T @ mxq(total, 0, "e4m3")


def e4m3fn_bytes(y):
    return np.clip(np.asarray(y, np.float64), -448.0, 448.0).astype(np.float32).astype(ml_dtypes.float8_e4m3fn).view(np.uint8)


def e4m3fn_values(b):
    return np.asarray(b, np.uint8).view(ml_dtypes.float8_e4m3fn).astype(np.float64)


def setup_inputs():
    d = draw0()
    x0 = np.asarray(d['ws']).astype(np.float64)
    s = (np.max(np.abs(x0), axis=(1,), keepdims=True) / 448.0).astype(np.float32)
    out = {}
    for k, v in d.items():
        if k == 'ws':
            out['ws_bytes'] = e4m3fn_bytes(x0 / s.astype(np.float64))
            out['ws_scale'] = s
        else:
            out[k] = v
    return out


def reference(x, ws_bytes, ws_scale, wd_words, wd_scales, noise):
    return core(x, e4m3fn_values(ws_bytes) * ws_scale.astype(np.float64), wd_words, wd_scales, noise)

@@ -1,0 +1,330 @@
+from contextlib import ExitStack
+
+import concourse.mybir as mybir
+from concourse.masks import make_identity
+
+M, K, B = 1536, 1024, 1024
+FLOPS = 3 * 2 * M * K * B
+
+F32 = mybir.dt.float32
+BF16 = mybir.dt.bfloat16
+I32 = mybir.dt.int32
+U32 = mybir.dt.uint32
+U8 = mybir.dt.uint8
+FP8 = mybir.dt.float8_e4m3fn
+FP8X4 = mybir.dt.float8_e4m3fn_x4
+FP4X4 = mybir.dt.float4_e2m1fn_x4
+ACT = mybir.ActivationFunctionType
+MULT = mybir.AluOpType.mult
+
+P = 128
+PACK = 4
+PASS = P * PACK
+KG = K // PASS
+MG = M // PASS
+CB = 256
+NCB = B // CB
+UNITS = MG * NCB
+HALVES = CB // P
+WIDEN_V = 0
+REC_G = 2
+LAG = 2
+
+
+def tile_monopulse_ratio_matrix_s11_kernel(tc, x, ws_bytes, ws_scale, wd_words, wd_scales, noise, out):
+    nc = tc.nc
+    with ExitStack() as ctx:
+        keep = ctx.enter_context(tc.tile_pool(name="keep", bufs=1))
+        work = ctx.enter_context(tc.tile_pool(name="work", bufs=2))
+        psum = ctx.enter_context(tc.psum_pool(name="psum", bufs=2))
+
+        x_raw = [keep.tile([P, PACK, K], BF16, name="x_raw%d" % g) for g in range(MG)]
+        x_codes = [keep.tile([P, KG, PASS], U32, name="x_codes%d" % g, align_bytes=64) for g in range(MG)]
+        x_planes = [keep.tile([P, KG, PASS], U8, name="x_planes%d" % g, align_bytes=64) for g in range(MG)]
+        ws_raw = [keep.tile([P, PACK, B], U8, name="ws_raw%d" % g, align_bytes=64) for g in range(KG)]
+        ws_factor = keep.tile([P, KG, PACK], F32, name="ws_factor")
+        ws_codes = [keep.tile([P, KG, CB], U32, name="ws_codes%d" % j, align_bytes=64) for j in range(NCB)]
+        ws_planes = [keep.tile([P, KG, CB], U8, name="ws_planes%d" % j, align_bytes=64) for j in range(NCB)]
+        wd_codes = keep.tile([P, KG, 2 * B], U8, name="wd_codes", align_bytes=64)
+        wd_planes = keep.tile([P, KG, B], U8, name="wd_planes", align_bytes=64)
+        noise_raw = keep.tile([P, MG, PACK], BF16, name="noise_raw")
+        noise_col = keep.tile([P, MG, PACK], F32, name="noise_col")
+        s_codes = [keep.tile([P, B], U32, name="s_codes%d" % g, align_bytes=64) for g in range(MG)]
+        s_planes = [keep.tile([P, B], U8, name="s_planes%d" % g, align_bytes=64) for g in range(MG)]
+        r_codes = [keep.tile([P, B], U32, name="r_codes%d" % g, align_bytes=64) for g in range(MG)]
+        r_planes = [keep.tile([P, B], U8, name="r_planes%d" % g, align_bytes=64) for g in range(MG)]
+        ident = keep.tile([P, P], F32, name="ident")
+        one = keep.tile([P, 1], F32, name="one")
+
+        nc.scalar.dma_start(out=ws_factor[:], in_=ws_scale.rearrange("(g p t) o -> p g (t o)", p=P, t=PACK))
+        nc.scalar.dma_start(out=noise_raw[:], in_=noise.rearrange("(g p t) -> p g t", p=P, t=PACK))
+        ws_rows = ws_bytes.rearrange("(g p t) n -> g p t n", p=P, t=PACK)
+        x_rows = x.rearrange("(g p t) k -> g p t k", p=P, t=PACK)
+        nc.vector.memset(wd_planes[:].rearrange("p g n -> p (g n)").bitcast(I32), 0)
+        nc.vector.memset(one[:], 1.0)
+        nc.sync.dma_start(out=ws_raw[0][:], in_=ws_rows[0])
+        for t in (0, 1):
+            nc.sync.dma_start(out=x_raw[0][:, t, :], in_=x_rows[0][:, t, :])
+        nc.sync.dma_start(out=ws_raw[1][:], in_=ws_rows[1])
+        for t in (2, 3):
+            nc.sync.dma_start(out=x_raw[0][:, t, :], in_=x_rows[0][:, t, :])
+        nc.sync.dma_start(out=x_raw[1][:], in_=x_rows[1])
+        nc.sync.dma_start(out=x_raw[2][:], in_=x_rows[2])
+        nc.sync.dma_start(out=wd_codes[:], in_=wd_words.rearrange("g p n -> p g n"))
+        for q in range(4):
+            nc.sync.dma_start(
+                out=wd_planes[32 * q : 32 * q + 4, :, :].bitcast(I32),
+                in_=wd_scales[:, 4 * q : 4 * q + 4, :].rearrange("g r n -> r g n").bitcast(I32),
+            )
+        make_identity(nc, ident[:])
+        warm = work.tile([P, 1], F32, name="warm")
+        nc.scalar.activation(out=warm[:], in_=one[:], func=ACT.Abs_reciprocal_sqrt)
+
+        live = {}
+
+        def ws_widen(j, g):
+            if g == 0:
+                live["wide", j] = work.tile([P, KG, PACK, CB], BF16, name="wide", tag="wide", bufs=2, align_bytes=64)
+            for t in range(PACK):
+                dst = live["wide", j][:, g, t, :]
+                src = ws_raw[g][:, t, j * CB : (j + 1) * CB].bitcast(FP8)
+                if t < WIDEN_V:
+                    nc.vector.tensor_scalar(out=dst, in0=src, scalar1=ws_factor[:, g, t : t + 1], scalar2=None, op0=MULT)
+                else:
+                    nc.scalar.activation(out=dst, in_=src, func=ACT.Copy, scale=ws_factor[:, g, t : t + 1])
+
+        def ws_interleave(j, g):
+            if ("wsg", j) not in live:
+                live["wsg", j] = work.tile([P, KG, CB, PACK], BF16, name="ws_grouped", tag="ws_grouped", bufs=2, align_bytes=64)
+            nc.vector.tensor_copy(out=live["wsg", j][:, g, :, :], in_=live["wide", j][:, g, :, :].rearrange("p t n -> p n t"))
+
+        def ws_quantise(j, lo, hi):
+            nc.vector.quantize_mx(
+                out=ws_codes[j][:, lo:hi, :].rearrange("p g n -> p (g n)").bitcast(FP8X4),
+                scales=ws_planes[j][:, lo:hi, :].rearrange("p g n -> p (g n)"),
+                in_=live["wsg", j][:, lo:hi, :, :].rearrange("p g n t -> p (g n t)"),
+            )
+
+        def x_transpose(gm, t):
+            bank = psum.tile([P, KG, 2, P], F32, name="xt", tag=("o", "d")[t % 2], bufs=2)
+            words = x_raw[gm][:].bitcast(F32)
+            for g in range(KG):
+                for u in range(2):
+                    nc.tensor.transpose(bank[:, g, u, :], words[:, t, 2 * P * g + u : 2 * P * (g + 1) : 2], ident[:])
+            live["xt", gm, t] = bank
+
+        def x_copy(gm, t):
+            if ("xg", gm) not in live:
+                live["xg", gm] = work.tile([P, KG, PASS, PACK], BF16, name="x_grouped", tag="x_grouped", bufs=2, align_bytes=64)
+            dst = live["xg", gm][:].bitcast(F32)[:, :, t * P : (t + 1) * P, :]
+            src = live.pop(("xt", gm, t))[:].rearrange("p g u r -> p g r u")
+            if t % 2:
+                nc.scalar.copy(out=dst, in_=src)
+            else:
+                nc.vector.tensor_copy(out=dst, in_=src)
+
+        def x_quantise_all(gm):
+            nc.vector.quantize_mx(
+                out=x_codes[gm][:].rearrange("p g r -> p (g r)").bitcast(FP8X4), scales=x_planes[gm][:].rearrange("p g r -> p (g r)"),
+                in_=live["xg", gm][:].rearrange("p g r t -> p (g r t)"),
+            )
+
+        def x_quantise(gm, g, lo, hi):
+            cols = slice(lo * P, hi * P)
+            nc.vector.quantize_mx(
+                out=x_codes[gm][:, g, cols].bitcast(FP8X4), scales=x_planes[gm][:, g, cols],
+                in_=live["xg", gm][:, g, cols, :].rearrange("p r t -> p (r t)"),
+            )
+
+        def project(u, h, tag, bufs, codes, planes, first, words_per_col, dtype):
+            gm = u % MG
+            bank = psum.tile([P, PACK, P], F32, name="bank_" + tag, tag=tag, bufs=bufs)
+            c0 = first + h * P
+            for t in range(PACK):
+                rows = slice(t * P, (t + 1) * P)
+                for g in range(KG):
+                    nc.tensor.matmul_mx(
+                        out=bank[:, t, :],
+                        lhsT=x_codes[gm][:, g, rows].bitcast(FP8X4), lhsT_scale=x_planes[gm][:, g, rows],
+                        rhs=codes[:, g, words_per_col * c0 : words_per_col * (c0 + P)].bitcast(dtype), rhs_scale=planes[:, g, c0 : c0 + P],
+                        start=(g == 0), stop=(g == KG - 1),
+                    )
+            live[tag, u, h] = bank
+
+        def project_s(u):
+            for h in range(HALVES):
+                project(u, h, "s", 4, ws_codes[u // MG], ws_planes[u // MG], 0, 1, FP8X4)
+
+        def project_d(u):
+            for h in range(HALVES):
+                project(u, h, "d", 2, wd_codes, wd_planes, u // MG * CB, 2, FP4X4)
+
+        def s_round(u, h):
+            if h == 0:
+                live["s16", u] = work.tile([P, CB, PACK], BF16, name="s16", tag="s16", bufs=3, align_bytes=64)
+            nc.vector.tensor_copy(out=live["s16", u][:, h * P : (h + 1) * P, :], in_=live["s", u, h][:].rearrange("p t b -> p b t"))
+
+        def s_square(u, h):
+            if ("sq", u) not in live:
+                live["sq", u] = work.tile([P, PACK, CB], F32, name="square", tag="square", bufs=2)
+            nc.scalar.activation(out=live["sq", u][:, :, h * P : (h + 1) * P], in_=live["s", u, h][:], func=ACT.Square)
+
+        def root(u):
+            gm = u % MG
+            rs = work.tile([P, PACK, CB], F32, name="root", tag="root", bufs=2)
+            for t in range(PACK):
+                nc.scalar.activation(out=rs[:, t, :], in_=live["sq", u][:, t, :], func=ACT.Abs_reciprocal_sqrt, bias=noise_col[:, gm, t : t + 1])
+            live["rs", u] = rs
+
+        def reciprocal(u):
+            rec = work.tile([P, CB, PACK], F32, name="rec", tag="rec", bufs=3)
+            for h in range(HALVES):
+                src = live["rs", u][:, :, h * P : (h + 1) * P].rearrange("p t b -> p b t")
+                dst = rec[:, h * P : (h + 1) * P, :]
+                if h < REC_G:
+                    nc.gpsimd.tensor_tensor(out=dst, in0=src, in1=src, op=MULT)
+                else:
+                    nc.scalar.activation(out=dst, in_=src, func=ACT.Square)
+            live["rec", u] = rec
+
+        def ratio(u, h):
+            if h == 0:
+                live["r16", u] = work.tile([P, CB, PACK], BF16, name="r16", tag="r16", bufs=3, align_bytes=64)
+            nc.vector.tensor_tensor(
+                out=live["r16", u][:, h * P : (h + 1) * P, :], in0=live["d", u, h][:].rearrange("p t b -> p b t"),
+                in1=live["rec", u][:, h * P : (h + 1) * P, :], op=MULT,
+            )
+
+        def quantise(kind, u, codes, planes):
+            j, gm = divmod(u, MG)
+            cols = slice(j * CB, (j + 1) * CB)
+            nc.vector.quantize_mx(
+                out=codes[gm][:, cols].bitcast(FP8X4), scales=planes[gm][:, cols],
+                in_=live.pop((kind, u))[:].rearrange("p b t -> p (b t)"),
+            )
+
+        def out_pass(bank, part, row, c0, width, gm):
+            nc.tensor.matmul_mx(
+                out=bank[:, part : part + width],
+                lhsT=r_codes[gm][:, row * P : (row + 1) * P].bitcast(FP8X4), lhsT_scale=r_planes[gm][:, row * P : (row + 1) * P],
+                rhs=s_codes[gm][:, c0 : c0 + width].bitcast(FP8X4), rhs_scale=s_planes[gm][:, c0 : c0 + width],
+                start=(gm == 0), stop=(gm == MG - 1),
+            )
+
+        def out_wide(row, half):
+            bank = psum.tile([P, 512], F32, name="ob", tag="o", bufs=2)
+            for gm in range(MG):
+                out_pass(bank, 0, row, half * 512, 512, gm)
+            return bank, out[row * P : (row + 1) * P, half * 512 : (half + 1) * 512], 1
+
+        def out_pair(pair, j):
+            bank = psum.tile([P, 512], F32, name="ob", tag="o", bufs=2)
+            for i in range(2):
+                for gm in range(MG):
+                    out_pass(bank, i * CB, 2 * pair + i, j * CB, CB, gm)
+            return bank, out[pair * CB : (pair + 1) * CB, j * CB : (j + 1) * CB].rearrange("(i p) c -> p i c", p=P), 2
+
+        def drain(item, on_vector):
+            bank, dst, rows = item
+            res = work.tile([P, 512], F32, name="res", tag="res", bufs=4)
+            if on_vector:
+                nc.vector.tensor_copy(out=res[:], in_=bank[:])
+            else:
+                nc.scalar.copy(out=res[:], in_=bank[:])
+            src = res[:] if rows == 1 else res[:].rearrange("p (i c) -> p i c", i=2)
+            nc.sync.dma_start(out=dst, in_=src)
+
+        OUT = {
+            5: [(out_pair, 0, 0)],
+            6: [],
+            7: [(out_pair, 0, 1)],
+            8: [(out_wide, 2, 0)],
+            9: [(out_wide, 3, 0)],
+            10: [(out_pair, 0, 2), (out_pair, 1, 2)],
+            11: [(out_wide, 4, 0), (out_wide, 5, 0)],
+            12: [(out_pair, 0, 3), (out_pair, 1, 3)],
+            13: [(out_wide, 4, 1), (out_wide, 5, 1)],
+        }
+
+        WS_STEPS = {
+            0: [(ws_widen, (1, 1))],
+            1: [(ws_interleave, (1, 0)), (ws_interleave, (1, 1)), (ws_widen, (2, 0))],
+            2: [(ws_quantise, (1, 0, KG)), (ws_widen, (2, 1))],
+            3: [(ws_interleave, (2, 0)), (ws_interleave, (2, 1))],
+            4: [(ws_quantise, (2, 0, KG)), (ws_widen, (3, 0))],
+            5: [(ws_widen, (3, 1))],
+            6: [(ws_interleave, (3, 0)), (ws_interleave, (3, 1))],
+            7: [(ws_quantise, (3, 0, KG))],
+        }
+
+        nc.vector.tensor_copy(out=noise_col[:], in_=noise_raw[:])
+        for t in range(PACK):
+            x_transpose(0, t)
+        ws_widen(0, 0)
+        x_copy(0, 0)
+        ws_interleave(0, 0)
+        x_copy(0, 1)
+        ws_widen(0, 1)
+        ws_quantise(0, 0, 1)
+        for g in range(KG):
+            x_quantise(0, g, 0, 2)
+        x_copy(0, 2)
+        x_copy(0, 3)
+        ws_interleave(0, 1)
+        for g in range(KG):
+            x_quantise(0, g, 2, 4)
+        ws_quantise(0, 1, 2)
+        for t in range(PACK):
+            x_transpose(1, t)
+        project_s(0)
+        for t in range(PACK):
+            x_copy(1, t)
+        ws_widen(1, 0)
+
+        last = [(row, half) for row in (6, 7) for half in range(2)]
+        tail = []
+        for k in range(UNITS + LAG):
+            if k == 0:
+                for t in range(PACK):
+                    x_transpose(2, t)
+            if k >= LAG:
+                project_d(k - LAG)
+            items = [f(a, b) for f, a, b in OUT.get(k, [])]
+            if k >= UNITS:
+                if k == UNITS:
+                    tail = [psum.tile([P, 512], F32, name="tb", tag="s", bufs=4) for i in range(4)]
+                for bank, (row, half) in zip(tail, last):
+                    out_pass(bank, 0, row, half * 512, 512, k - UNITS)
+            if k == 0:
+                x_quantise_all(1)
+            if k < UNITS:
+                for h in range(HALVES):
+                    s_round(k, h)
+                for h in range(HALVES):
+                    s_square(k, h)
+            if k == 0:
+                for t in range(PACK):
+                    x_copy(2, t)
+            if k < UNITS:
+                root(k)
+                reciprocal(k)
+            if k >= LAG:
+                ratio(k - LAG, 0)
+            if k < UNITS:
+                quantise("s16", k, s_codes, s_planes)
+            if k == 0:
+                x_quantise_all(2)
+            if k >= LAG:
+                ratio(k - LAG, 1)
+            for f, args in WS_STEPS.get(k, []):
+                f(*args)
+            if k + 1 < UNITS:
+                project_s(k + 1)
+            for i, item in enumerate(items):
+                drain(item, k >= UNITS and i % 2 == 0)
+            if k >= LAG:
+                quantise("r16", k - LAG, r_codes, r_planes)
+        for bank, (row, half) in zip(tail, last):
+            out_pass(bank, 0, row, half * 512, 512, MG - 1)
+        for i, (bank, (row, half)) in enumerate(zip(tail, last)):
+            drain((bank, out[row * P : (row + 1) * P, half * 512 : (half + 1) * 512], 1), i % 2 == 0)

@@ -22,124 +22,162 @@ PACK = 4
 PASS = P * PACK
 KG = K // PASS
 MG = M // PASS
+WIDTHS = [2, 2, 2, 1, 1]
+NB = len(WIDTHS)
+FIRST = [sum(WIDTHS[:j]) for j in range(NB + 1)]
 CB = 256
 NCB = B // CB
-UNITS = MG * NCB
-HALVES = CB // P
-WIDEN_V = 0
-REC_G = 2
+ORDER = [(j, gm) for gm in range(MG) for j in range(2)] + [(j, gm) for j in range(2, NB) for gm in range(MG)]
+UNITS = len(ORDER)
 LAG = 2
+RUN = 2
+IL = 4
+G_SHARE = 8
+G_UNITS = 15
+OUT_STEP = 660
+RING = 3
+WS2 = 1
+WS3 = 4
+ROUND_S = []
+DRAIN_V = 13
+XV = [(0, 1), (0, 2), (1, 1)]
 
 
 def tile_monopulse_ratio_matrix_s11_kernel(tc, x, ws_bytes, ws_scale, wd_words, wd_scales, noise, out):
     nc = tc.nc
     with ExitStack() as ctx:
         keep = ctx.enter_context(tc.tile_pool(name="keep", bufs=1))
-        work = ctx.enter_context(tc.tile_pool(name="work", bufs=2))
-        psum = ctx.enter_context(tc.psum_pool(name="psum", bufs=2))
+        psum = ctx.enter_context(tc.psum_pool(name="psum", bufs=1))
+        ctx.enter_context(tc.manual_schedule())
 
-        x_raw = [keep.tile([P, PACK, K], BF16, name="x_raw%d" % g) for g in range(MG)]
-        x_codes = [keep.tile([P, KG, PASS], U32, name="x_codes%d" % g, align_bytes=64) for g in range(MG)]
-        x_planes = [keep.tile([P, KG, PASS], U8, name="x_planes%d" % g, align_bytes=64) for g in range(MG)]
-        ws_raw = [keep.tile([P, PACK, B], U8, name="ws_raw%d" % g, align_bytes=64) for g in range(KG)]
+        def tiles(name, n, shape, dtype):
+            return [keep.tile(shape, dtype, name="%s%d" % (name, i), align_bytes=64) for i in range(n)]
+
+        x_raw = [tiles("x_raw%d_" % g, PACK, [P, K], BF16) for g in range(1)] + [tiles("x_all%d_" % g, 1, [P, PACK * K], BF16) for g in range(1, MG)]
+        x_grouped = tiles("x_grouped", 2, [P, KG, PASS, PACK], BF16)
+        x_codes = tiles("x_codes", MG, [P, KG, PASS], U32)
+        x_planes = tiles("x_planes", MG, [P, KG, PASS], U8)
+        ws_raw = tiles("ws_raw", NCB, [P, KG, PACK, CB], U8)
         ws_factor = keep.tile([P, KG, PACK], F32, name="ws_factor")
-        ws_codes = [keep.tile([P, KG, CB], U32, name="ws_codes%d" % j, align_bytes=64) for j in range(NCB)]
-        ws_planes = [keep.tile([P, KG, CB], U8, name="ws_planes%d" % j, align_bytes=64) for j in range(NCB)]
+        ws_wide = tiles("ws_wide", 2 * KG, [P, PACK, CB], BF16)
+        ws_grouped = tiles("ws_grouped", 2, [P, KG, CB, PACK], BF16)
+        ws_codes = tiles("ws_codes", NCB, [P, KG, CB], U32)
+        ws_planes = tiles("ws_planes", NCB, [P, KG, CB], U8)
         wd_codes = keep.tile([P, KG, 2 * B], U8, name="wd_codes", align_bytes=64)
         wd_planes = keep.tile([P, KG, B], U8, name="wd_planes", align_bytes=64)
         noise_raw = keep.tile([P, MG, PACK], BF16, name="noise_raw")
         noise_col = keep.tile([P, MG, PACK], F32, name="noise_col")
-        s_codes = [keep.tile([P, B], U32, name="s_codes%d" % g, align_bytes=64) for g in range(MG)]
-        s_planes = [keep.tile([P, B], U8, name="s_planes%d" % g, align_bytes=64) for g in range(MG)]
-        r_codes = [keep.tile([P, B], U32, name="r_codes%d" % g, align_bytes=64) for g in range(MG)]
-        r_planes = [keep.tile([P, B], U8, name="r_planes%d" % g, align_bytes=64) for g in range(MG)]
+        s_codes = tiles("s_codes", MG, [P, B], U32)
+        s_planes = tiles("s_planes", MG, [P, B], U8)
+        r_codes = tiles("r_codes", MG, [P, B], U32)
+        r_planes = tiles("r_planes", MG, [P, B], U8)
+        square = tiles("square", 2, [P, PACK * CB], F32)
+        root = tiles("root", 2, [P, PACK * CB], F32)
+        ring = tiles("ring", RING, [P, 2 * CB * PACK], BF16)
+        s_round16 = tiles("s_round", 2, [P, CB * PACK], BF16)
+        result = tiles("result", 8, [P, 512], F32)
         ident = keep.tile([P, P], F32, name="ident")
         one = keep.tile([P, 1], F32, name="one")
+        warm = keep.tile([P, 1], F32, name="warm")
+        banks = [psum.tile([P, 512], F32, name="bank%d" % i) for i in range(8)]
+        free = list(banks)
+        held = {}
+
+        def take(key):
+            held[key] = free.pop(0)
+            return held[key]
+
+        def give(key):
+            free.append(held.pop(key))
 
         nc.scalar.dma_start(out=ws_factor[:], in_=ws_scale.rearrange("(g p t) o -> p g (t o)", p=P, t=PACK))
         nc.scalar.dma_start(out=noise_raw[:], in_=noise.rearrange("(g p t) -> p g t", p=P, t=PACK))
         ws_rows = ws_bytes.rearrange("(g p t) n -> g p t n", p=P, t=PACK)
         x_rows = x.rearrange("(g p t) k -> g p t k", p=P, t=PACK)
-        nc.vector.memset(wd_planes[:].rearrange("p g n -> p (g n)").bitcast(I32), 0)
         nc.vector.memset(one[:], 1.0)
-        nc.sync.dma_start(out=ws_raw[0][:], in_=ws_rows[0])
-        for t in (0, 1):
-            nc.sync.dma_start(out=x_raw[0][:, t, :], in_=x_rows[0][:, t, :])
-        nc.sync.dma_start(out=ws_raw[1][:], in_=ws_rows[1])
-        for t in (2, 3):
-            nc.sync.dma_start(out=x_raw[0][:, t, :], in_=x_rows[0][:, t, :])
-        nc.sync.dma_start(out=x_raw[1][:], in_=x_rows[1])
-        nc.sync.dma_start(out=x_raw[2][:], in_=x_rows[2])
-        nc.sync.dma_start(out=wd_codes[:], in_=wd_words.rearrange("g p n -> p g n"))
+        nc.vector.memset(wd_planes[:].rearrange("p g n -> p (g n)").bitcast(I32), 0)
+
+        def ws_load(j, passes=range(KG)):
+            for g in passes:
+                nc.sync.dma_start(out=ws_raw[j][:, g, :, :], in_=ws_rows[g][:, :, j * CB : (j + 1) * CB])
+
+        ws_load(0, [0])
+        nc.sync.dma_start(out=x_raw[0][0][:], in_=x_rows[0][:, 0, :])
+        ws_load(0, [1])
+        for t in range(1, PACK):
+            nc.sync.dma_start(out=x_raw[0][t][:], in_=x_rows[0][:, t, :])
+        ws_load(1)
+        nc.sync.dma_start(out=x_raw[1][0][:], in_=x_rows[1].rearrange("p t k -> p (t k)"))
         for q in range(4):
             nc.sync.dma_start(
                 out=wd_planes[32 * q : 32 * q + 4, :, :].bitcast(I32),
                 in_=wd_scales[:, 4 * q : 4 * q + 4, :].rearrange("g r n -> r g n").bitcast(I32),
             )
+        nc.sync.dma_start(out=wd_codes[:], in_=wd_words.rearrange("g p n -> p g n"))
+        nc.sync.dma_start(out=x_raw[2][0][:], in_=x_rows[2].rearrange("p t k -> p (t k)"))
+        for j in range(2, NCB):
+            ws_load(j)
         make_identity(nc, ident[:])
-        warm = work.tile([P, 1], F32, name="warm")
         nc.scalar.activation(out=warm[:], in_=one[:], func=ACT.Abs_reciprocal_sqrt)
 
-        live = {}
-
-        def ws_widen(j, g):
-            if g == 0:
-                live["wide", j] = work.tile([P, KG, PACK, CB], BF16, name="wide", tag="wide", bufs=2, align_bytes=64)
+        def ws_widen(j, g, on_vector=0):
             for t in range(PACK):
-                dst = live["wide", j][:, g, t, :]
-                src = ws_raw[g][:, t, j * CB : (j + 1) * CB].bitcast(FP8)
-                if t < WIDEN_V:
+                dst = ws_wide[KG * (j % 2) + g][:, t, :]
+                src = ws_raw[j][:, g, t, :].bitcast(FP8)
+                if t < on_vector:
                     nc.vector.tensor_scalar(out=dst, in0=src, scalar1=ws_factor[:, g, t : t + 1], scalar2=None, op0=MULT)
                 else:
                     nc.scalar.activation(out=dst, in_=src, func=ACT.Copy, scale=ws_factor[:, g, t : t + 1])
 
         def ws_interleave(j, g):
-            if ("wsg", j) not in live:
-                live["wsg", j] = work.tile([P, KG, CB, PACK], BF16, name="ws_grouped", tag="ws_grouped", bufs=2, align_bytes=64)
-            nc.vector.tensor_copy(out=live["wsg", j][:, g, :, :], in_=live["wide", j][:, g, :, :].rearrange("p t n -> p n t"))
+            nc.vector.tensor_copy(
+                out=ws_grouped[j % 2][:, g, :, :].rearrange("p (c i) t -> p c t i", i=IL),
+                in_=ws_wide[KG * (j % 2) + g][:].rearrange("p t (c i) -> p c t i", i=IL),
+            )
 
         def ws_quantise(j, lo, hi):
             nc.vector.quantize_mx(
                 out=ws_codes[j][:, lo:hi, :].rearrange("p g n -> p (g n)").bitcast(FP8X4),
                 scales=ws_planes[j][:, lo:hi, :].rearrange("p g n -> p (g n)"),
-                in_=live["wsg", j][:, lo:hi, :, :].rearrange("p g n t -> p (g n t)"),
+                in_=ws_grouped[j % 2][:, lo:hi, :, :].rearrange("p g n t -> p (g n t)"),
             )
 
         def x_transpose(gm, t):
-            bank = psum.tile([P, KG, 2, P], F32, name="xt", tag=("o", "d")[t % 2], bufs=2)
-            words = x_raw[gm][:].bitcast(F32)
+            bank = take(("x", gm, t))[:].rearrange("p (g u r) -> p g u r", g=KG, u=2)
+            words = x_raw[0][t][:].bitcast(F32) if gm == 0 else x_raw[gm][0][:, t * K : (t + 1) * K].bitcast(F32)
             for g in range(KG):
                 for u in range(2):
-                    nc.tensor.transpose(bank[:, g, u, :], words[:, t, 2 * P * g + u : 2 * P * (g + 1) : 2], ident[:])
-            live["xt", gm, t] = bank
+                    nc.tensor.transpose(bank[:, g, u, :], words[:, 2 * P * g + u : 2 * P * (g + 1) : 2], ident[:])
 
-        def x_copy(gm, t):
-            if ("xg", gm) not in live:
-                live["xg", gm] = work.tile([P, KG, PASS, PACK], BF16, name="x_grouped", tag="x_grouped", bufs=2, align_bytes=64)
-            dst = live["xg", gm][:].bitcast(F32)[:, :, t * P : (t + 1) * P, :]
-            src = live.pop(("xt", gm, t))[:].rearrange("p g u r -> p g r u")
-            if t % 2:
-                nc.scalar.copy(out=dst, in_=src)
-            else:
+        def x_copy(gm, t, on_vector):
+            dst = x_grouped[gm % 2][:].bitcast(F32)[:, :, t * P : (t + 1) * P, :]
+            src = held["x", gm, t][:].rearrange("p (g u r) -> p g r u", g=KG, u=2)
+            if on_vector:
                 nc.vector.tensor_copy(out=dst, in_=src)
+            else:
+                nc.scalar.copy(out=dst, in_=src)
+            give(("x", gm, t))
 
-        def x_quantise_all(gm):
-            nc.vector.quantize_mx(
-                out=x_codes[gm][:].rearrange("p g r -> p (g r)").bitcast(FP8X4), scales=x_planes[gm][:].rearrange("p g r -> p (g r)"),
-                in_=live["xg", gm][:].rearrange("p g r t -> p (g r t)"),
-            )
-
-        def x_quantise(gm, g, lo, hi):
+        def x_quantise(gm, lo, hi, passes=range(KG)):
             cols = slice(lo * P, hi * P)
-            nc.vector.quantize_mx(
-                out=x_codes[gm][:, g, cols].bitcast(FP8X4), scales=x_planes[gm][:, g, cols],
-                in_=live["xg", gm][:, g, cols, :].rearrange("p r t -> p (r t)"),
-            )
+            for g in passes:
+                nc.vector.quantize_mx(
+                    out=x_codes[gm][:, g, cols].bitcast(FP8X4), scales=x_planes[gm][:, g, cols],
+                    in_=x_grouped[gm % 2][:, g, cols, :].rearrange("p r t -> p (r t)"),
+                )
 
-        def project(u, h, tag, bufs, codes, planes, first, words_per_col, dtype):
-            gm = u % MG
-            bank = psum.tile([P, PACK, P], F32, name="bank_" + tag, tag=tag, bufs=bufs)
-            c0 = first + h * P
+        def halves(u):
+            return range(WIDTHS[ORDER[u][0]])
+
+        def beams(u):
+            return P * WIDTHS[ORDER[u][0]]
+
+        def slots(key):
+            return held[key][:].rearrange("p (t b) -> p t b", t=PACK)
+
+        def project(key, gm, codes, planes, c0, words_per_col, dtype):
+            take(key)
+            bank = slots(key)
             for t in range(PACK):
                 rows = slice(t * P, (t + 1) * P)
                 for g in range(KG):
@@ -149,182 +187,209 @@ def tile_monopulse_ratio_matrix_s11_kernel(tc, x, ws_bytes, ws_scale, wd_words, 
                         rhs=codes[:, g, words_per_col * c0 : words_per_col * (c0 + P)].bitcast(dtype), rhs_scale=planes[:, g, c0 : c0 + P],
                         start=(g == 0), stop=(g == KG - 1),
                     )
-            live[tag, u, h] = bank
 
         def project_s(u):
-            for h in range(HALVES):
-                project(u, h, "s", 4, ws_codes[u // MG], ws_planes[u // MG], 0, 1, FP8X4)
+            j, gm = ORDER[u]
+            for h in halves(u):
+                piece, c0 = divmod((FIRST[j] + h) * P, CB)
+                project(("s", u, h), gm, ws_codes[piece], ws_planes[piece], c0, 1, FP8X4)
 
         def project_d(u):
-            for h in range(HALVES):
-                project(u, h, "d", 2, wd_codes, wd_planes, u // MG * CB, 2, FP4X4)
+            j, gm = ORDER[u]
+            for h in halves(u):
+                project(("d", u, h), gm, wd_codes, wd_planes, (FIRST[j] + h) * P, 2, FP4X4)
+
+        def s16(u):
+            return (ring[u % RING] if u < LAG else s_round16[u % 2])[:, : beams(u) * PACK]
+
+        def r16(u):
+            return ring[(u + LAG) % RING][:, : beams(u) * PACK]
+
+        def rec(u):
+            return ring[u % RING][:].bitcast(F32)[:, : beams(u) * PACK]
+
+        def planar(ap, u):
+            return ap[:, : beams(u) * PACK].rearrange("p (t b) -> p t b", t=PACK)
 
         def s_round(u, h):
-            if h == 0:
-                live["s16", u] = work.tile([P, CB, PACK], BF16, name="s16", tag="s16", bufs=3, align_bytes=64)
-            nc.vector.tensor_copy(out=live["s16", u][:, h * P : (h + 1) * P, :], in_=live["s", u, h][:].rearrange("p t b -> p b t"))
+            dst = s16(u).rearrange("p (b t) -> p b t", t=PACK)[:, h * P : (h + 1) * P, :]
+            src = slots(("s", u, h)).rearrange("p t b -> p b t")
+            if (u, h) in ROUND_S:
+                nc.scalar.copy(out=dst, in_=src)
+            else:
+                nc.vector.tensor_copy(out=dst, in_=src)
+            give(("s", u, h))
 
         def s_square(u, h):
-            if ("sq", u) not in live:
-                live["sq", u] = work.tile([P, PACK, CB], F32, name="square", tag="square", bufs=2)
-            nc.scalar.activation(out=live["sq", u][:, :, h * P : (h + 1) * P], in_=live["s", u, h][:], func=ACT.Square)
+            nc.scalar.activation(out=planar(square[u % 2], u)[:, :, h * P : (h + 1) * P], in_=slots(("s", u, h)), func=ACT.Square)
 
-        def root(u):
-            gm = u % MG
-            rs = work.tile([P, PACK, CB], F32, name="root", tag="root", bufs=2)
+        def s_root(u):
             for t in range(PACK):
-                nc.scalar.activation(out=rs[:, t, :], in_=live["sq", u][:, t, :], func=ACT.Abs_reciprocal_sqrt, bias=noise_col[:, gm, t : t + 1])
-            live["rs", u] = rs
+                nc.scalar.activation(
+                    out=planar(root[u % 2], u)[:, t, :], in_=planar(square[u % 2], u)[:, t, :], func=ACT.Abs_reciprocal_sqrt,
+                    bias=noise_col[:, ORDER[u][1], t : t + 1],
+                )
 
-        def reciprocal(u):
-            rec = work.tile([P, CB, PACK], F32, name="rec", tag="rec", bufs=3)
-            for h in range(HALVES):
-                src = live["rs", u][:, :, h * P : (h + 1) * P].rearrange("p t b -> p b t")
-                dst = rec[:, h * P : (h + 1) * P, :]
-                if h < REC_G:
-                    nc.gpsimd.tensor_tensor(out=dst, in0=src, in1=src, op=MULT)
-                else:
-                    nc.scalar.activation(out=dst, in_=src, func=ACT.Square)
-            live["rec", u] = rec
+        def share(u):
+            return G_SHARE * beams(u) * PACK // 8 if u < G_UNITS else 0
+
+        def rec_gpsimd(u):
+            n = share(u)
+            if n:
+                src = root[u % 2][:, :n]
+                nc.gpsimd.tensor_tensor(out=rec(u)[:, :n], in0=src, in1=src, op=MULT)
+
+        def rec_scalar(u):
+            n = share(u)
+            if n < PACK * beams(u):
+                nc.scalar.activation(out=rec(u)[:, n:], in_=root[u % 2][:, n : PACK * beams(u)], func=ACT.Square)
 
         def ratio(u, h):
-            if h == 0:
-                live["r16", u] = work.tile([P, CB, PACK], BF16, name="r16", tag="r16", bufs=3, align_bytes=64)
+            cols = slice(h * P, (h + 1) * P)
             nc.vector.tensor_tensor(
-                out=live["r16", u][:, h * P : (h + 1) * P, :], in0=live["d", u, h][:].rearrange("p t b -> p b t"),
-                in1=live["rec", u][:, h * P : (h + 1) * P, :], op=MULT,
+                out=r16(u).rearrange("p (b t) -> p b t", t=PACK)[:, cols, :].rearrange("p (c i) t -> p c t i", i=RUN),
+                in0=slots(("d", u, h)).rearrange("p t (c i) -> p c t i", i=RUN),
+                in1=planar(rec(u), u)[:, :, cols].rearrange("p t (c i) -> p c t i", i=RUN),
+                op=MULT,
             )
+            give(("d", u, h))
 
-        def quantise(kind, u, codes, planes):
-            j, gm = divmod(u, MG)
-            cols = slice(j * CB, (j + 1) * CB)
-            nc.vector.quantize_mx(
-                out=codes[gm][:, cols].bitcast(FP8X4), scales=planes[gm][:, cols],
-                in_=live.pop((kind, u))[:].rearrange("p b t -> p (b t)"),
-            )
+        def quantise(src, u, codes, planes):
+            j, gm = ORDER[u]
+            cols = slice(FIRST[j] * P, FIRST[j + 1] * P)
+            nc.vector.quantize_mx(out=codes[gm][:, cols].bitcast(FP8X4), scales=planes[gm][:, cols], in_=src)
 
-        def out_pass(bank, part, row, c0, width, gm):
-            nc.tensor.matmul_mx(
-                out=bank[:, part : part + width],
-                lhsT=r_codes[gm][:, row * P : (row + 1) * P].bitcast(FP8X4), lhsT_scale=r_planes[gm][:, row * P : (row + 1) * P],
-                rhs=s_codes[gm][:, c0 : c0 + width].bitcast(FP8X4), rhs_scale=s_planes[gm][:, c0 : c0 + width],
-                start=(gm == 0), stop=(gm == MG - 1),
-            )
+        def out_pass(piece, passes):
+            row, rows, c0, width = piece
+            if piece not in held:
+                take(piece)
+            for i in range(rows):
+                r = slice((row + i) * P, (row + i + 1) * P)
+                for g in passes:
+                    nc.tensor.matmul_mx(
+                        out=held[piece][:, i * width : (i + 1) * width],
+                        lhsT=r_codes[g][:, r].bitcast(FP8X4), lhsT_scale=r_planes[g][:, r],
+                        rhs=s_codes[g][:, c0 : c0 + width].bitcast(FP8X4), rhs_scale=s_planes[g][:, c0 : c0 + width],
+                        start=(g == 0), stop=(g == MG - 1),
+                    )
 
-        def out_wide(row, half):
-            bank = psum.tile([P, 512], F32, name="ob", tag="o", bufs=2)
-            for gm in range(MG):
-                out_pass(bank, 0, row, half * 512, 512, gm)
-            return bank, out[row * P : (row + 1) * P, half * 512 : (half + 1) * 512], 1
+        stored = []
 
-        def out_pair(pair, j):
-            bank = psum.tile([P, 512], F32, name="ob", tag="o", bufs=2)
-            for i in range(2):
-                for gm in range(MG):
-                    out_pass(bank, i * CB, 2 * pair + i, j * CB, CB, gm)
-            return bank, out[pair * CB : (pair + 1) * CB, j * CB : (j + 1) * CB].rearrange("(i p) c -> p i c", p=P), 2
-
-        def drain(item, on_vector):
-            bank, dst, rows = item
-            res = work.tile([P, 512], F32, name="res", tag="res", bufs=4)
+        def drain(piece, on_vector):
+            row, rows, c0, width = piece
+            res = result[len(stored) % len(result)][:, : rows * width]
+            stored.append(piece)
             if on_vector:
-                nc.vector.tensor_copy(out=res[:], in_=bank[:])
+                nc.vector.tensor_copy(out=res, in_=held[piece][:, : rows * width])
             else:
-                nc.scalar.copy(out=res[:], in_=bank[:])
-            src = res[:] if rows == 1 else res[:].rearrange("p (i c) -> p i c", i=2)
-            nc.sync.dma_start(out=dst, in_=src)
+                nc.scalar.copy(out=res, in_=held[piece][:, : rows * width])
+            give(piece)
+            nc.sync.dma_start(
+                out=out[row * P : (row + rows) * P, c0 : c0 + width].rearrange("(i p) c -> p i c", p=P),
+                in_=res.rearrange("p (i c) -> p i c", i=rows),
+            )
 
-        OUT = {
-            5: [(out_pair, 0, 0)],
-            6: [],
-            7: [(out_pair, 0, 1)],
-            8: [(out_wide, 2, 0)],
-            9: [(out_wide, 3, 0)],
-            10: [(out_pair, 0, 2), (out_pair, 1, 2)],
-            11: [(out_wide, 4, 0), (out_wide, 5, 0)],
-            12: [(out_pair, 0, 3), (out_pair, 1, 3)],
-            13: [(out_wide, 4, 1), (out_wide, 5, 1)],
-        }
+        def pieces(r0, r1, c0, c1):
+            found = []
+            while c0 < c1:
+                w = max(n for n in (1, 2, 4) if n <= c1 - c0)
+                found = found + [(r, min(4 // w, r1 - r), c0 * P, w * P) for r in range(r0, r1, 4 // w)]
+                c0 = c0 + w
+            return found
 
-        WS_STEPS = {
-            0: [(ws_widen, (1, 1))],
-            1: [(ws_interleave, (1, 0)), (ws_interleave, (1, 1)), (ws_widen, (2, 0))],
-            2: [(ws_quantise, (1, 0, KG)), (ws_widen, (2, 1))],
-            3: [(ws_interleave, (2, 0)), (ws_interleave, (2, 1))],
-            4: [(ws_quantise, (2, 0, KG)), (ws_widen, (3, 0))],
-            5: [(ws_widen, (3, 1))],
-            6: [(ws_interleave, (3, 0)), (ws_interleave, (3, 1))],
-            7: [(ws_quantise, (3, 0, KG))],
-        }
-
-        nc.vector.tensor_copy(out=noise_col[:], in_=noise_raw[:])
         for t in range(PACK):
             x_transpose(0, t)
-        ws_widen(0, 0)
-        x_copy(0, 0)
+        ws_widen(0, 0, 3)
+        x_copy(0, 0, False)
         ws_interleave(0, 0)
-        x_copy(0, 1)
-        ws_widen(0, 1)
+        ws_widen(0, 1, 2)
+        x_copy(0, 1, False)
         ws_quantise(0, 0, 1)
-        for g in range(KG):
-            x_quantise(0, g, 0, 2)
-        x_copy(0, 2)
-        x_copy(0, 3)
         ws_interleave(0, 1)
-        for g in range(KG):
-            x_quantise(0, g, 2, 4)
+        x_copy(0, 2, False)
+        x_quantise(0, 0, 2)
         ws_quantise(0, 1, 2)
-        for t in range(PACK):
-            x_transpose(1, t)
+        x_copy(0, 3, False)
+        nc.vector.tensor_copy(out=noise_col[:], in_=noise_raw[:])
+        ws_widen(1, 0, 2)
+        x_quantise(0, 2, 4)
         project_s(0)
-        for t in range(PACK):
-            x_copy(1, t)
-        ws_widen(1, 0)
+        ws_widen(1, 1, 1)
+        ws_interleave(1, 0)
+        ws_interleave(1, 1)
 
-        last = [(row, half) for row in (6, 7) for half in range(2)]
-        tail = []
+        waiting = []
+        made = []
+        rows_done, cols_done = 0, 0
+        last = pieces(FIRST[NB - 1], FIRST[NB], 0, FIRST[NB])
         for k in range(UNITS + LAG):
-            if k == 0:
-                for t in range(PACK):
-                    x_transpose(2, t)
-            if k >= LAG:
-                project_d(k - LAG)
-            items = [f(a, b) for f, a, b in OUT.get(k, [])]
-            if k >= UNITS:
-                if k == UNITS:
-                    tail = [psum.tile([P, 512], F32, name="tb", tag="s", bufs=4) for i in range(4)]
-                for bank, (row, half) in zip(tail, last):
-                    out_pass(bank, 0, row, half * 512, 512, k - UNITS)
-            if k == 0:
-                x_quantise_all(1)
-            if k < UNITS:
-                for h in range(HALVES):
-                    s_round(k, h)
-                for h in range(HALVES):
+            has_s, has_r = k < UNITS, k >= LAG
+            x_next, x_slots = (1, range(PACK)) if k == 0 else (2, range(2 * k - 2, 2 * k) if k <= 2 else [])
+            for t in x_slots:
+                x_transpose(x_next, t)
+            if has_s:
+                for h in halves(k):
                     s_square(k, h)
+            if has_r:
+                for h in halves(k - LAG):
+                    ratio(k - LAG, h)
+            for i, piece in enumerate(made):
+                drain(piece, k >= DRAIN_V and i % 2 == 1)
+            if 1 <= k <= UNITS:
+                rec_scalar(k - 1)
             if k == 0:
-                for t in range(PACK):
-                    x_copy(2, t)
-            if k < UNITS:
-                root(k)
-                reciprocal(k)
-            if k >= LAG:
-                ratio(k - LAG, 0)
-            if k < UNITS:
-                quantise("s16", k, s_codes, s_planes)
-            if k == 0:
-                x_quantise_all(2)
-            if k >= LAG:
-                ratio(k - LAG, 1)
-            for f, args in WS_STEPS.get(k, []):
-                f(*args)
+                s_round(0, 0)
+                ws_quantise(1, 0, KG)
             if k + 1 < UNITS:
                 project_s(k + 1)
-            for i, item in enumerate(items):
-                drain(item, k >= UNITS and i % 2 == 0)
-            if k >= LAG:
-                quantise("r16", k - LAG, r_codes, r_planes)
-        for bank, (row, half) in zip(tail, last):
-            out_pass(bank, 0, row, half * 512, 512, MG - 1)
-        for i, (bank, (row, half)) in enumerate(zip(tail, last)):
-            drain((bank, out[row * P : (row + 1) * P, half * 512 : (half + 1) * 512], 1), i % 2 == 0)
+            if 0 <= k + 1 - LAG < UNITS:
+                project_d(k + 1 - LAG)
+            for t in x_slots[:1]:
+                x_copy(x_next, t, False)
+            if has_s:
+                for h in halves(k)[k == 0 :]:
+                    s_round(k, h)
+                s_root(k)
+            for t in x_slots[1:]:
+                x_copy(x_next, t, (k, t) in XV)
+            made = []
+            room = OUT_STEP * len(halves(min(k, UNITS - 1)))
+            while waiting and room > 0 and len(free) > 0:
+                piece = waiting.pop(0)
+                out_pass(piece, range(MG))
+                made.append(piece)
+                room = room - piece[1] * piece[3]
+            if k >= UNITS:
+                for piece in last:
+                    out_pass(piece, [k - UNITS])
+            for i in range(KG):
+                if k in (WS2 + i, WS3 + i):
+                    ws_widen(2 + (k >= WS3), i)
+                if k - 1 in (WS2 + i, WS3 + i):
+                    ws_interleave(2 + (k > WS3), i)
+            if k - KG - 1 in (WS2, WS3):
+                ws_quantise(2 + (k > WS3 + 1), 0, KG)
+            if x_slots:
+                x_quantise(x_next, x_slots[0], x_slots[-1] + 1, range(KG - (k < LAG)))
+            if has_r:
+                quantise(r16(k - LAG), k - LAG, r_codes, r_planes)
+                j, gm = ORDER[k - LAG]
+                if gm == MG - 1 and j < NB - 1:
+                    waiting = waiting + pieces(rows_done, FIRST[j + 1], 0, cols_done)
+                    rows_done = FIRST[j + 1]
+            if has_s:
+                quantise(s16(k), k, s_codes, s_planes)
+                j, gm = ORDER[k]
+                if gm == MG - 1:
+                    waiting = waiting + pieces(0, rows_done, cols_done, FIRST[j + 1])
+                    cols_done = FIRST[j + 1]
+            if k < LAG:
+                x_quantise(x_next, x_slots[0], x_slots[-1] + 1, [KG - 1])
+            if has_s:
+                rec_gpsimd(k)
+        for piece in waiting:
+            out_pass(piece, range(MG))
+        for piece in last:
+            out_pass(piece, [MG - 1])
+        for i, piece in enumerate(made + waiting + last):
+            drain(piece, i % 2 == 0)

@@ -26,21 +26,31 @@ WIDTHS = [2, 2, 2, 1, 1]
 NB = len(WIDTHS)
 FIRST = [sum(WIDTHS[:j]) for j in range(NB + 1)]
 CB = 256
-NCB = B // CB
+LOAD = 512
 ORDER = [(j, gm) for gm in range(MG) for j in range(2)] + [(j, gm) for j in range(2, NB) for gm in range(MG)]
 UNITS = len(ORDER)
 LAG = 2
 RUN = 2
 IL = 4
-G_SHARE = 8
+G_SHARE = 6
 G_UNITS = 15
 OUT_STEP = 660
 RING = 3
-WS2 = 1
-WS3 = 4
-ROUND_S = []
-DRAIN_V = 13
-XV = [(0, 1), (0, 2), (1, 1)]
+IL_S = []
+EARLY = 4
+LAST_W = 256
+S_LATE = []
+X_LOAD = [1, 2, 4]
+HW = 4
+HV = 2
+HX = False
+WS_LEAD = 0
+ROUND_S = 64
+ROUND_U = range(3, 8)
+G_NARROW = 8
+G_HEAD = 6
+DRAIN_V = 11
+XV = [(0, 3), (1, 1), (2, 3)]
 
 
 def tile_monopulse_ratio_matrix_s11_kernel(tc, x, ws_bytes, ws_scale, wd_words, wd_scales, noise, out):
@@ -53,20 +63,19 @@ def tile_monopulse_ratio_matrix_s11_kernel(tc, x, ws_bytes, ws_scale, wd_words, 
         def tiles(name, n, shape, dtype):
             return [keep.tile(shape, dtype, name="%s%d" % (name, i), align_bytes=64) for i in range(n)]
 
-        x_raw = [tiles("x_raw%d_" % g, PACK, [P, K], BF16) for g in range(1)] + [tiles("x_all%d_" % g, 1, [P, PACK * K], BF16) for g in range(1, MG)]
+        x_raw = [tiles("x_raw%d_" % g, PACK // n, [P, n * K], BF16) for g, n in enumerate(X_LOAD)]
         x_grouped = tiles("x_grouped", 2, [P, KG, PASS, PACK], BF16)
         x_codes = tiles("x_codes", MG, [P, KG, PASS], U32)
         x_planes = tiles("x_planes", MG, [P, KG, PASS], U8)
-        ws_raw = tiles("ws_raw", NCB, [P, KG, PACK, CB], U8)
+        ws_raw = tiles("ws_raw", B // LOAD * KG, [P, PACK, LOAD], U8)
         ws_factor = keep.tile([P, KG, PACK], F32, name="ws_factor")
-        ws_wide = tiles("ws_wide", 2 * KG, [P, PACK, CB], BF16)
-        ws_grouped = tiles("ws_grouped", 2, [P, KG, CB, PACK], BF16)
-        ws_codes = tiles("ws_codes", NCB, [P, KG, CB], U32)
-        ws_planes = tiles("ws_planes", NCB, [P, KG, CB], U8)
+        ws_wide = tiles("ws_wide", 2 * KG, [P, PACK * CB], BF16)
+        ws_grouped = tiles("ws_grouped", 2, [P, KG * CB * PACK], BF16)
+        ws_codes = tiles("ws_codes", NB, [P, KG * CB], U32)
+        ws_planes = tiles("ws_planes", NB, [P, KG * CB], U8)
         wd_codes = keep.tile([P, KG, 2 * B], U8, name="wd_codes", align_bytes=64)
         wd_planes = keep.tile([P, KG, B], U8, name="wd_planes", align_bytes=64)
         noise_raw = keep.tile([P, MG, PACK], BF16, name="noise_raw")
-        noise_col = keep.tile([P, MG, PACK], F32, name="noise_col")
         s_codes = tiles("s_codes", MG, [P, B], U32)
         s_planes = tiles("s_planes", MG, [P, B], U8)
         r_codes = tiles("r_codes", MG, [P, B], U32)
@@ -91,7 +100,6 @@ def tile_monopulse_ratio_matrix_s11_kernel(tc, x, ws_bytes, ws_scale, wd_words, 
             free.append(held.pop(key))
 
         nc.scalar.dma_start(out=ws_factor[:], in_=ws_scale.rearrange("(g p t) o -> p g (t o)", p=P, t=PACK))
-        nc.scalar.dma_start(out=noise_raw[:], in_=noise.rearrange("(g p t) -> p g t", p=P, t=PACK))
         ws_rows = ws_bytes.rearrange("(g p t) n -> g p t n", p=P, t=PACK)
         x_rows = x.rearrange("(g p t) k -> g p t k", p=P, t=PACK)
         nc.vector.memset(one[:], 1.0)
@@ -99,52 +107,59 @@ def tile_monopulse_ratio_matrix_s11_kernel(tc, x, ws_bytes, ws_scale, wd_words, 
 
         def ws_load(j, passes=range(KG)):
             for g in passes:
-                nc.sync.dma_start(out=ws_raw[j][:, g, :, :], in_=ws_rows[g][:, :, j * CB : (j + 1) * CB])
+                nc.sync.dma_start(out=ws_raw[KG * j + g][:], in_=ws_rows[g][:, :, j * LOAD : (j + 1) * LOAD])
 
-        ws_load(0, [0])
-        nc.sync.dma_start(out=x_raw[0][0][:], in_=x_rows[0][:, 0, :])
-        ws_load(0, [1])
-        for t in range(1, PACK):
-            nc.sync.dma_start(out=x_raw[0][t][:], in_=x_rows[0][:, t, :])
-        ws_load(1)
-        nc.sync.dma_start(out=x_raw[1][0][:], in_=x_rows[1].rearrange("p t k -> p (t k)"))
+        def x_load(gm):
+            n = X_LOAD[gm]
+            for i, dst in enumerate(x_raw[gm]):
+                nc.sync.dma_start(out=dst[:], in_=x_rows[gm][:, n * i : n * (i + 1), :].rearrange("p t k -> p (t k)"))
+
+        ws_load(0)
+        x_load(0)
+        x_load(1)
+        nc.sync.dma_start(out=noise_raw[:], in_=noise.rearrange("(g p t) -> p g t", p=P, t=PACK))
         for q in range(4):
             nc.sync.dma_start(
                 out=wd_planes[32 * q : 32 * q + 4, :, :].bitcast(I32),
                 in_=wd_scales[:, 4 * q : 4 * q + 4, :].rearrange("g r n -> r g n").bitcast(I32),
             )
         nc.sync.dma_start(out=wd_codes[:], in_=wd_words.rearrange("g p n -> p g n"))
-        nc.sync.dma_start(out=x_raw[2][0][:], in_=x_rows[2].rearrange("p t k -> p (t k)"))
-        for j in range(2, NCB):
-            ws_load(j)
+        x_load(2)
+        ws_load(1)
         make_identity(nc, ident[:])
         nc.scalar.activation(out=warm[:], in_=one[:], func=ACT.Abs_reciprocal_sqrt)
 
         def ws_widen(j, g, on_vector=0):
+            n = P * WIDTHS[j]
+            piece, c0 = divmod(P * FIRST[j], LOAD)
             for t in range(PACK):
-                dst = ws_wide[KG * (j % 2) + g][:, t, :]
-                src = ws_raw[j][:, g, t, :].bitcast(FP8)
+                dst = ws_wide[KG * (j % 2) + g][:, t * n : (t + 1) * n]
+                src = ws_raw[KG * piece + g][:, t, c0 : c0 + n].bitcast(FP8)
                 if t < on_vector:
                     nc.vector.tensor_scalar(out=dst, in0=src, scalar1=ws_factor[:, g, t : t + 1], scalar2=None, op0=MULT)
                 else:
                     nc.scalar.activation(out=dst, in_=src, func=ACT.Copy, scale=ws_factor[:, g, t : t + 1])
 
         def ws_interleave(j, g):
-            nc.vector.tensor_copy(
-                out=ws_grouped[j % 2][:, g, :, :].rearrange("p (c i) t -> p c t i", i=IL),
-                in_=ws_wide[KG * (j % 2) + g][:].rearrange("p t (c i) -> p c t i", i=IL),
-            )
+            n = PACK * P * WIDTHS[j]
+            dst = ws_grouped[j % 2][:, g * n : (g + 1) * n].rearrange("p (c i t) -> p c t i", i=IL, t=PACK)
+            src = ws_wide[KG * (j % 2) + g][:, :n].rearrange("p (t c i) -> p c t i", i=IL, t=PACK)
+            if (j, g) in IL_S:
+                nc.scalar.copy(out=dst, in_=src)
+            else:
+                nc.vector.tensor_copy(out=dst, in_=src)
 
         def ws_quantise(j, lo, hi):
+            n = P * WIDTHS[j]
             nc.vector.quantize_mx(
-                out=ws_codes[j][:, lo:hi, :].rearrange("p g n -> p (g n)").bitcast(FP8X4),
-                scales=ws_planes[j][:, lo:hi, :].rearrange("p g n -> p (g n)"),
-                in_=ws_grouped[j % 2][:, lo:hi, :, :].rearrange("p g n t -> p (g n t)"),
+                out=ws_codes[j][:, lo * n : hi * n].bitcast(FP8X4), scales=ws_planes[j][:, lo * n : hi * n],
+                in_=ws_grouped[j % 2][:, lo * n * PACK : hi * n * PACK],
             )
 
         def x_transpose(gm, t):
             bank = take(("x", gm, t))[:].rearrange("p (g u r) -> p g u r", g=KG, u=2)
-            words = x_raw[0][t][:].bitcast(F32) if gm == 0 else x_raw[gm][0][:, t * K : (t + 1) * K].bitcast(F32)
+            n = X_LOAD[gm]
+            words = x_raw[gm][t // n][:, t % n * K : (t % n + 1) * K].bitcast(F32)
             for g in range(KG):
                 for u in range(2):
                     nc.tensor.transpose(bank[:, g, u, :], words[:, 2 * P * g + u : 2 * P * (g + 1) : 2], ident[:])
@@ -191,8 +206,9 @@ def tile_monopulse_ratio_matrix_s11_kernel(tc, x, ws_bytes, ws_scale, wd_words, 
         def project_s(u):
             j, gm = ORDER[u]
             for h in halves(u):
-                piece, c0 = divmod((FIRST[j] + h) * P, CB)
-                project(("s", u, h), gm, ws_codes[piece], ws_planes[piece], c0, 1, FP8X4)
+                codes = ws_codes[j][:, : KG * beams(u)].rearrange("p (g n) -> p g n", g=KG)
+                planes = ws_planes[j][:, : KG * beams(u)].rearrange("p (g n) -> p g n", g=KG)
+                project(("s", u, h), gm, codes, planes, h * P, 1, FP8X4)
 
         def project_d(u):
             j, gm = ORDER[u]
@@ -211,14 +227,15 @@ def tile_monopulse_ratio_matrix_s11_kernel(tc, x, ws_bytes, ws_scale, wd_words, 
         def planar(ap, u):
             return ap[:, : beams(u) * PACK].rearrange("p (t b) -> p t b", t=PACK)
 
-        def s_round(u, h):
+        def s_round(u, h, on_vector):
             dst = s16(u).rearrange("p (b t) -> p b t", t=PACK)[:, h * P : (h + 1) * P, :]
             src = slots(("s", u, h)).rearrange("p t b -> p b t")
-            if (u, h) in ROUND_S:
-                nc.scalar.copy(out=dst, in_=src)
-            else:
-                nc.vector.tensor_copy(out=dst, in_=src)
-            give(("s", u, h))
+            n = P - (ROUND_S if h == 1 and u in ROUND_U else 0)
+            if on_vector:
+                nc.vector.tensor_copy(out=dst[:, :n, :], in_=src[:, :n, :])
+                give(("s", u, h))
+            elif n < P:
+                nc.scalar.copy(out=dst[:, n:, :], in_=src[:, n:, :])
 
         def s_square(u, h):
             nc.scalar.activation(out=planar(square[u % 2], u)[:, :, h * P : (h + 1) * P], in_=slots(("s", u, h)), func=ACT.Square)
@@ -227,11 +244,11 @@ def tile_monopulse_ratio_matrix_s11_kernel(tc, x, ws_bytes, ws_scale, wd_words, 
             for t in range(PACK):
                 nc.scalar.activation(
                     out=planar(root[u % 2], u)[:, t, :], in_=planar(square[u % 2], u)[:, t, :], func=ACT.Abs_reciprocal_sqrt,
-                    bias=noise_col[:, ORDER[u][1], t : t + 1],
+                    bias=noise_raw[:, ORDER[u][1], t : t + 1],
                 )
 
         def share(u):
-            return G_SHARE * beams(u) * PACK // 8 if u < G_UNITS else 0
+            return (G_HEAD if u < LAG else G_SHARE if beams(u) > P else G_NARROW) * beams(u) * PACK // 8 if u < G_UNITS else 0
 
         def rec_gpsimd(u):
             n = share(u)
@@ -297,39 +314,67 @@ def tile_monopulse_ratio_matrix_s11_kernel(tc, x, ws_bytes, ws_scale, wd_words, 
                 c0 = c0 + w
             return found
 
+        for g in range(KG):
+            ws_widen(0, g, 2)
+        ws_interleave(0, 0)
+        ws_widen(1, 0, HV)
+        ws_interleave(0, 1)
         for t in range(PACK):
             x_transpose(0, t)
-        ws_widen(0, 0, 3)
         x_copy(0, 0, False)
-        ws_interleave(0, 0)
-        ws_widen(0, 1, 2)
         x_copy(0, 1, False)
-        ws_quantise(0, 0, 1)
-        ws_interleave(0, 1)
+        ws_widen(1, 1, HW)
+        ws_quantise(0, 0, KG)
         x_copy(0, 2, False)
         x_quantise(0, 0, 2)
-        ws_quantise(0, 1, 2)
-        x_copy(0, 3, False)
-        nc.vector.tensor_copy(out=noise_col[:], in_=noise_raw[:])
-        ws_widen(1, 0, 2)
+        x_copy(0, 3, HX)
+        for t in range(2):
+            x_transpose(1, t)
+        ws_interleave(1, 0)
         x_quantise(0, 2, 4)
         project_s(0)
-        ws_widen(1, 1, 1)
-        ws_interleave(1, 0)
+        for t in range(2):
+            x_copy(1, t, False)
         ws_interleave(1, 1)
+        ws_quantise(1, 0, KG)
 
-        waiting = []
+        s_step = {unit: u for u, unit in enumerate(ORDER)}
+        block = [j for j in range(NB) for h in range(WIDTHS[j])]
+
+        def ready(piece, gm):
+            row, rows, c0, width = piece
+            r_last = max(s_step[block[r], gm] + LAG for r in range(row, row + rows))
+            s_last = max(s_step[block[c], gm] for c in range(c0 // P, (c0 + width) // P))
+            return max(r_last, s_last)
+
+        plan = []
+        for j in range(1, NB):
+            if j > 1:
+                plan = plan + pieces(0, FIRST[j], FIRST[j], FIRST[j + 1])
+            plan = plan + pieces(FIRST[j] if j > 1 else 0, FIRST[j + 1], 0, FIRST[j + 1])
+        plan = plan[:-2] + [(FIRST[NB] - 1, 1, c0, LAST_W) for c0 in range(0, B, LAST_W)]
+        plan = sorted(plan, key=lambda piece: ready(piece, MG - 1))
+        done = {piece: 0 for piece in plan}
+        ws_steps = {}
+        for j in range(2, NB):
+            first = s_step[j, 0] - WS_LEAD
+            for g in range(KG):
+                late = g if WIDTHS[j] > 1 else 1
+                ws_steps.setdefault(("widen", first - 5 + late), []).append((j, g))
+                ws_steps.setdefault(("interleave", first - 4 + late), []).append((j, g))
+            ws_steps["quantise", first - 2] = [j]
+
         made = []
-        rows_done, cols_done = 0, 0
-        last = pieces(FIRST[NB - 1], FIRST[NB], 0, FIRST[NB])
-        for k in range(UNITS + LAG):
-            has_s, has_r = k < UNITS, k >= LAG
-            x_next, x_slots = (1, range(PACK)) if k == 0 else (2, range(2 * k - 2, 2 * k) if k <= 2 else [])
+        for k in range(UNITS + LAG + 1):
+            has_s, has_r = k < UNITS, LAG <= k < UNITS + LAG
+            x_next, x_first = divmod(2 * k + 6, PACK)
+            x_slots = range(x_first, x_first + 2) if x_next < MG else []
             for t in x_slots:
                 x_transpose(x_next, t)
             if has_s:
                 for h in halves(k):
                     s_square(k, h)
+                    s_round(k, h, False)
             if has_r:
                 for h in halves(k - LAG):
                     ratio(k - LAG, h)
@@ -337,59 +382,52 @@ def tile_monopulse_ratio_matrix_s11_kernel(tc, x, ws_bytes, ws_scale, wd_words, 
                 drain(piece, k >= DRAIN_V and i % 2 == 1)
             if 1 <= k <= UNITS:
                 rec_scalar(k - 1)
-            if k == 0:
-                s_round(0, 0)
-                ws_quantise(1, 0, KG)
-            if k + 1 < UNITS:
+            if k + 1 < UNITS and k not in S_LATE:
                 project_s(k + 1)
             if 0 <= k + 1 - LAG < UNITS:
                 project_d(k + 1 - LAG)
             for t in x_slots[:1]:
-                x_copy(x_next, t, False)
+                x_copy(x_next, t, (k, t) in XV)
             if has_s:
-                for h in halves(k)[k == 0 :]:
-                    s_round(k, h)
+                for h in halves(k):
+                    s_round(k, h, True)
                 s_root(k)
+            for j, g in ws_steps.get(("widen", k), []):
+                ws_widen(j, g)
+            if k + 1 < UNITS and k in S_LATE:
+                project_s(k + 1)
             for t in x_slots[1:]:
                 x_copy(x_next, t, (k, t) in XV)
             made = []
-            room = OUT_STEP * len(halves(min(k, UNITS - 1)))
-            while waiting and room > 0 and len(free) > 0:
-                piece = waiting.pop(0)
-                out_pass(piece, range(MG))
-                made.append(piece)
-                room = room - piece[1] * piece[3]
-            if k >= UNITS:
-                for piece in last:
-                    out_pass(piece, [k - UNITS])
-            for i in range(KG):
-                if k in (WS2 + i, WS3 + i):
-                    ws_widen(2 + (k >= WS3), i)
-                if k - 1 in (WS2 + i, WS3 + i):
-                    ws_interleave(2 + (k > WS3), i)
-            if k - KG - 1 in (WS2, WS3):
-                ws_quantise(2 + (k > WS3 + 1), 0, KG)
+            room = OUT_STEP * len(halves(min(k, UNITS - 1))) if k < UNITS else 9999
+            spare = 8 - sum(len(halves(u)) for u in (k + 1, k + 2, k + 2 - LAG)[k + 1 in S_LATE :] if 0 <= u < UNITS) - 2 * (k < 2)
+            for piece in plan:
+                passes = [gm for gm in range(done[piece], MG) if ready(piece, gm) < k]
+                whole = done[piece] + len(passes) == MG
+                opened = sum(0 < done[p] < MG for p in plan)
+                if not passes or room <= 0:
+                    continue
+                if piece not in held and not (free and (whole or piece[1] == 1 and opened < min(spare, EARLY))):
+                    continue
+                out_pass(piece, passes)
+                done[piece] = done[piece] + len(passes)
+                room = room - piece[1] * piece[3] * len(passes) // MG
+                if whole:
+                    made.append(piece)
+            for j, g in ws_steps.get(("interleave", k), []):
+                ws_interleave(j, g)
+            for j in ws_steps.get(("quantise", k), []):
+                ws_quantise(j, 0, KG)
             if x_slots:
-                x_quantise(x_next, x_slots[0], x_slots[-1] + 1, range(KG - (k < LAG)))
+                x_quantise(x_next, x_slots[0] * (k > 0), x_slots[-1] + 1, range(KG - (k < LAG)))
             if has_r:
                 quantise(r16(k - LAG), k - LAG, r_codes, r_planes)
-                j, gm = ORDER[k - LAG]
-                if gm == MG - 1 and j < NB - 1:
-                    waiting = waiting + pieces(rows_done, FIRST[j + 1], 0, cols_done)
-                    rows_done = FIRST[j + 1]
             if has_s:
                 quantise(s16(k), k, s_codes, s_planes)
-                j, gm = ORDER[k]
-                if gm == MG - 1:
-                    waiting = waiting + pieces(0, rows_done, cols_done, FIRST[j + 1])
-                    cols_done = FIRST[j + 1]
             if k < LAG:
-                x_quantise(x_next, x_slots[0], x_slots[-1] + 1, [KG - 1])
+                x_quantise(x_next, x_slots[0] * (k > 0), x_slots[-1] + 1, [KG - 1])
             if has_s:
                 rec_gpsimd(k)
-        for piece in waiting:
-            out_pass(piece, range(MG))
-        for piece in last:
-            out_pass(piece, [MG - 1])
-        for i, piece in enumerate(made + waiting + last):
+        for i, piece in enumerate(made):
             drain(piece, i % 2 == 0)
+        assert all(n == MG for n in done.values()) and sum(p[1] * p[3] for p in stored) * P == B * B

@@ -20,37 +20,28 @@ MULT = mybir.AluOpType.mult
 P = 128
 PACK = 4
 PASS = P * PACK
+BANK = 512
+BANKS = 8
+ALIGN = 256
 KG = K // PASS
 MG = M // PASS
+
 WIDTHS = [2, 2, 2, 1, 1]
 NB = len(WIDTHS)
 FIRST = [sum(WIDTHS[:j]) for j in range(NB + 1)]
-CB = 256
-LOAD = 512
-ORDER = [(j, gm) for gm in range(MG) for j in range(2)] + [(j, gm) for j in range(2, NB) for gm in range(MG)]
+WIDE = P * max(WIDTHS)
+SHARED = 2
+ORDER = [(j, gm) for gm in range(MG) for j in range(SHARED)] + [(j, gm) for j in range(SHARED, NB) for gm in range(MG)]
 UNITS = len(ORDER)
 LAG = 2
-RUN = 2
-IL = 4
-G_SHARE = 6
-G_UNITS = 15
-OUT_STEP = 660
-RING = 3
-IL_S = []
-EARLY = 4
-LAST_W = 256
-S_LATE = []
+WS_LOAD = P * FIRST[SHARED]
 X_LOAD = [1, 2, 4]
-HW = 4
-HV = 2
-HX = False
-WS_LEAD = 0
-ROUND_S = 64
-ROUND_U = range(3, 8)
-G_NARROW = 8
-G_HEAD = 6
-DRAIN_V = 11
-XV = [(0, 3), (1, 1), (2, 3)]
+RATIO_RUN = 2
+COPY_RUN = 4
+ROOT_SCALAR = WIDE * PACK // 4
+ROUND_SCALAR = 64
+LAST_WIDTH = 256
+RESULTS = 8
 
 
 def tile_monopulse_ratio_matrix_s11_kernel(tc, x, ws_bytes, ws_scale, wd_words, wd_scales, noise, out):
@@ -61,63 +52,62 @@ def tile_monopulse_ratio_matrix_s11_kernel(tc, x, ws_bytes, ws_scale, wd_words, 
         ctx.enter_context(tc.manual_schedule())
 
         def tiles(name, n, shape, dtype):
-            return [keep.tile(shape, dtype, name="%s%d" % (name, i), align_bytes=64) for i in range(n)]
+            return [keep.tile(shape, dtype, name="%s%d" % (name, i), align_bytes=ALIGN) for i in range(n)]
 
-        x_raw = [tiles("x_raw%d_" % g, PACK // n, [P, n * K], BF16) for g, n in enumerate(X_LOAD)]
+        x_raw = [tiles("x_raw%d_" % gm, PACK // n, [P, n * K], BF16) for gm, n in enumerate(X_LOAD)]
         x_grouped = tiles("x_grouped", 2, [P, KG, PASS, PACK], BF16)
         x_codes = tiles("x_codes", MG, [P, KG, PASS], U32)
         x_planes = tiles("x_planes", MG, [P, KG, PASS], U8)
-        ws_raw = tiles("ws_raw", B // LOAD * KG, [P, PACK, LOAD], U8)
+        ws_raw = tiles("ws_raw", B // WS_LOAD * KG, [P, PACK, WS_LOAD], U8)
         ws_factor = keep.tile([P, KG, PACK], F32, name="ws_factor")
-        ws_wide = tiles("ws_wide", 2 * KG, [P, PACK * CB], BF16)
-        ws_grouped = tiles("ws_grouped", 2, [P, KG * CB * PACK], BF16)
-        ws_codes = tiles("ws_codes", NB, [P, KG * CB], U32)
-        ws_planes = tiles("ws_planes", NB, [P, KG * CB], U8)
-        wd_codes = keep.tile([P, KG, 2 * B], U8, name="wd_codes", align_bytes=64)
-        wd_planes = keep.tile([P, KG, B], U8, name="wd_planes", align_bytes=64)
-        noise_raw = keep.tile([P, MG, PACK], BF16, name="noise_raw")
+        ws_wide = tiles("ws_wide", 2 * KG, [P, PACK * WIDE], BF16)
+        ws_grouped = tiles("ws_grouped", 2, [P, KG * WIDE * PACK], BF16)
+        ws_codes = tiles("ws_codes", NB, [P, KG * WIDE], U32)
+        ws_planes = tiles("ws_planes", NB, [P, KG * WIDE], U8)
+        wd_codes = keep.tile([P, KG, 2 * B], U8, name="wd_codes", align_bytes=ALIGN)
+        wd_planes = keep.tile([P, KG, B], U8, name="wd_planes", align_bytes=ALIGN)
+        noise_col = keep.tile([P, MG, PACK], BF16, name="noise_col")
         s_codes = tiles("s_codes", MG, [P, B], U32)
         s_planes = tiles("s_planes", MG, [P, B], U8)
         r_codes = tiles("r_codes", MG, [P, B], U32)
         r_planes = tiles("r_planes", MG, [P, B], U8)
-        square = tiles("square", 2, [P, PACK * CB], F32)
-        root = tiles("root", 2, [P, PACK * CB], F32)
-        ring = tiles("ring", RING, [P, 2 * CB * PACK], BF16)
-        s_round16 = tiles("s_round", 2, [P, CB * PACK], BF16)
-        result = tiles("result", 8, [P, 512], F32)
+        square = tiles("square", 2, [P, PACK * WIDE], F32)
+        root = tiles("root", 2, [P, PACK * WIDE], F32)
+        ring = tiles("ring", LAG + 1, [P, 2 * WIDE * PACK], BF16)
+        s_rounded = tiles("s_rounded", 2, [P, WIDE * PACK], BF16)
+        result = tiles("result", RESULTS, [P, BANK], F32)
         ident = keep.tile([P, P], F32, name="ident")
         one = keep.tile([P, 1], F32, name="one")
         warm = keep.tile([P, 1], F32, name="warm")
-        banks = [psum.tile([P, 512], F32, name="bank%d" % i) for i in range(8)]
-        free = list(banks)
+
+        free = [psum.tile([P, BANK], F32, name="bank%d" % i) for i in range(BANKS)]
         held = {}
 
         def take(key):
             held[key] = free.pop(0)
-            return held[key]
 
         def give(key):
             free.append(held.pop(key))
 
-        nc.scalar.dma_start(out=ws_factor[:], in_=ws_scale.rearrange("(g p t) o -> p g (t o)", p=P, t=PACK))
         ws_rows = ws_bytes.rearrange("(g p t) n -> g p t n", p=P, t=PACK)
         x_rows = x.rearrange("(g p t) k -> g p t k", p=P, t=PACK)
-        nc.vector.memset(one[:], 1.0)
-        nc.vector.memset(wd_planes[:].rearrange("p g n -> p (g n)").bitcast(I32), 0)
 
-        def ws_load(j, passes=range(KG)):
-            for g in passes:
-                nc.sync.dma_start(out=ws_raw[KG * j + g][:], in_=ws_rows[g][:, :, j * LOAD : (j + 1) * LOAD])
+        def ws_load(part):
+            for g in range(KG):
+                nc.sync.dma_start(out=ws_raw[KG * part + g][:], in_=ws_rows[g][:, :, part * WS_LOAD : (part + 1) * WS_LOAD])
 
         def x_load(gm):
             n = X_LOAD[gm]
             for i, dst in enumerate(x_raw[gm]):
                 nc.sync.dma_start(out=dst[:], in_=x_rows[gm][:, n * i : n * (i + 1), :].rearrange("p t k -> p (t k)"))
 
+        nc.scalar.dma_start(out=ws_factor[:], in_=ws_scale.rearrange("(g p t) o -> p g (t o)", p=P, t=PACK))
+        nc.vector.memset(one[:], 1.0)
+        nc.vector.memset(wd_planes[:].rearrange("p g n -> p (g n)").bitcast(I32), 0)
         ws_load(0)
         x_load(0)
         x_load(1)
-        nc.sync.dma_start(out=noise_raw[:], in_=noise.rearrange("(g p t) -> p g t", p=P, t=PACK))
+        nc.sync.dma_start(out=noise_col[:], in_=noise.rearrange("(g p t) -> p g t", p=P, t=PACK))
         for q in range(4):
             nc.sync.dma_start(
                 out=wd_planes[32 * q : 32 * q + 4, :, :].bitcast(I32),
@@ -129,35 +119,31 @@ def tile_monopulse_ratio_matrix_s11_kernel(tc, x, ws_bytes, ws_scale, wd_words, 
         make_identity(nc, ident[:])
         nc.scalar.activation(out=warm[:], in_=one[:], func=ACT.Abs_reciprocal_sqrt)
 
-        def ws_widen(j, g, on_vector=0):
+        def ws_widen(j, g, vector_slots=0):
             n = P * WIDTHS[j]
-            piece, c0 = divmod(P * FIRST[j], LOAD)
+            part, c0 = divmod(P * FIRST[j], WS_LOAD)
             for t in range(PACK):
                 dst = ws_wide[KG * (j % 2) + g][:, t * n : (t + 1) * n]
-                src = ws_raw[KG * piece + g][:, t, c0 : c0 + n].bitcast(FP8)
-                if t < on_vector:
+                src = ws_raw[KG * part + g][:, t, c0 : c0 + n].bitcast(FP8)
+                if t < vector_slots:
                     nc.vector.tensor_scalar(out=dst, in0=src, scalar1=ws_factor[:, g, t : t + 1], scalar2=None, op0=MULT)
                 else:
                     nc.scalar.activation(out=dst, in_=src, func=ACT.Copy, scale=ws_factor[:, g, t : t + 1])
 
         def ws_interleave(j, g):
             n = PACK * P * WIDTHS[j]
-            dst = ws_grouped[j % 2][:, g * n : (g + 1) * n].rearrange("p (c i t) -> p c t i", i=IL, t=PACK)
-            src = ws_wide[KG * (j % 2) + g][:, :n].rearrange("p (t c i) -> p c t i", i=IL, t=PACK)
-            if (j, g) in IL_S:
-                nc.scalar.copy(out=dst, in_=src)
-            else:
-                nc.vector.tensor_copy(out=dst, in_=src)
-
-        def ws_quantise(j, lo, hi):
-            n = P * WIDTHS[j]
-            nc.vector.quantize_mx(
-                out=ws_codes[j][:, lo * n : hi * n].bitcast(FP8X4), scales=ws_planes[j][:, lo * n : hi * n],
-                in_=ws_grouped[j % 2][:, lo * n * PACK : hi * n * PACK],
+            nc.vector.tensor_copy(
+                out=ws_grouped[j % 2][:, g * n : (g + 1) * n].rearrange("p (c i t) -> p c t i", i=COPY_RUN, t=PACK),
+                in_=ws_wide[KG * (j % 2) + g][:, :n].rearrange("p (t c i) -> p c t i", i=COPY_RUN, t=PACK),
             )
 
+        def ws_quantise(j):
+            n = KG * P * WIDTHS[j]
+            nc.vector.quantize_mx(out=ws_codes[j][:, :n].bitcast(FP8X4), scales=ws_planes[j][:, :n], in_=ws_grouped[j % 2][:, : n * PACK])
+
         def x_transpose(gm, t):
-            bank = take(("x", gm, t))[:].rearrange("p (g u r) -> p g u r", g=KG, u=2)
+            take(("x", gm, t))
+            bank = held["x", gm, t][:].rearrange("p (g u r) -> p g u r", g=KG, u=2)
             n = X_LOAD[gm]
             words = x_raw[gm][t // n][:, t % n * K : (t % n + 1) * K].bitcast(F32)
             for g in range(KG):
@@ -173,100 +159,96 @@ def tile_monopulse_ratio_matrix_s11_kernel(tc, x, ws_bytes, ws_scale, wd_words, 
                 nc.scalar.copy(out=dst, in_=src)
             give(("x", gm, t))
 
-        def x_quantise(gm, lo, hi, passes=range(KG)):
-            cols = slice(lo * P, hi * P)
+        def x_quantise(gm, t0, t1, passes):
+            cols = slice(t0 * P, t1 * P)
             for g in passes:
                 nc.vector.quantize_mx(
                     out=x_codes[gm][:, g, cols].bitcast(FP8X4), scales=x_planes[gm][:, g, cols],
                     in_=x_grouped[gm % 2][:, g, cols, :].rearrange("p r t -> p (r t)"),
                 )
 
-        def halves(u):
+        def beam_tiles(u):
             return range(WIDTHS[ORDER[u][0]])
 
-        def beams(u):
-            return P * WIDTHS[ORDER[u][0]]
+        def values(u):
+            return PACK * P * WIDTHS[ORDER[u][0]]
 
-        def slots(key):
-            return held[key][:].rearrange("p (t b) -> p t b", t=PACK)
+        def by_slot(ap):
+            return ap.rearrange("p (t b) -> p t b", t=PACK)
 
-        def project(key, gm, codes, planes, c0, words_per_col, dtype):
+        def by_beam(ap):
+            return ap.rearrange("p (b t) -> p b t", t=PACK)
+
+        def project(key, gm, codes, planes, c0, per_beam, dtype):
             take(key)
-            bank = slots(key)
             for t in range(PACK):
                 rows = slice(t * P, (t + 1) * P)
                 for g in range(KG):
                     nc.tensor.matmul_mx(
-                        out=bank[:, t, :],
+                        out=by_slot(held[key][:])[:, t, :],
                         lhsT=x_codes[gm][:, g, rows].bitcast(FP8X4), lhsT_scale=x_planes[gm][:, g, rows],
-                        rhs=codes[:, g, words_per_col * c0 : words_per_col * (c0 + P)].bitcast(dtype), rhs_scale=planes[:, g, c0 : c0 + P],
+                        rhs=codes[:, g, per_beam * c0 : per_beam * (c0 + P)].bitcast(dtype), rhs_scale=planes[:, g, c0 : c0 + P],
                         start=(g == 0), stop=(g == KG - 1),
                     )
 
         def project_s(u):
             j, gm = ORDER[u]
-            for h in halves(u):
-                codes = ws_codes[j][:, : KG * beams(u)].rearrange("p (g n) -> p g n", g=KG)
-                planes = ws_planes[j][:, : KG * beams(u)].rearrange("p (g n) -> p g n", g=KG)
+            n = KG * P * WIDTHS[j]
+            codes = ws_codes[j][:, :n].rearrange("p (g n) -> p g n", g=KG)
+            planes = ws_planes[j][:, :n].rearrange("p (g n) -> p g n", g=KG)
+            for h in beam_tiles(u):
                 project(("s", u, h), gm, codes, planes, h * P, 1, FP8X4)
 
         def project_d(u):
             j, gm = ORDER[u]
-            for h in halves(u):
+            for h in beam_tiles(u):
                 project(("d", u, h), gm, wd_codes, wd_planes, (FIRST[j] + h) * P, 2, FP4X4)
 
         def s16(u):
-            return (ring[u % RING] if u < LAG else s_round16[u % 2])[:, : beams(u) * PACK]
+            return (ring[u] if u < LAG else s_rounded[u % 2])[:, : values(u)]
 
         def r16(u):
-            return ring[(u + LAG) % RING][:, : beams(u) * PACK]
+            return ring[(u + LAG) % len(ring)][:, : values(u)]
 
-        def rec(u):
-            return ring[u % RING][:].bitcast(F32)[:, : beams(u) * PACK]
+        def reciprocal(u):
+            return ring[u % len(ring)][:].bitcast(F32)[:, : values(u)]
 
-        def planar(ap, u):
-            return ap[:, : beams(u) * PACK].rearrange("p (t b) -> p t b", t=PACK)
-
-        def s_round(u, h, on_vector):
-            dst = s16(u).rearrange("p (b t) -> p b t", t=PACK)[:, h * P : (h + 1) * P, :]
-            src = slots(("s", u, h)).rearrange("p t b -> p b t")
-            n = P - (ROUND_S if h == 1 and u in ROUND_U else 0)
+        def s_round(u, h, b0, b1, on_vector):
+            dst = by_beam(s16(u))[:, h * P + b0 : h * P + b1, :]
+            src = by_slot(held["s", u, h][:]).rearrange("p t b -> p b t")[:, b0:b1, :]
             if on_vector:
-                nc.vector.tensor_copy(out=dst[:, :n, :], in_=src[:, :n, :])
-                give(("s", u, h))
-            elif n < P:
-                nc.scalar.copy(out=dst[:, n:, :], in_=src[:, n:, :])
+                nc.vector.tensor_copy(out=dst, in_=src)
+            else:
+                nc.scalar.copy(out=dst, in_=src)
 
         def s_square(u, h):
-            nc.scalar.activation(out=planar(square[u % 2], u)[:, :, h * P : (h + 1) * P], in_=slots(("s", u, h)), func=ACT.Square)
+            dst = by_slot(square[u % 2][:, : values(u)])[:, :, h * P : (h + 1) * P]
+            nc.scalar.activation(out=dst, in_=by_slot(held["s", u, h][:]), func=ACT.Square)
 
-        def s_root(u):
+        def inverse_root(u):
             for t in range(PACK):
                 nc.scalar.activation(
-                    out=planar(root[u % 2], u)[:, t, :], in_=planar(square[u % 2], u)[:, t, :], func=ACT.Abs_reciprocal_sqrt,
-                    bias=noise_raw[:, ORDER[u][1], t : t + 1],
+                    out=by_slot(root[u % 2][:, : values(u)])[:, t, :], in_=by_slot(square[u % 2][:, : values(u)])[:, t, :],
+                    func=ACT.Abs_reciprocal_sqrt, bias=noise_col[:, ORDER[u][1], t : t + 1],
                 )
 
-        def share(u):
-            return (G_HEAD if u < LAG else G_SHARE if beams(u) > P else G_NARROW) * beams(u) * PACK // 8 if u < G_UNITS else 0
+        def is_wide(u):
+            return values(u) == PACK * WIDE
 
-        def rec_gpsimd(u):
-            n = share(u)
-            if n:
-                src = root[u % 2][:, :n]
-                nc.gpsimd.tensor_tensor(out=rec(u)[:, :n], in0=src, in1=src, op=MULT)
+        def root_square_gpsimd(u):
+            n = values(u) - ROOT_SCALAR * is_wide(u)
+            nc.gpsimd.tensor_tensor(out=reciprocal(u)[:, :n], in0=root[u % 2][:, :n], in1=root[u % 2][:, :n], op=MULT)
 
-        def rec_scalar(u):
-            n = share(u)
-            if n < PACK * beams(u):
-                nc.scalar.activation(out=rec(u)[:, n:], in_=root[u % 2][:, n : PACK * beams(u)], func=ACT.Square)
+        def root_square_scalar(u):
+            n = values(u) - ROOT_SCALAR
+            nc.scalar.activation(out=reciprocal(u)[:, n:], in_=root[u % 2][:, n : values(u)], func=ACT.Square)
 
         def ratio(u, h):
             cols = slice(h * P, (h + 1) * P)
             nc.vector.tensor_tensor(
-                out=r16(u).rearrange("p (b t) -> p b t", t=PACK)[:, cols, :].rearrange("p (c i) t -> p c t i", i=RUN),
-                in0=slots(("d", u, h)).rearrange("p t (c i) -> p c t i", i=RUN),
-                in1=planar(rec(u), u)[:, :, cols].rearrange("p t (c i) -> p c t i", i=RUN),
+                out=by_beam(r16(u))[:, cols, :].rearrange("p (c i) t -> p c t i", i=RATIO_RUN),
+                in0=by_slot(held["d", u, h][:]).rearrange("p t (c i) -> p c t i", i=RATIO_RUN),
+                in1=by_slot(reciprocal(u))[:, :, cols].rearrange("p t (c i) -> p c t i", i=RATIO_RUN),
                 op=MULT,
             )
             give(("d", u, h))
@@ -276,25 +258,25 @@ def tile_monopulse_ratio_matrix_s11_kernel(tc, x, ws_bytes, ws_scale, wd_words, 
             cols = slice(FIRST[j] * P, FIRST[j + 1] * P)
             nc.vector.quantize_mx(out=codes[gm][:, cols].bitcast(FP8X4), scales=planes[gm][:, cols], in_=src)
 
-        def out_pass(piece, passes):
+        def out_passes(piece, groups):
             row, rows, c0, width = piece
             if piece not in held:
                 take(piece)
             for i in range(rows):
                 r = slice((row + i) * P, (row + i + 1) * P)
-                for g in passes:
+                for gm in groups:
                     nc.tensor.matmul_mx(
                         out=held[piece][:, i * width : (i + 1) * width],
-                        lhsT=r_codes[g][:, r].bitcast(FP8X4), lhsT_scale=r_planes[g][:, r],
-                        rhs=s_codes[g][:, c0 : c0 + width].bitcast(FP8X4), rhs_scale=s_planes[g][:, c0 : c0 + width],
-                        start=(g == 0), stop=(g == MG - 1),
+                        lhsT=r_codes[gm][:, r].bitcast(FP8X4), lhsT_scale=r_planes[gm][:, r],
+                        rhs=s_codes[gm][:, c0 : c0 + width].bitcast(FP8X4), rhs_scale=s_planes[gm][:, c0 : c0 + width],
+                        start=(gm == 0), stop=(gm == MG - 1),
                     )
 
         stored = []
 
-        def drain(piece, on_vector):
+        def store(piece, on_vector):
             row, rows, c0, width = piece
-            res = result[len(stored) % len(result)][:, : rows * width]
+            res = result[len(stored) % RESULTS][:, : rows * width]
             stored.append(piece)
             if on_vector:
                 nc.vector.tensor_copy(out=res, in_=held[piece][:, : rows * width])
@@ -314,120 +296,122 @@ def tile_monopulse_ratio_matrix_s11_kernel(tc, x, ws_bytes, ws_scale, wd_words, 
                 c0 = c0 + w
             return found
 
+        step_of = {unit: u for u, unit in enumerate(ORDER)}
+        block_of = [j for j in range(NB) for h in range(WIDTHS[j])]
+
+        def ready(piece, gm):
+            row, rows, c0, width = piece
+            r_step = max(step_of[block_of[r], gm] + LAG for r in range(row, row + rows))
+            s_step = max(step_of[block_of[c], gm] for c in range(c0 // P, (c0 + width) // P))
+            return max(r_step, s_step)
+
+        plan = pieces(0, FIRST[SHARED], 0, FIRST[SHARED])
+        for j in range(SHARED, NB):
+            plan = plan + pieces(0, FIRST[j], FIRST[j], FIRST[j + 1])
+            if j < NB - 1:
+                plan = plan + pieces(FIRST[j], FIRST[j + 1], 0, FIRST[j + 1])
+        plan = plan + [(FIRST[NB - 1], 1, c0, LAST_WIDTH) for c0 in range(0, B, LAST_WIDTH)]
+        plan = sorted(plan, key=lambda piece: ready(piece, MG - 1))
+        done = {piece: 0 for piece in plan}
+
+        widen_at, interleave_at, quantise_at = {}, {}, {}
+        for j in range(SHARED, NB):
+            due = step_of[j, 0] - 2
+            for g in range(KG):
+                ahead = (KG - 1 - g) * (WIDTHS[j] - 1)
+                widen_at.setdefault(due - 2 - ahead, []).append((j, g))
+                interleave_at.setdefault(due - 1 - ahead, []).append((j, g))
+            quantise_at[due] = j
+
         for g in range(KG):
-            ws_widen(0, g, 2)
+            ws_widen(0, g, PACK // 2)
         ws_interleave(0, 0)
-        ws_widen(1, 0, HV)
+        ws_widen(1, 0, PACK // 2)
         ws_interleave(0, 1)
         for t in range(PACK):
             x_transpose(0, t)
         x_copy(0, 0, False)
         x_copy(0, 1, False)
-        ws_widen(1, 1, HW)
-        ws_quantise(0, 0, KG)
+        ws_widen(1, 1, PACK)
+        ws_quantise(0)
         x_copy(0, 2, False)
-        x_quantise(0, 0, 2)
-        x_copy(0, 3, HX)
+        x_quantise(0, 0, 2, range(KG))
+        x_copy(0, 3, False)
         for t in range(2):
             x_transpose(1, t)
         ws_interleave(1, 0)
-        x_quantise(0, 2, 4)
+        x_quantise(0, 2, PACK, range(KG))
         project_s(0)
         for t in range(2):
             x_copy(1, t, False)
         ws_interleave(1, 1)
-        ws_quantise(1, 0, KG)
+        ws_quantise(1)
 
-        s_step = {unit: u for u, unit in enumerate(ORDER)}
-        block = [j for j in range(NB) for h in range(WIDTHS[j])]
-
-        def ready(piece, gm):
-            row, rows, c0, width = piece
-            r_last = max(s_step[block[r], gm] + LAG for r in range(row, row + rows))
-            s_last = max(s_step[block[c], gm] for c in range(c0 // P, (c0 + width) // P))
-            return max(r_last, s_last)
-
-        plan = []
-        for j in range(1, NB):
-            if j > 1:
-                plan = plan + pieces(0, FIRST[j], FIRST[j], FIRST[j + 1])
-            plan = plan + pieces(FIRST[j] if j > 1 else 0, FIRST[j + 1], 0, FIRST[j + 1])
-        plan = plan[:-2] + [(FIRST[NB] - 1, 1, c0, LAST_W) for c0 in range(0, B, LAST_W)]
-        plan = sorted(plan, key=lambda piece: ready(piece, MG - 1))
-        done = {piece: 0 for piece in plan}
-        ws_steps = {}
-        for j in range(2, NB):
-            first = s_step[j, 0] - WS_LEAD
-            for g in range(KG):
-                late = g if WIDTHS[j] > 1 else 1
-                ws_steps.setdefault(("widen", first - 5 + late), []).append((j, g))
-                ws_steps.setdefault(("interleave", first - 4 + late), []).append((j, g))
-            ws_steps["quantise", first - 2] = [j]
-
-        made = []
+        closed = []
         for k in range(UNITS + LAG + 1):
             has_s, has_r = k < UNITS, LAG <= k < UNITS + LAG
-            x_next, x_first = divmod(2 * k + 6, PACK)
-            x_slots = range(x_first, x_first + 2) if x_next < MG else []
-            for t in x_slots:
-                x_transpose(x_next, t)
+            x_gm, x_t = divmod(PACK + 2 + 2 * k, PACK)
+            has_x = x_gm < MG
+            x_from = x_t if k else 0
+            split = P - ROUND_SCALAR if has_s and is_wide(k) and not has_x and not closed else P
+
+            if has_x:
+                x_transpose(x_gm, x_t)
+                x_transpose(x_gm, x_t + 1)
             if has_s:
-                for h in halves(k):
+                for h in beam_tiles(k):
                     s_square(k, h)
-                    s_round(k, h, False)
+                if split < P:
+                    s_round(k, 1, split, P, False)
             if has_r:
-                for h in halves(k - LAG):
+                for h in beam_tiles(k - LAG):
                     ratio(k - LAG, h)
-            for i, piece in enumerate(made):
-                drain(piece, k >= DRAIN_V and i % 2 == 1)
-            if 1 <= k <= UNITS:
-                rec_scalar(k - 1)
-            if k + 1 < UNITS and k not in S_LATE:
+            for i, piece in enumerate(closed):
+                store(piece, k >= step_of[NB - 1, 0] and i % 2 == 1)
+            if 1 <= k <= UNITS and is_wide(k - 1):
+                root_square_scalar(k - 1)
+            if k + 1 < UNITS:
                 project_s(k + 1)
             if 0 <= k + 1 - LAG < UNITS:
                 project_d(k + 1 - LAG)
-            for t in x_slots[:1]:
-                x_copy(x_next, t, (k, t) in XV)
+            if has_x:
+                x_copy(x_gm, x_t, False)
             if has_s:
-                for h in halves(k):
-                    s_round(k, h, True)
-                s_root(k)
-            for j, g in ws_steps.get(("widen", k), []):
+                for h in beam_tiles(k):
+                    s_round(k, h, 0, split if h == 1 else P, True)
+                    give(("s", k, h))
+                inverse_root(k)
+            for j, g in widen_at.get(k, []):
                 ws_widen(j, g)
-            if k + 1 < UNITS and k in S_LATE:
-                project_s(k + 1)
-            for t in x_slots[1:]:
-                x_copy(x_next, t, (k, t) in XV)
-            made = []
-            room = OUT_STEP * len(halves(min(k, UNITS - 1))) if k < UNITS else 9999
-            spare = 8 - sum(len(halves(u)) for u in (k + 1, k + 2, k + 2 - LAG)[k + 1 in S_LATE :] if 0 <= u < UNITS) - 2 * (k < 2)
+            if has_x:
+                x_copy(x_gm, x_t + 1, True)
+
+            closed = []
+            spare = BANKS - sum(len(beam_tiles(u)) for u in (k + 1, k + 2, k + 2 - LAG) if u < UNITS) - 2 * (k + 1 < MG)
             for piece in plan:
-                passes = [gm for gm in range(done[piece], MG) if ready(piece, gm) < k]
-                whole = done[piece] + len(passes) == MG
-                opened = sum(0 < done[p] < MG for p in plan)
-                if not passes or room <= 0:
-                    continue
-                if piece not in held and not (free and (whole or piece[1] == 1 and opened < min(spare, EARLY))):
-                    continue
-                out_pass(piece, passes)
-                done[piece] = done[piece] + len(passes)
-                room = room - piece[1] * piece[3] * len(passes) // MG
-                if whole:
-                    made.append(piece)
-            for j, g in ws_steps.get(("interleave", k), []):
+                groups = [gm for gm in range(done[piece], MG) if ready(piece, gm) < k]
+                whole = done[piece] + len(groups) == MG
+                opened = sum(0 < n < MG for n in done.values())
+                if groups and (piece in held or free and (whole or piece[1] == 1 and opened < spare)):
+                    out_passes(piece, groups)
+                    done[piece] = done[piece] + len(groups)
+                    if whole:
+                        closed.append(piece)
+
+            for j, g in interleave_at.get(k, []):
                 ws_interleave(j, g)
-            for j in ws_steps.get(("quantise", k), []):
-                ws_quantise(j, 0, KG)
-            if x_slots:
-                x_quantise(x_next, x_slots[0] * (k > 0), x_slots[-1] + 1, range(KG - (k < LAG)))
+            if k in quantise_at:
+                ws_quantise(quantise_at[k])
+            if has_x:
+                x_quantise(x_gm, x_from, x_t + 2, range(KG if has_r else KG - 1))
             if has_r:
                 quantise(r16(k - LAG), k - LAG, r_codes, r_planes)
             if has_s:
                 quantise(s16(k), k, s_codes, s_planes)
             if k < LAG:
-                x_quantise(x_next, x_slots[0] * (k > 0), x_slots[-1] + 1, [KG - 1])
+                x_quantise(x_gm, x_from, x_t + 2, [KG - 1])
             if has_s:
-                rec_gpsimd(k)
-        for i, piece in enumerate(made):
-            drain(piece, i % 2 == 0)
-        assert all(n == MG for n in done.values()) and sum(p[1] * p[3] for p in stored) * P == B * B
+                root_square_gpsimd(k)
+        for i, piece in enumerate(closed):
+            store(piece, i % 2 == 0)
+        assert sum(rows * width for row, rows, c0, width in stored) * P == B * B

@@ -34,12 +34,14 @@ SHARED = 2
 ORDER = [(j, gm) for gm in range(MG) for j in range(SHARED)] + [(j, gm) for j in range(SHARED, NB) for gm in range(MG)]
 UNITS = len(ORDER)
 LAG = 2
-WS_LOAD = P * FIRST[SHARED]
-X_LOAD = [1, 2, 4]
+WS_LOADS = [(0, 512), (512, 512)]
+X_LOAD = [1, 2, 2]
 RATIO_RUN = 2
 COPY_RUN = 4
-ROOT_SCALAR = WIDE * PACK // 4
-ROUND_SCALAR = 64
+ROOT_SCALAR = {1: 256, 2: 384}
+ROUND_SCALAR = 96
+WIDEN_VECTOR = {1: 2, 2: 4}
+WS_AHEAD = 3
 LAST_WIDTH = 256
 RESULTS = 8
 
@@ -58,13 +60,13 @@ def tile_monopulse_ratio_matrix_s11_kernel(tc, x, ws_bytes, ws_scale, wd_words, 
         x_grouped = tiles("x_grouped", 2, [P, KG, PASS, PACK], BF16)
         x_codes = tiles("x_codes", MG, [P, KG, PASS], U32)
         x_planes = tiles("x_planes", MG, [P, KG, PASS], U8)
-        ws_raw = tiles("ws_raw", B // WS_LOAD * KG, [P, PACK, WS_LOAD], U8)
+        ws_raw = [tiles("ws_raw%d_" % i, KG, [P, PACK, n], U8) for i, (c0, n) in enumerate(WS_LOADS)]
         ws_factor = keep.tile([P, KG, PACK], F32, name="ws_factor")
         ws_wide = tiles("ws_wide", 2 * KG, [P, PACK * WIDE], BF16)
         ws_grouped = tiles("ws_grouped", 2, [P, KG * WIDE * PACK], BF16)
         ws_codes = tiles("ws_codes", NB, [P, KG * WIDE], U32)
         ws_planes = tiles("ws_planes", NB, [P, KG * WIDE], U8)
-        wd_codes = keep.tile([P, KG, 2 * B], U8, name="wd_codes", align_bytes=ALIGN)
+        wd_codes = tiles("wd_codes", 2, [P, KG, B], U8)
         wd_planes = keep.tile([P, KG, B], U8, name="wd_planes", align_bytes=ALIGN)
         noise_col = keep.tile([P, MG, PACK], BF16, name="noise_col")
         s_codes = tiles("s_codes", MG, [P, B], U32)
@@ -93,8 +95,9 @@ def tile_monopulse_ratio_matrix_s11_kernel(tc, x, ws_bytes, ws_scale, wd_words, 
         x_rows = x.rearrange("(g p t) k -> g p t k", p=P, t=PACK)
 
         def ws_load(part):
+            c0, n = WS_LOADS[part]
             for g in range(KG):
-                nc.sync.dma_start(out=ws_raw[KG * part + g][:], in_=ws_rows[g][:, :, part * WS_LOAD : (part + 1) * WS_LOAD])
+                nc.sync.dma_start(out=ws_raw[part][g][:], in_=ws_rows[g][:, :, c0 : c0 + n])
 
         def x_load(gm):
             n = X_LOAD[gm]
@@ -113,18 +116,21 @@ def tile_monopulse_ratio_matrix_s11_kernel(tc, x, ws_bytes, ws_scale, wd_words, 
                 out=wd_planes[32 * q : 32 * q + 4, :, :].bitcast(I32),
                 in_=wd_scales[:, 4 * q : 4 * q + 4, :].rearrange("g r n -> r g n").bitcast(I32),
             )
-        nc.sync.dma_start(out=wd_codes[:], in_=wd_words.rearrange("g p n -> p g n"))
+        wd_rows = wd_words.rearrange("g p n -> p g n")
+        nc.sync.dma_start(out=wd_codes[0][:], in_=wd_rows[:, :, :B])
         x_load(2)
         ws_load(1)
+        nc.sync.dma_start(out=wd_codes[1][:], in_=wd_rows[:, :, B:])
         make_identity(nc, ident[:])
         nc.scalar.activation(out=warm[:], in_=one[:], func=ACT.Abs_reciprocal_sqrt)
 
-        def ws_widen(j, g, vector_slots=0):
+        def ws_widen(j, g, vector_slots):
             n = P * WIDTHS[j]
-            part, c0 = divmod(P * FIRST[j], WS_LOAD)
+            part = max(i for i, (first, beams) in enumerate(WS_LOADS) if first <= P * FIRST[j])
+            c0 = P * FIRST[j] - WS_LOADS[part][0]
             for t in range(PACK):
                 dst = ws_wide[KG * (j % 2) + g][:, t * n : (t + 1) * n]
-                src = ws_raw[KG * part + g][:, t, c0 : c0 + n].bitcast(FP8)
+                src = ws_raw[part][g][:, t, c0 : c0 + n].bitcast(FP8)
                 if t < vector_slots:
                     nc.vector.tensor_scalar(out=dst, in0=src, scalar1=ws_factor[:, g, t : t + 1], scalar2=None, op0=MULT)
                 else:
@@ -137,9 +143,12 @@ def tile_monopulse_ratio_matrix_s11_kernel(tc, x, ws_bytes, ws_scale, wd_words, 
                 in_=ws_wide[KG * (j % 2) + g][:, :n].rearrange("p (t c i) -> p c t i", i=COPY_RUN, t=PACK),
             )
 
-        def ws_quantise(j):
-            n = KG * P * WIDTHS[j]
-            nc.vector.quantize_mx(out=ws_codes[j][:, :n].bitcast(FP8X4), scales=ws_planes[j][:, :n], in_=ws_grouped[j % 2][:, : n * PACK])
+        def ws_quantise(j, g0=0, g1=KG):
+            n = P * WIDTHS[j]
+            nc.vector.quantize_mx(
+                out=ws_codes[j][:, g0 * n : g1 * n].bitcast(FP8X4), scales=ws_planes[j][:, g0 * n : g1 * n],
+                in_=ws_grouped[j % 2][:, g0 * n * PACK : g1 * n * PACK],
+            )
 
         def x_transpose(gm, t):
             take(("x", gm, t))
@@ -202,7 +211,8 @@ def tile_monopulse_ratio_matrix_s11_kernel(tc, x, ws_bytes, ws_scale, wd_words, 
         def project_d(u):
             j, gm = ORDER[u]
             for h in beam_tiles(u):
-                project(("d", u, h), gm, wd_codes, wd_planes, (FIRST[j] + h) * P, 2, FP4X4)
+                half, c0 = divmod((FIRST[j] + h) * P, B // 2)
+                project(("d", u, h), gm, wd_codes[half], wd_planes[:, :, half * B // 2 :], c0, 2, FP4X4)
 
         def s16(u):
             return (ring[u] if u < LAG else s_rounded[u % 2])[:, : values(u)]
@@ -232,16 +242,12 @@ def tile_monopulse_ratio_matrix_s11_kernel(tc, x, ws_bytes, ws_scale, wd_words, 
                     func=ACT.Abs_reciprocal_sqrt, bias=noise_col[:, ORDER[u][1], t : t + 1],
                 )
 
-        def is_wide(u):
-            return values(u) == PACK * WIDE
-
-        def root_square_gpsimd(u):
-            n = values(u) - ROOT_SCALAR * is_wide(u)
-            nc.gpsimd.tensor_tensor(out=reciprocal(u)[:, :n], in0=root[u % 2][:, :n], in1=root[u % 2][:, :n], op=MULT)
-
-        def root_square_scalar(u):
-            n = values(u) - ROOT_SCALAR
-            nc.scalar.activation(out=reciprocal(u)[:, n:], in_=root[u % 2][:, n : values(u)], func=ACT.Square)
+        def root_square(u, on_scalar):
+            n = values(u) - ROOT_SCALAR[len(beam_tiles(u))]
+            if on_scalar:
+                nc.scalar.activation(out=reciprocal(u)[:, n:], in_=root[u % 2][:, n : values(u)], func=ACT.Square)
+            else:
+                nc.gpsimd.tensor_tensor(out=reciprocal(u)[:, :n], in0=root[u % 2][:, :n], in1=root[u % 2][:, :n], op=MULT)
 
         def ratio(u, h):
             cols = slice(h * P, (h + 1) * P)
@@ -258,13 +264,12 @@ def tile_monopulse_ratio_matrix_s11_kernel(tc, x, ws_bytes, ws_scale, wd_words, 
             cols = slice(FIRST[j] * P, FIRST[j + 1] * P)
             nc.vector.quantize_mx(out=codes[gm][:, cols].bitcast(FP8X4), scales=planes[gm][:, cols], in_=src)
 
-        def out_passes(piece, groups):
+        def out_passes(piece):
             row, rows, c0, width = piece
-            if piece not in held:
-                take(piece)
+            take(piece)
             for i in range(rows):
                 r = slice((row + i) * P, (row + i + 1) * P)
-                for gm in groups:
+                for gm in range(MG):
                     nc.tensor.matmul_mx(
                         out=held[piece][:, i * width : (i + 1) * width],
                         lhsT=r_codes[gm][:, r].bitcast(FP8X4), lhsT_scale=r_planes[gm][:, r],
@@ -299,10 +304,10 @@ def tile_monopulse_ratio_matrix_s11_kernel(tc, x, ws_bytes, ws_scale, wd_words, 
         step_of = {unit: u for u, unit in enumerate(ORDER)}
         block_of = [j for j in range(NB) for h in range(WIDTHS[j])]
 
-        def ready(piece, gm):
+        def ready(piece):
             row, rows, c0, width = piece
-            r_step = max(step_of[block_of[r], gm] + LAG for r in range(row, row + rows))
-            s_step = max(step_of[block_of[c], gm] for c in range(c0 // P, (c0 + width) // P))
+            r_step = max(step_of[block_of[r], MG - 1] + LAG for r in range(row, row + rows))
+            s_step = max(step_of[block_of[c], MG - 1] for c in range(c0 // P, (c0 + width) // P))
             return max(r_step, s_step)
 
         plan = pieces(0, FIRST[SHARED], 0, FIRST[SHARED])
@@ -311,17 +316,12 @@ def tile_monopulse_ratio_matrix_s11_kernel(tc, x, ws_bytes, ws_scale, wd_words, 
             if j < NB - 1:
                 plan = plan + pieces(FIRST[j], FIRST[j + 1], 0, FIRST[j + 1])
         plan = plan + [(FIRST[NB - 1], 1, c0, LAST_WIDTH) for c0 in range(0, B, LAST_WIDTH)]
-        plan = sorted(plan, key=lambda piece: ready(piece, MG - 1))
-        done = {piece: 0 for piece in plan}
+        plan = sorted(plan, key=ready)
 
-        widen_at, interleave_at, quantise_at = {}, {}, {}
+        ws_phase = {}
         for j in range(SHARED, NB):
-            due = step_of[j, 0] - 2
-            for g in range(KG):
-                ahead = (KG - 1 - g) * (WIDTHS[j] - 1)
-                widen_at.setdefault(due - 2 - ahead, []).append((j, g))
-                interleave_at.setdefault(due - 1 - ahead, []).append((j, g))
-            quantise_at[due] = j
+            for phase in range(3):
+                ws_phase[step_of[j, 0] - WS_AHEAD - 2 + phase] = (j, phase)
 
         for g in range(KG):
             ws_widen(0, g, PACK // 2)
@@ -345,73 +345,87 @@ def tile_monopulse_ratio_matrix_s11_kernel(tc, x, ws_bytes, ws_scale, wd_words, 
         for t in range(2):
             x_copy(1, t, False)
         ws_interleave(1, 1)
+        x_quantise(1, 0, 2, range(KG))
         ws_quantise(1)
 
         closed = []
         for k in range(UNITS + LAG + 1):
             has_s, has_r = k < UNITS, LAG <= k < UNITS + LAG
+            wide = has_s and len(beam_tiles(k)) == 2
             x_gm, x_t = divmod(PACK + 2 + 2 * k, PACK)
             has_x = x_gm < MG
-            x_from = x_t if k else 0
-            split = P - ROUND_SCALAR if has_s and is_wide(k) and not has_x and not closed else P
+            split = ROUND_SCALAR if wide and not has_x else 0
+            emptying = closed
+            closed = [piece for piece in plan if ready(piece) < k][: 2 if wide else 1]
+            plan = [piece for piece in plan if piece not in closed]
+
+            s_work = [(len(beam_tiles(k + 1)), project_s, k + 1)] if k + 1 < UNITS else []
+            d_work = [(len(beam_tiles(k + 1 - LAG)), project_d, k + 1 - LAG)] if 0 <= k + 1 - LAG < UNITS else []
+            o_work = [(1, out_passes, piece) for piece in closed]
+            todo = s_work + o_work + d_work if wide else s_work + d_work + o_work
+
+            def multiply():
+                while todo and todo[0][0] <= len(free):
+                    banks, call, argument = todo.pop(0)
+                    call(argument)
 
             if has_x:
                 x_transpose(x_gm, x_t)
                 x_transpose(x_gm, x_t + 1)
+            multiply()
             if has_s:
                 for h in beam_tiles(k):
                     s_square(k, h)
-                if split < P:
-                    s_round(k, 1, split, P, False)
             if has_r:
                 for h in beam_tiles(k - LAG):
                     ratio(k - LAG, h)
-            for i, piece in enumerate(closed):
-                store(piece, k >= step_of[NB - 1, 0] and i % 2 == 1)
-            if 1 <= k <= UNITS and is_wide(k - 1):
-                root_square_scalar(k - 1)
-            if k + 1 < UNITS:
-                project_s(k + 1)
-            if 0 <= k + 1 - LAG < UNITS:
-                project_d(k + 1 - LAG)
-            if has_x:
-                x_copy(x_gm, x_t, False)
+            multiply()
+            if split:
+                s_round(k, 0, 0, split, False)
+            for i, piece in enumerate(emptying):
+                store(piece, i % 2 == 1)
+                multiply()
             if has_s:
                 for h in beam_tiles(k):
-                    s_round(k, h, 0, split if h == 1 else P, True)
+                    s_round(k, h, split if h == 0 else 0, P, True)
                     give(("s", k, h))
-                inverse_root(k)
-            for j, g in widen_at.get(k, []):
-                ws_widen(j, g)
-            if has_x:
+                    multiply()
+            if has_x and not has_r:
                 x_copy(x_gm, x_t + 1, True)
-
-            closed = []
-            spare = BANKS - sum(len(beam_tiles(u)) for u in (k + 1, k + 2, k + 2 - LAG) if u < UNITS) - 2 * (k + 1 < MG)
-            for piece in plan:
-                groups = [gm for gm in range(done[piece], MG) if ready(piece, gm) < k]
-                whole = done[piece] + len(groups) == MG
-                opened = sum(0 < n < MG for n in done.values())
-                if groups and (piece in held or free and (whole or piece[1] == 1 and opened < spare)):
-                    out_passes(piece, groups)
-                    done[piece] = done[piece] + len(groups)
-                    if whole:
-                        closed.append(piece)
-
-            for j, g in interleave_at.get(k, []):
-                ws_interleave(j, g)
-            if k in quantise_at:
-                ws_quantise(quantise_at[k])
+            if 1 <= k <= UNITS:
+                root_square(k - 1, True)
             if has_x:
-                x_quantise(x_gm, x_from, x_t + 2, range(KG if has_r else KG - 1))
+                x_copy(x_gm, x_t, False)
+                if has_r:
+                    x_copy(x_gm, x_t + 1, False)
+            multiply()
+            if has_s:
+                inverse_root(k)
+
+            j, phase = ws_phase.get(k, (None, None))
+            if has_x and has_r:
+                x_quantise(x_gm, x_t, x_t + 2, range(KG))
+            for g in range(KG):
+                if phase == 0:
+                    ws_widen(j, g, WIDEN_VECTOR[WIDTHS[j]])
+                if phase == 1:
+                    ws_interleave(j, g)
+            if phase == 2:
+                ws_quantise(j)
+            if has_x and not has_r:
+                x_quantise(x_gm, x_t, x_t + 2, range(KG - 1))
             if has_r:
                 quantise(r16(k - LAG), k - LAG, r_codes, r_planes)
             if has_s:
                 quantise(s16(k), k, s_codes, s_planes)
-            if k < LAG:
-                x_quantise(x_gm, x_from, x_t + 2, [KG - 1])
+            if has_x and not has_r:
+                x_quantise(x_gm, x_t, x_t + 2, [KG - 1])
             if has_s:
-                root_square_gpsimd(k)
-        for i, piece in enumerate(closed):
-            store(piece, i % 2 == 0)
+                root_square(k, False)
+            assert not todo
+        for piece in closed:
+            store(piece, len(stored) % 2 == 0)
+        for piece in plan:
+            out_passes(piece)
+            store(piece, len(stored) % 2 == 0)
         assert sum(rows * width for row, rows, c0, width in stored) * P == B * B

@@ -34,13 +34,13 @@ SHARED = 2
 ORDER = [(j, gm) for gm in range(MG) for j in range(SHARED)] + [(j, gm) for j in range(SHARED, NB) for gm in range(MG)]
 UNITS = len(ORDER)
 LAG = 2
-WS_LOADS = [(0, 512), (512, 512)]
+WS_LOADS = [(0, 512), (512, 256), (768, 256)]
 X_LOAD = [1, 2, 2]
 RATIO_RUN = 2
 COPY_RUN = 4
-ROOT_SCALAR = {1: 256, 2: 384}
+ROOT_SCALAR = {1: 128, 2: 384}
 ROUND_SCALAR = 96
-WIDEN_VECTOR = {1: 2, 2: 4}
+WIDEN_VECTOR = {1: 3, 2: 4}
 WS_AHEAD = 3
 LAST_WIDTH = 256
 RESULTS = 8
@@ -57,9 +57,9 @@ def tile_monopulse_ratio_matrix_s11_kernel(tc, x, ws_bytes, ws_scale, wd_words, 
             return [keep.tile(shape, dtype, name="%s%d" % (name, i), align_bytes=ALIGN) for i in range(n)]
 
         x_raw = [tiles("x_raw%d_" % gm, PACK // n, [P, n * K], BF16) for gm, n in enumerate(X_LOAD)]
-        x_grouped = tiles("x_grouped", 2, [P, KG, PASS, PACK], BF16)
-        x_codes = tiles("x_codes", MG, [P, KG, PASS], U32)
-        x_planes = tiles("x_planes", MG, [P, KG, PASS], U8)
+        x_grouped = tiles("x_grouped", 2, [P, PACK, KG * P * PACK], BF16)
+        x_codes = tiles("x_codes", MG, [P, PACK, KG, P], U32)
+        x_planes = tiles("x_planes", MG, [P, PACK, KG, P], U8)
         ws_raw = [tiles("ws_raw%d_" % i, KG, [P, PACK, n], U8) for i, (c0, n) in enumerate(WS_LOADS)]
         ws_factor = keep.tile([P, KG, PACK], F32, name="ws_factor")
         ws_wide = tiles("ws_wide", 2 * KG, [P, PACK * WIDE], BF16)
@@ -99,9 +99,9 @@ def tile_monopulse_ratio_matrix_s11_kernel(tc, x, ws_bytes, ws_scale, wd_words, 
             for g in range(KG):
                 nc.sync.dma_start(out=ws_raw[part][g][:], in_=ws_rows[g][:, :, c0 : c0 + n])
 
-        def x_load(gm):
+        def x_load(gm, first=0, last=PACK):
             n = X_LOAD[gm]
-            for i, dst in enumerate(x_raw[gm]):
+            for i, dst in list(enumerate(x_raw[gm]))[first:last]:
                 nc.sync.dma_start(out=dst[:], in_=x_rows[gm][:, n * i : n * (i + 1), :].rearrange("p t k -> p (t k)"))
 
         nc.scalar.dma_start(out=ws_factor[:], in_=ws_scale.rearrange("(g p t) o -> p g (t o)", p=P, t=PACK))
@@ -109,8 +109,11 @@ def tile_monopulse_ratio_matrix_s11_kernel(tc, x, ws_bytes, ws_scale, wd_words, 
         nc.vector.memset(wd_planes[:].rearrange("p g n -> p (g n)").bitcast(I32), 0)
         ws_load(0)
         x_load(0)
-        x_load(1)
+        x_load(1, 0, 1)
+        ws_load(1)
+        x_load(1, 1, 2)
         nc.sync.dma_start(out=noise_col[:], in_=noise.rearrange("(g p t) -> p g t", p=P, t=PACK))
+        x_load(2, 0, 1)
         for q in range(4):
             nc.sync.dma_start(
                 out=wd_planes[32 * q : 32 * q + 4, :, :].bitcast(I32),
@@ -118,8 +121,8 @@ def tile_monopulse_ratio_matrix_s11_kernel(tc, x, ws_bytes, ws_scale, wd_words, 
             )
         wd_rows = wd_words.rearrange("g p n -> p g n")
         nc.sync.dma_start(out=wd_codes[0][:], in_=wd_rows[:, :, :B])
-        x_load(2)
-        ws_load(1)
+        x_load(2, 1, 2)
+        ws_load(2)
         nc.sync.dma_start(out=wd_codes[1][:], in_=wd_rows[:, :, B:])
         make_identity(nc, ident[:])
         nc.scalar.activation(out=warm[:], in_=one[:], func=ACT.Abs_reciprocal_sqrt)
@@ -160,7 +163,7 @@ def tile_monopulse_ratio_matrix_s11_kernel(tc, x, ws_bytes, ws_scale, wd_words, 
                     nc.tensor.transpose(bank[:, g, u, :], words[:, 2 * P * g + u : 2 * P * (g + 1) : 2], ident[:])
 
         def x_copy(gm, t, on_vector):
-            dst = x_grouped[gm % 2][:].bitcast(F32)[:, :, t * P : (t + 1) * P, :]
+            dst = x_grouped[gm % 2][:, t, :].bitcast(F32).rearrange("p (g r u) -> p g r u", g=KG, u=2)
             src = held["x", gm, t][:].rearrange("p (g u r) -> p g r u", g=KG, u=2)
             if on_vector:
                 nc.vector.tensor_copy(out=dst, in_=src)
@@ -168,13 +171,12 @@ def tile_monopulse_ratio_matrix_s11_kernel(tc, x, ws_bytes, ws_scale, wd_words, 
                 nc.scalar.copy(out=dst, in_=src)
             give(("x", gm, t))
 
-        def x_quantise(gm, t0, t1, passes):
-            cols = slice(t0 * P, t1 * P)
-            for g in passes:
-                nc.vector.quantize_mx(
-                    out=x_codes[gm][:, g, cols].bitcast(FP8X4), scales=x_planes[gm][:, g, cols],
-                    in_=x_grouped[gm % 2][:, g, cols, :].rearrange("p r t -> p (r t)"),
-                )
+        def x_quantise(gm, t0, t1):
+            nc.vector.quantize_mx(
+                out=x_codes[gm][:, t0:t1].rearrange("p t g r -> p (t g r)").bitcast(FP8X4),
+                scales=x_planes[gm][:, t0:t1].rearrange("p t g r -> p (t g r)"),
+                in_=x_grouped[gm % 2][:, t0:t1].rearrange("p t n -> p (t n)"),
+            )
 
         def beam_tiles(u):
             return range(WIDTHS[ORDER[u][0]])
@@ -191,11 +193,10 @@ def tile_monopulse_ratio_matrix_s11_kernel(tc, x, ws_bytes, ws_scale, wd_words, 
         def project(key, gm, codes, planes, c0, per_beam, dtype):
             take(key)
             for t in range(PACK):
-                rows = slice(t * P, (t + 1) * P)
                 for g in range(KG):
                     nc.tensor.matmul_mx(
                         out=by_slot(held[key][:])[:, t, :],
-                        lhsT=x_codes[gm][:, g, rows].bitcast(FP8X4), lhsT_scale=x_planes[gm][:, g, rows],
+                        lhsT=x_codes[gm][:, t, g].bitcast(FP8X4), lhsT_scale=x_planes[gm][:, t, g],
                         rhs=codes[:, g, per_beam * c0 : per_beam * (c0 + P)].bitcast(dtype), rhs_scale=planes[:, g, c0 : c0 + P],
                         start=(g == 0), stop=(g == KG - 1),
                     )
@@ -310,11 +311,11 @@ def tile_monopulse_ratio_matrix_s11_kernel(tc, x, ws_bytes, ws_scale, wd_words, 
             s_step = max(step_of[block_of[c], MG - 1] for c in range(c0 // P, (c0 + width) // P))
             return max(r_step, s_step)
 
+        wide_tiles = FIRST[NB - 2]
         plan = pieces(0, FIRST[SHARED], 0, FIRST[SHARED])
-        for j in range(SHARED, NB):
-            plan = plan + pieces(0, FIRST[j], FIRST[j], FIRST[j + 1])
-            if j < NB - 1:
-                plan = plan + pieces(FIRST[j], FIRST[j + 1], 0, FIRST[j + 1])
+        for j in range(SHARED, NB - 2):
+            plan = plan + pieces(0, FIRST[j], FIRST[j], FIRST[j + 1]) + pieces(FIRST[j], FIRST[j + 1], 0, FIRST[j + 1])
+        plan = plan + pieces(0, wide_tiles, wide_tiles, FIRST[NB]) + pieces(wide_tiles, FIRST[NB - 1], 0, FIRST[NB])
         plan = plan + [(FIRST[NB - 1], 1, c0, LAST_WIDTH) for c0 in range(0, B, LAST_WIDTH)]
         plan = sorted(plan, key=ready)
 
@@ -326,27 +327,29 @@ def tile_monopulse_ratio_matrix_s11_kernel(tc, x, ws_bytes, ws_scale, wd_words, 
         for g in range(KG):
             ws_widen(0, g, PACK // 2)
         ws_interleave(0, 0)
-        ws_widen(1, 0, PACK // 2)
+        ws_widen(1, 0, 1)
         ws_interleave(0, 1)
         for t in range(PACK):
             x_transpose(0, t)
         x_copy(0, 0, False)
         x_copy(0, 1, False)
-        ws_widen(1, 1, PACK)
+        ws_widen(1, 1, 3)
         ws_quantise(0)
         x_copy(0, 2, False)
-        x_quantise(0, 0, 2, range(KG))
+        x_quantise(0, 0, 2)
         x_copy(0, 3, False)
         for t in range(2):
             x_transpose(1, t)
         ws_interleave(1, 0)
-        x_quantise(0, 2, PACK, range(KG))
+        x_quantise(0, 2, PACK)
         project_s(0)
         for t in range(2):
             x_copy(1, t, False)
+        ws_widen(SHARED, 0, 0)
         ws_interleave(1, 1)
-        x_quantise(1, 0, 2, range(KG))
+        x_quantise(1, 0, 2)
         ws_quantise(1)
+        ws_interleave(SHARED, 0)
 
         closed = []
         for k in range(UNITS + LAG + 1):
@@ -404,8 +407,8 @@ def tile_monopulse_ratio_matrix_s11_kernel(tc, x, ws_bytes, ws_scale, wd_words, 
 
             j, phase = ws_phase.get(k, (None, None))
             if has_x and has_r:
-                x_quantise(x_gm, x_t, x_t + 2, range(KG))
-            for g in range(KG):
+                x_quantise(x_gm, x_t, x_t + 2)
+            for g in range(1 if j == SHARED else 0, KG):
                 if phase == 0:
                     ws_widen(j, g, WIDEN_VECTOR[WIDTHS[j]])
                 if phase == 1:
@@ -413,13 +416,13 @@ def tile_monopulse_ratio_matrix_s11_kernel(tc, x, ws_bytes, ws_scale, wd_words, 
             if phase == 2:
                 ws_quantise(j)
             if has_x and not has_r:
-                x_quantise(x_gm, x_t, x_t + 2, range(KG - 1))
+                x_quantise(x_gm, x_t, x_t + 1)
             if has_r:
                 quantise(r16(k - LAG), k - LAG, r_codes, r_planes)
             if has_s:
                 quantise(s16(k), k, s_codes, s_planes)
             if has_x and not has_r:
-                x_quantise(x_gm, x_t, x_t + 2, [KG - 1])
+                x_quantise(x_gm, x_t + 1, x_t + 2)
             if has_s:
                 root_square(k, False)
             assert not todo

@@ -16,6 +16,7 @@ FP8X4 = mybir.dt.float8_e4m3fn_x4
 FP4X4 = mybir.dt.float4_e2m1fn_x4
 ACT = mybir.ActivationFunctionType
 MULT = mybir.AluOpType.mult
+ADD = mybir.AluOpType.add
 
 P = 128
 PACK = 4
@@ -35,12 +36,13 @@ ORDER = [(j, gm) for gm in range(MG) for j in range(SHARED)] + [(j, gm) for j in
 UNITS = len(ORDER)
 LAG = 2
 WS_LOADS = [(0, 512), (512, 256), (768, 256)]
-X_LOAD = [1, 2, 2]
+X_LOAD = [1, 1, 1]
 RATIO_RUN = 2
 COPY_RUN = 4
 ROOT_SCALAR = {1: 128, 2: 384}
+ROOT_SCALAR_LONG = 192
 ROUND_SCALAR = 96
-WIDEN_VECTOR = {1: 3, 2: 4}
+WIDEN_VECTOR = 3
 WS_AHEAD = 3
 LAST_WIDTH = 256
 RESULTS = 8
@@ -109,9 +111,9 @@ def tile_monopulse_ratio_matrix_s11_kernel(tc, x, ws_bytes, ws_scale, wd_words, 
         nc.vector.memset(wd_planes[:].rearrange("p g n -> p (g n)").bitcast(I32), 0)
         ws_load(0)
         x_load(0)
-        x_load(1, 0, 1)
+        x_load(1, 0, 3)
         ws_load(1)
-        x_load(1, 1, 2)
+        x_load(1, 3, 4)
         nc.sync.dma_start(out=noise_col[:], in_=noise.rearrange("(g p t) -> p g t", p=P, t=PACK))
         x_load(2, 0, 1)
         for q in range(4):
@@ -121,7 +123,7 @@ def tile_monopulse_ratio_matrix_s11_kernel(tc, x, ws_bytes, ws_scale, wd_words, 
             )
         wd_rows = wd_words.rearrange("g p n -> p g n")
         nc.sync.dma_start(out=wd_codes[0][:], in_=wd_rows[:, :, :B])
-        x_load(2, 1, 2)
+        x_load(2, 1, 4)
         ws_load(2)
         nc.sync.dma_start(out=wd_codes[1][:], in_=wd_rows[:, :, B:])
         make_identity(nc, ident[:])
@@ -139,18 +141,23 @@ def tile_monopulse_ratio_matrix_s11_kernel(tc, x, ws_bytes, ws_scale, wd_words, 
                 else:
                     nc.scalar.activation(out=dst, in_=src, func=ACT.Copy, scale=ws_factor[:, g, t : t + 1])
 
-        def ws_interleave(j, g):
+        def grouped(j):
+            return ws_grouped[(j - (j >= SHARED)) % 2]
+
+        def ws_interleave(j, g, on_gpsimd=False):
             n = PACK * P * WIDTHS[j]
-            nc.vector.tensor_copy(
-                out=ws_grouped[j % 2][:, g * n : (g + 1) * n].rearrange("p (c i t) -> p c t i", i=COPY_RUN, t=PACK),
-                in_=ws_wide[KG * (j % 2) + g][:, :n].rearrange("p (t c i) -> p c t i", i=COPY_RUN, t=PACK),
-            )
+            dst = grouped(j)[:, g * n : (g + 1) * n].rearrange("p (c i t) -> p c t i", i=COPY_RUN, t=PACK)
+            src = ws_wide[KG * (j % 2) + g][:, :n].rearrange("p (t c i) -> p c t i", i=COPY_RUN, t=PACK)
+            if on_gpsimd:
+                nc.gpsimd.tensor_scalar(out=dst, in0=src, scalar1=1.0, scalar2=0.0, op0=MULT, op1=ADD)
+            else:
+                nc.vector.tensor_copy(out=dst, in_=src)
 
         def ws_quantise(j, g0=0, g1=KG):
             n = P * WIDTHS[j]
             nc.vector.quantize_mx(
                 out=ws_codes[j][:, g0 * n : g1 * n].bitcast(FP8X4), scales=ws_planes[j][:, g0 * n : g1 * n],
-                in_=ws_grouped[j % 2][:, g0 * n * PACK : g1 * n * PACK],
+                in_=grouped(j)[:, g0 * n * PACK : g1 * n * PACK],
             )
 
         def x_transpose(gm, t):
@@ -243,8 +250,10 @@ def tile_monopulse_ratio_matrix_s11_kernel(tc, x, ws_bytes, ws_scale, wd_words, 
                     func=ACT.Abs_reciprocal_sqrt, bias=noise_col[:, ORDER[u][1], t : t + 1],
                 )
 
+        root_scalar = {}
+
         def root_square(u, on_scalar):
-            n = values(u) - ROOT_SCALAR[len(beam_tiles(u))]
+            n = values(u) - root_scalar[u]
             if on_scalar:
                 nc.scalar.activation(out=reciprocal(u)[:, n:], in_=root[u % 2][:, n : values(u)], func=ACT.Square)
             else:
@@ -324,32 +333,33 @@ def tile_monopulse_ratio_matrix_s11_kernel(tc, x, ws_bytes, ws_scale, wd_words, 
             for phase in range(3):
                 ws_phase[step_of[j, 0] - WS_AHEAD - 2 + phase] = (j, phase)
 
-        for g in range(KG):
-            ws_widen(0, g, PACK // 2)
+        ws_widen(0, 0, 2)
+        ws_widen(1, 0, 2)
+        ws_widen(0, 1, 2)
         ws_interleave(0, 0)
-        ws_widen(1, 0, 1)
         ws_interleave(0, 1)
+        ws_widen(1, 1, 2)
         for t in range(PACK):
             x_transpose(0, t)
         x_copy(0, 0, False)
         x_copy(0, 1, False)
-        ws_widen(1, 1, 3)
         ws_quantise(0)
         x_copy(0, 2, False)
         x_quantise(0, 0, 2)
         x_copy(0, 3, False)
-        for t in range(2):
+        for t in range(3):
             x_transpose(1, t)
         ws_interleave(1, 0)
         x_quantise(0, 2, PACK)
         project_s(0)
-        for t in range(2):
+        for t in range(3):
             x_copy(1, t, False)
         ws_widen(SHARED, 0, 0)
         ws_interleave(1, 1)
+        ws_widen(SHARED, 1, PACK)
         x_quantise(1, 0, 2)
         ws_quantise(1)
-        ws_interleave(SHARED, 0)
+        ws_interleave(SHARED, 0, True)
 
         closed = []
         for k in range(UNITS + LAG + 1):
@@ -372,9 +382,9 @@ def tile_monopulse_ratio_matrix_s11_kernel(tc, x, ws_bytes, ws_scale, wd_words, 
                     banks, call, argument = todo.pop(0)
                     call(argument)
 
-            if has_x:
-                x_transpose(x_gm, x_t)
-                x_transpose(x_gm, x_t + 1)
+            turned = [divmod(n, PACK) for n in (PACK + 3 + 2 * k, PACK + 4 + 2 * k) if n < MG * PACK]
+            for slot in turned:
+                x_transpose(*slot)
             multiply()
             if has_s:
                 for h in beam_tiles(k):
@@ -393,14 +403,12 @@ def tile_monopulse_ratio_matrix_s11_kernel(tc, x, ws_bytes, ws_scale, wd_words, 
                     s_round(k, h, split if h == 0 else 0, P, True)
                     give(("s", k, h))
                     multiply()
-            if has_x and not has_r:
-                x_copy(x_gm, x_t + 1, True)
+            for slot in turned[1:]:
+                x_copy(*slot, True)
             if 1 <= k <= UNITS:
                 root_square(k - 1, True)
-            if has_x:
-                x_copy(x_gm, x_t, False)
-                if has_r:
-                    x_copy(x_gm, x_t + 1, False)
+            for slot in turned[:1]:
+                x_copy(*slot, False)
             multiply()
             if has_s:
                 inverse_root(k)
@@ -409,8 +417,8 @@ def tile_monopulse_ratio_matrix_s11_kernel(tc, x, ws_bytes, ws_scale, wd_words, 
             if has_x and has_r:
                 x_quantise(x_gm, x_t, x_t + 2)
             for g in range(1 if j == SHARED else 0, KG):
-                if phase == 0:
-                    ws_widen(j, g, WIDEN_VECTOR[WIDTHS[j]])
+                if phase == 0 and j != SHARED:
+                    ws_widen(j, g, WIDEN_VECTOR)
                 if phase == 1:
                     ws_interleave(j, g)
             if phase == 2:
@@ -424,6 +432,8 @@ def tile_monopulse_ratio_matrix_s11_kernel(tc, x, ws_bytes, ws_scale, wd_words, 
             if has_x and not has_r:
                 x_quantise(x_gm, x_t + 1, x_t + 2)
             if has_s:
+                long_read = k + 1 == LAG or len(closed) == 2
+                root_scalar[k] = ROOT_SCALAR_LONG if wide and long_read else ROOT_SCALAR[len(beam_tiles(k))]
                 root_square(k, False)
             assert not todo
         for piece in closed:

@@ -16,7 +16,6 @@ FP8X4 = mybir.dt.float8_e4m3fn_x4
 FP4X4 = mybir.dt.float4_e2m1fn_x4
 ACT = mybir.ActivationFunctionType
 MULT = mybir.AluOpType.mult
-ADD = mybir.AluOpType.add
 
 P = 128
 PACK = 4
@@ -42,7 +41,7 @@ COPY_RUN = 4
 ROOT_SCALAR = {1: 128, 2: 384}
 ROOT_SCALAR_LONG = 192
 ROUND_SCALAR = 96
-WIDEN_VECTOR = 3
+WIDEN_VECTOR = 2
 WS_AHEAD = 3
 LAST_WIDTH = 256
 RESULTS = 8
@@ -141,23 +140,17 @@ def tile_monopulse_ratio_matrix_s11_kernel(tc, x, ws_bytes, ws_scale, wd_words, 
                 else:
                     nc.scalar.activation(out=dst, in_=src, func=ACT.Copy, scale=ws_factor[:, g, t : t + 1])
 
-        def grouped(j):
-            return ws_grouped[(j - (j >= SHARED)) % 2]
-
-        def ws_interleave(j, g, on_gpsimd=False):
+        def ws_interleave(j, g):
             n = PACK * P * WIDTHS[j]
-            dst = grouped(j)[:, g * n : (g + 1) * n].rearrange("p (c i t) -> p c t i", i=COPY_RUN, t=PACK)
+            dst = ws_grouped[j % 2][:, g * n : (g + 1) * n].rearrange("p (c i t) -> p c t i", i=COPY_RUN, t=PACK)
             src = ws_wide[KG * (j % 2) + g][:, :n].rearrange("p (t c i) -> p c t i", i=COPY_RUN, t=PACK)
-            if on_gpsimd:
-                nc.gpsimd.tensor_scalar(out=dst, in0=src, scalar1=1.0, scalar2=0.0, op0=MULT, op1=ADD)
-            else:
-                nc.vector.tensor_copy(out=dst, in_=src)
+            nc.vector.tensor_copy(out=dst, in_=src)
 
         def ws_quantise(j, g0=0, g1=KG):
             n = P * WIDTHS[j]
             nc.vector.quantize_mx(
                 out=ws_codes[j][:, g0 * n : g1 * n].bitcast(FP8X4), scales=ws_planes[j][:, g0 * n : g1 * n],
-                in_=grouped(j)[:, g0 * n * PACK : g1 * n * PACK],
+                in_=ws_grouped[j % 2][:, g0 * n * PACK : g1 * n * PACK],
             )
 
         def x_transpose(gm, t):
@@ -328,10 +321,9 @@ def tile_monopulse_ratio_matrix_s11_kernel(tc, x, ws_bytes, ws_scale, wd_words, 
         plan = plan + [(FIRST[NB - 1], 1, c0, LAST_WIDTH) for c0 in range(0, B, LAST_WIDTH)]
         plan = sorted(plan, key=ready)
 
-        ws_phase = {}
-        for j in range(SHARED, NB):
-            for phase in range(3):
-                ws_phase[step_of[j, 0] - WS_AHEAD - 2 + phase] = (j, phase)
+        quantise_at = {step_of[j, 0] - WS_AHEAD: j for j in range(SHARED, NB)}
+        interleave_at = {k - (j < NB - 1): j for k, j in quantise_at.items()}
+        widen_at = {k - 1: j for k, j in interleave_at.items() if j > SHARED}
 
         ws_widen(0, 0, 2)
         ws_widen(1, 0, 2)
@@ -359,7 +351,7 @@ def tile_monopulse_ratio_matrix_s11_kernel(tc, x, ws_bytes, ws_scale, wd_words, 
         ws_widen(SHARED, 1, PACK)
         x_quantise(1, 0, 2)
         ws_quantise(1)
-        ws_interleave(SHARED, 0, True)
+        ws_interleave(SHARED, 0)
 
         closed = []
         for k in range(UNITS + LAG + 1):
@@ -413,22 +405,24 @@ def tile_monopulse_ratio_matrix_s11_kernel(tc, x, ws_bytes, ws_scale, wd_words, 
             if has_s:
                 inverse_root(k)
 
-            j, phase = ws_phase.get(k, (None, None))
             if has_x and has_r:
                 x_quantise(x_gm, x_t, x_t + 2)
-            for g in range(1 if j == SHARED else 0, KG):
-                if phase == 0 and j != SHARED:
-                    ws_widen(j, g, WIDEN_VECTOR)
-                if phase == 1:
-                    ws_interleave(j, g)
-            if phase == 2:
-                ws_quantise(j)
+            for g in range(KG):
+                if k in widen_at:
+                    ws_widen(widen_at[k], g, WIDEN_VECTOR)
+                if k in interleave_at and (interleave_at[k], g) != (SHARED, 0):
+                    ws_interleave(interleave_at[k], g)
+            ws_now = KG - (k in interleave_at)
+            if k in quantise_at:
+                ws_quantise(quantise_at[k], 0, ws_now)
             if has_x and not has_r:
                 x_quantise(x_gm, x_t, x_t + 1)
             if has_r:
                 quantise(r16(k - LAG), k - LAG, r_codes, r_planes)
             if has_s:
                 quantise(s16(k), k, s_codes, s_planes)
+            if k in quantise_at and ws_now < KG:
+                ws_quantise(quantise_at[k], ws_now, KG)
             if has_x and not has_r:
                 x_quantise(x_gm, x_t + 1, x_t + 2)
             if has_s:

@@ -68,7 +68,7 @@ def tile_monopulse_ratio_matrix_s11_kernel(tc, x, ws_bytes, ws_scale, wd_words, 
         ws_codes = tiles("ws_codes", NB, [P, KG * WIDE], U32)
         ws_planes = tiles("ws_planes", NB, [P, KG * WIDE], U8)
         wd_codes = tiles("wd_codes", 2, [P, KG, B], U8)
-        wd_planes = keep.tile([P, KG, B], U8, name="wd_planes", align_bytes=ALIGN)
+        wd_planes = tiles("wd_planes", 2, [P, KG, B // 2], U8)
         noise_col = keep.tile([P, MG, PACK], BF16, name="noise_col")
         s_codes = tiles("s_codes", MG, [P, B], U32)
         s_planes = tiles("s_planes", MG, [P, B], U8)
@@ -105,26 +105,31 @@ def tile_monopulse_ratio_matrix_s11_kernel(tc, x, ws_bytes, ws_scale, wd_words, 
             for i, dst in list(enumerate(x_raw[gm]))[first:last]:
                 nc.sync.dma_start(out=dst[:], in_=x_rows[gm][:, n * i : n * (i + 1), :].rearrange("p t k -> p (t k)"))
 
+        def wd_load(half):
+            cols = slice(half * B // 2, (half + 1) * B // 2)
+            for q in range(4):
+                nc.sync.dma_start(
+                    out=wd_planes[half][32 * q : 32 * q + 4, :, :].bitcast(I32),
+                    in_=wd_scales[:, 4 * q : 4 * q + 4, cols].rearrange("g r n -> r g n").bitcast(I32),
+                )
+            words = wd_words.rearrange("g p n -> p g n")
+            nc.sync.dma_start(out=wd_codes[half][:], in_=words[:, :, half * B : (half + 1) * B])
+
         nc.scalar.dma_start(out=ws_factor[:], in_=ws_scale.rearrange("(g p t) o -> p g (t o)", p=P, t=PACK))
         nc.vector.memset(one[:], 1.0)
-        nc.vector.memset(wd_planes[:].rearrange("p g n -> p (g n)").bitcast(I32), 0)
+        for plane in wd_planes:
+            nc.vector.memset(plane[:].rearrange("p g n -> p (g n)").bitcast(I32), 0)
         ws_load(0)
         x_load(0)
         x_load(1, 0, 3)
         ws_load(1)
         x_load(1, 3, 4)
         nc.sync.dma_start(out=noise_col[:], in_=noise.rearrange("(g p t) -> p g t", p=P, t=PACK))
-        x_load(2, 0, 1)
-        for q in range(4):
-            nc.sync.dma_start(
-                out=wd_planes[32 * q : 32 * q + 4, :, :].bitcast(I32),
-                in_=wd_scales[:, 4 * q : 4 * q + 4, :].rearrange("g r n -> r g n").bitcast(I32),
-            )
-        wd_rows = wd_words.rearrange("g p n -> p g n")
-        nc.sync.dma_start(out=wd_codes[0][:], in_=wd_rows[:, :, :B])
-        x_load(2, 1, 4)
+        x_load(2, 0, 3)
+        wd_load(0)
+        x_load(2, 3, 4)
         ws_load(2)
-        nc.sync.dma_start(out=wd_codes[1][:], in_=wd_rows[:, :, B:])
+        wd_load(1)
         make_identity(nc, ident[:])
         nc.scalar.activation(out=warm[:], in_=one[:], func=ACT.Abs_reciprocal_sqrt)
 
@@ -213,7 +218,7 @@ def tile_monopulse_ratio_matrix_s11_kernel(tc, x, ws_bytes, ws_scale, wd_words, 
             j, gm = ORDER[u]
             for h in beam_tiles(u):
                 half, c0 = divmod((FIRST[j] + h) * P, B // 2)
-                project(("d", u, h), gm, wd_codes[half], wd_planes[:, :, half * B // 2 :], c0, 2, FP4X4)
+                project(("d", u, h), gm, wd_codes[half], wd_planes[half], c0, 2, FP4X4)
 
         def s16(u):
             return (ring[u] if u < LAG else s_rounded[u % 2])[:, : values(u)]

@@ -43,6 +43,7 @@ ROOT_SCALAR_LONG = 192
 ROUND_SCALAR = 96
 WIDEN_VECTOR = 2
 WS_AHEAD = 3
+WARM_UPS = 4
 LAST_WIDTH = 256
 RESULTS = 8
 
@@ -182,6 +183,12 @@ def tile_monopulse_ratio_matrix_s11_kernel(tc, x, ws_bytes, ws_scale, wd_words, 
                 scales=x_planes[gm][:, t0:t1].rearrange("p t g r -> p (t g r)"),
                 in_=x_grouped[gm % 2][:, t0:t1].rearrange("p t n -> p (t n)"),
             )
+
+        def warm_tensor(n):
+            take("warm")
+            for i in range(n):
+                nc.tensor.matmul(out=held["warm"][:, :P], lhsT=ident[:], rhs=ident[:], start=True, stop=True)
+            give("warm")
 
         def beam_tiles(u):
             return range(WIDTHS[ORDER[u][0]])
@@ -336,6 +343,7 @@ def tile_monopulse_ratio_matrix_s11_kernel(tc, x, ws_bytes, ws_scale, wd_words, 
         ws_interleave(0, 0)
         ws_interleave(0, 1)
         ws_widen(1, 1, 2)
+        warm_tensor(WARM_UPS)
         for t in range(PACK):
             x_transpose(0, t)
         x_copy(0, 0, False)

@@ -16,6 +16,7 @@ FP8X4 = mybir.dt.float8_e4m3fn_x4
 FP4X4 = mybir.dt.float4_e2m1fn_x4
 ACT = mybir.ActivationFunctionType
 MULT = mybir.AluOpType.mult
+ADD = mybir.AluOpType.add
 
 P = 128
 PACK = 4
@@ -38,10 +39,10 @@ WS_LOADS = [(0, 512), (512, 256), (768, 256)]
 X_LOAD = [1, 1, 1]
 RATIO_RUN = 2
 COPY_RUN = 4
-ROOT_SCALAR = {1: 128, 2: 384}
+ROOT_SCALAR = {1: 128, 2: 352}
 ROOT_SCALAR_LONG = 192
-ROUND_SCALAR = 96
-WIDEN_VECTOR = 2
+ROUND_SCALAR = 80
+WIDEN_VECTOR = 3
 WS_AHEAD = 3
 WARM_UPS = 4
 LAST_WIDTH = 256
@@ -146,11 +147,14 @@ def tile_monopulse_ratio_matrix_s11_kernel(tc, x, ws_bytes, ws_scale, wd_words, 
                 else:
                     nc.scalar.activation(out=dst, in_=src, func=ACT.Copy, scale=ws_factor[:, g, t : t + 1])
 
-        def ws_interleave(j, g):
+        def ws_interleave(j, g, on_gpsimd=False):
             n = PACK * P * WIDTHS[j]
             dst = ws_grouped[j % 2][:, g * n : (g + 1) * n].rearrange("p (c i t) -> p c t i", i=COPY_RUN, t=PACK)
             src = ws_wide[KG * (j % 2) + g][:, :n].rearrange("p (t c i) -> p c t i", i=COPY_RUN, t=PACK)
-            nc.vector.tensor_copy(out=dst, in_=src)
+            if on_gpsimd:
+                nc.gpsimd.tensor_scalar(out=dst, in0=src, scalar1=1.0, scalar2=0.0, op0=MULT, op1=ADD)
+            else:
+                nc.vector.tensor_copy(out=dst, in_=src)
 
         def ws_quantise(j, g0=0, g1=KG):
             n = P * WIDTHS[j]
@@ -361,10 +365,11 @@ def tile_monopulse_ratio_matrix_s11_kernel(tc, x, ws_bytes, ws_scale, wd_words, 
             x_copy(1, t, False)
         ws_widen(SHARED, 0, 0)
         ws_interleave(1, 1)
-        ws_widen(SHARED, 1, PACK)
         x_quantise(1, 0, 2)
         ws_quantise(1)
+        ws_widen(SHARED, 1, PACK)
         ws_interleave(SHARED, 0)
+        ws_interleave(SHARED, 1, True)
 
         closed = []
         for k in range(UNITS + LAG + 1):
@@ -423,7 +428,7 @@ def tile_monopulse_ratio_matrix_s11_kernel(tc, x, ws_bytes, ws_scale, wd_words, 
             for g in range(KG):
                 if k in widen_at:
                     ws_widen(widen_at[k], g, WIDEN_VECTOR)
-                if k in interleave_at and (interleave_at[k], g) != (SHARED, 0):
+                if k in interleave_at and interleave_at[k] != SHARED:
                     ws_interleave(interleave_at[k], g)
             ws_now = KG - (k in interleave_at)
             if k in quantise_at:

@@ -24,6 +24,7 @@ PASS = P * PACK
 BANK = 512
 BANKS = 8
 ALIGN = 256
+MOVING_ROW = 4
 KG = K // PASS
 MG = M // PASS
 
@@ -39,8 +40,8 @@ WS_LOADS = [(0, 512), (512, 256), (768, 256)]
 X_LOAD = [1, 1, 1]
 RATIO_RUN = 2
 COPY_RUN = 4
-ROOT_SCALAR = {1: 128, 2: 352}
-ROOT_SCALAR_LONG = 192
+ROOT_SCALAR = {1: 64, 2: 256}
+ROOT_SCALAR_LONG = 128
 ROUND_SCALAR = 80
 WIDEN_VECTOR = 3
 WS_AHEAD = 3
@@ -159,7 +160,7 @@ def tile_monopulse_ratio_matrix_s11_kernel(tc, x, ws_bytes, ws_scale, wd_words, 
         def ws_quantise(j, g0=0, g1=KG):
             n = P * WIDTHS[j]
             nc.vector.quantize_mx(
-                out=ws_codes[j][:, g0 * n : g1 * n].bitcast(FP8X4), scales=ws_planes[j][:, g0 * n : g1 * n],
+                out=ws_codes[j][:, g0 * n : g1 * n].bitcast(FP8X4), scales=ws_planes[j][MOVING_ROW:, g0 * n : g1 * n],
                 in_=ws_grouped[j % 2][:, g0 * n * PACK : g1 * n * PACK],
             )
 
@@ -221,7 +222,7 @@ def tile_monopulse_ratio_matrix_s11_kernel(tc, x, ws_bytes, ws_scale, wd_words, 
             j, gm = ORDER[u]
             n = KG * P * WIDTHS[j]
             codes = ws_codes[j][:, :n].rearrange("p (g n) -> p g n", g=KG)
-            planes = ws_planes[j][:, :n].rearrange("p (g n) -> p g n", g=KG)
+            planes = ws_planes[j][MOVING_ROW:, :n].rearrange("p (g n) -> p g n", g=KG)
             for h in beam_tiles(u):
                 project(("s", u, h), gm, codes, planes, h * P, 1, FP8X4)
 
@@ -278,10 +279,10 @@ def tile_monopulse_ratio_matrix_s11_kernel(tc, x, ws_bytes, ws_scale, wd_words, 
             )
             give(("d", u, h))
 
-        def quantise(src, u, codes, planes):
+        def quantise(src, u, codes, planes, row=0):
             j, gm = ORDER[u]
             cols = slice(FIRST[j] * P, FIRST[j + 1] * P)
-            nc.vector.quantize_mx(out=codes[gm][:, cols].bitcast(FP8X4), scales=planes[gm][:, cols], in_=src)
+            nc.vector.quantize_mx(out=codes[gm][:, cols].bitcast(FP8X4), scales=planes[gm][row:, cols], in_=src)
 
         def out_passes(piece):
             row, rows, c0, width = piece
@@ -292,7 +293,7 @@ def tile_monopulse_ratio_matrix_s11_kernel(tc, x, ws_bytes, ws_scale, wd_words, 
                     nc.tensor.matmul_mx(
                         out=held[piece][:, i * width : (i + 1) * width],
                         lhsT=r_codes[gm][:, r].bitcast(FP8X4), lhsT_scale=r_planes[gm][:, r],
-                        rhs=s_codes[gm][:, c0 : c0 + width].bitcast(FP8X4), rhs_scale=s_planes[gm][:, c0 : c0 + width],
+                        rhs=s_codes[gm][:, c0 : c0 + width].bitcast(FP8X4), rhs_scale=s_planes[gm][MOVING_ROW:, c0 : c0 + width],
                         start=(gm == 0), stop=(gm == MG - 1),
                     )
 
@@ -438,7 +439,7 @@ def tile_monopulse_ratio_matrix_s11_kernel(tc, x, ws_bytes, ws_scale, wd_words, 
             if has_r:
                 quantise(r16(k - LAG), k - LAG, r_codes, r_planes)
             if has_s:
-                quantise(s16(k), k, s_codes, s_planes)
+                quantise(s16(k), k, s_codes, s_planes, MOVING_ROW)
             if k in quantise_at and ws_now < KG:
                 ws_quantise(quantise_at[k], ws_now, KG)
             if has_x and not has_r:

@@ -24,7 +24,6 @@ PASS = P * PACK
 BANK = 512
 BANKS = 8
 ALIGN = 256
-MOVING_ROW = 4
 KG = K // PASS
 MG = M // PASS
 
@@ -42,7 +41,8 @@ RATIO_RUN = 2
 COPY_RUN = 4
 ROOT_SCALAR = {1: 64, 2: 256}
 ROOT_SCALAR_LONG = 128
-ROUND_SCALAR = 80
+ROUND_SCALAR = 112
+ROUND_SCALAR_NARROW = 64
 WIDEN_VECTOR = 3
 WS_AHEAD = 3
 WARM_UPS = 4
@@ -80,7 +80,7 @@ def tile_monopulse_ratio_matrix_s11_kernel(tc, x, ws_bytes, ws_scale, wd_words, 
         square = tiles("square", 2, [P, PACK * WIDE], F32)
         root = tiles("root", 2, [P, PACK * WIDE], F32)
         ring = tiles("ring", LAG + 1, [P, 2 * WIDE * PACK], BF16)
-        s_rounded = tiles("s_rounded", 2, [P, WIDE * PACK], BF16)
+        s_rounded = tiles("s_rounded", 3, [P, WIDE * PACK], BF16)
         result = tiles("result", RESULTS, [P, BANK], F32)
         ident = keep.tile([P, P], F32, name="ident")
         one = keep.tile([P, 1], F32, name="one")
@@ -157,11 +157,10 @@ def tile_monopulse_ratio_matrix_s11_kernel(tc, x, ws_bytes, ws_scale, wd_words, 
             else:
                 nc.vector.tensor_copy(out=dst, in_=src)
 
-        def ws_quantise(j, g0=0, g1=KG):
-            n = P * WIDTHS[j]
+        def ws_quantise(j):
+            n = KG * P * WIDTHS[j]
             nc.vector.quantize_mx(
-                out=ws_codes[j][:, g0 * n : g1 * n].bitcast(FP8X4), scales=ws_planes[j][MOVING_ROW:, g0 * n : g1 * n],
-                in_=ws_grouped[j % 2][:, g0 * n * PACK : g1 * n * PACK],
+                out=ws_codes[j][:, :n].bitcast(FP8X4), scales=ws_planes[j][:, :n], in_=ws_grouped[j % 2][:, : n * PACK]
             )
 
         def x_transpose(gm, t):
@@ -222,7 +221,7 @@ def tile_monopulse_ratio_matrix_s11_kernel(tc, x, ws_bytes, ws_scale, wd_words, 
             j, gm = ORDER[u]
             n = KG * P * WIDTHS[j]
             codes = ws_codes[j][:, :n].rearrange("p (g n) -> p g n", g=KG)
-            planes = ws_planes[j][MOVING_ROW:, :n].rearrange("p (g n) -> p g n", g=KG)
+            planes = ws_planes[j][:, :n].rearrange("p (g n) -> p g n", g=KG)
             for h in beam_tiles(u):
                 project(("s", u, h), gm, codes, planes, h * P, 1, FP8X4)
 
@@ -233,7 +232,7 @@ def tile_monopulse_ratio_matrix_s11_kernel(tc, x, ws_bytes, ws_scale, wd_words, 
                 project(("d", u, h), gm, wd_codes[half], wd_planes[half], c0, 2, FP4X4)
 
         def s16(u):
-            return (ring[u] if u < LAG else s_rounded[u % 2])[:, : values(u)]
+            return (ring[u] if u < LAG else s_rounded[u % len(s_rounded)])[:, : values(u)]
 
         def r16(u):
             return ring[(u + LAG) % len(ring)][:, : values(u)]
@@ -253,8 +252,8 @@ def tile_monopulse_ratio_matrix_s11_kernel(tc, x, ws_bytes, ws_scale, wd_words, 
             dst = by_slot(square[u % 2][:, : values(u)])[:, :, h * P : (h + 1) * P]
             nc.scalar.activation(out=dst, in_=by_slot(held["s", u, h][:]), func=ACT.Square)
 
-        def inverse_root(u):
-            for t in range(PACK):
+        def inverse_root(u, t0, t1):
+            for t in range(t0, t1):
                 nc.scalar.activation(
                     out=by_slot(root[u % 2][:, : values(u)])[:, t, :], in_=by_slot(square[u % 2][:, : values(u)])[:, t, :],
                     func=ACT.Abs_reciprocal_sqrt, bias=noise_col[:, ORDER[u][1], t : t + 1],
@@ -279,10 +278,10 @@ def tile_monopulse_ratio_matrix_s11_kernel(tc, x, ws_bytes, ws_scale, wd_words, 
             )
             give(("d", u, h))
 
-        def quantise(src, u, codes, planes, row=0):
+        def quantise(src, u, codes, planes):
             j, gm = ORDER[u]
             cols = slice(FIRST[j] * P, FIRST[j + 1] * P)
-            nc.vector.quantize_mx(out=codes[gm][:, cols].bitcast(FP8X4), scales=planes[gm][row:, cols], in_=src)
+            nc.vector.quantize_mx(out=codes[gm][:, cols].bitcast(FP8X4), scales=planes[gm][:, cols], in_=src)
 
         def out_passes(piece):
             row, rows, c0, width = piece
@@ -293,7 +292,7 @@ def tile_monopulse_ratio_matrix_s11_kernel(tc, x, ws_bytes, ws_scale, wd_words, 
                     nc.tensor.matmul_mx(
                         out=held[piece][:, i * width : (i + 1) * width],
                         lhsT=r_codes[gm][:, r].bitcast(FP8X4), lhsT_scale=r_planes[gm][:, r],
-                        rhs=s_codes[gm][:, c0 : c0 + width].bitcast(FP8X4), rhs_scale=s_planes[gm][MOVING_ROW:, c0 : c0 + width],
+                        rhs=s_codes[gm][:, c0 : c0 + width].bitcast(FP8X4), rhs_scale=s_planes[gm][:, c0 : c0 + width],
                         start=(gm == 0), stop=(gm == MG - 1),
                     )
 
@@ -378,7 +377,10 @@ def tile_monopulse_ratio_matrix_s11_kernel(tc, x, ws_bytes, ws_scale, wd_words, 
             wide = has_s and len(beam_tiles(k)) == 2
             x_gm, x_t = divmod(PACK + 2 + 2 * k, PACK)
             has_x = x_gm < MG
-            split = ROUND_SCALAR if wide and not has_x else 0
+            split = 0
+            if has_s and not has_x:
+                split = ROUND_SCALAR if wide else ROUND_SCALAR_NARROW * (len(beam_tiles(k - LAG)) - 1)
+            s_order = list(beam_tiles(k))[:: 1 if k == 0 else -1] if has_s else []
             emptying = closed
             closed = [piece for piece in plan if ready(piece) < k][: 2 if wide else 1]
             plan = [piece for piece in plan if piece not in closed]
@@ -397,11 +399,10 @@ def tile_monopulse_ratio_matrix_s11_kernel(tc, x, ws_bytes, ws_scale, wd_words, 
             for slot in turned:
                 x_transpose(*slot)
             multiply()
-            if has_s:
-                for h in beam_tiles(k):
-                    s_square(k, h)
+            for h in s_order:
+                s_square(k, h)
             if has_r:
-                for h in beam_tiles(k - LAG):
+                for h in reversed(beam_tiles(k - LAG)):
                     ratio(k - LAG, h)
             multiply()
             if split:
@@ -409,20 +410,21 @@ def tile_monopulse_ratio_matrix_s11_kernel(tc, x, ws_bytes, ws_scale, wd_words, 
             for i, piece in enumerate(emptying):
                 store(piece, i % 2 == 1)
                 multiply()
-            if has_s:
-                for h in beam_tiles(k):
-                    s_round(k, h, split if h == 0 else 0, P, True)
-                    give(("s", k, h))
-                    multiply()
+            for h in s_order:
+                s_round(k, h, split if h == 0 else 0, P, True)
+                give(("s", k, h))
+                multiply()
             for slot in turned[1:]:
                 x_copy(*slot, True)
-            if 1 <= k <= UNITS:
-                root_square(k - 1, True)
             for slot in turned[:1]:
                 x_copy(*slot, False)
             multiply()
             if has_s:
-                inverse_root(k)
+                inverse_root(k, 0, 1)
+            if 1 <= k <= UNITS:
+                root_square(k - 1, True)
+            if has_s:
+                inverse_root(k, 1, PACK)
 
             if has_x and has_r:
                 x_quantise(x_gm, x_t, x_t + 2)
@@ -431,17 +433,14 @@ def tile_monopulse_ratio_matrix_s11_kernel(tc, x, ws_bytes, ws_scale, wd_words, 
                     ws_widen(widen_at[k], g, WIDEN_VECTOR)
                 if k in interleave_at and interleave_at[k] != SHARED:
                     ws_interleave(interleave_at[k], g)
-            ws_now = KG - (k in interleave_at)
-            if k in quantise_at:
-                ws_quantise(quantise_at[k], 0, ws_now)
             if has_x and not has_r:
                 x_quantise(x_gm, x_t, x_t + 1)
             if has_r:
                 quantise(r16(k - LAG), k - LAG, r_codes, r_planes)
+            if k in quantise_at:
+                ws_quantise(quantise_at[k])
             if has_s:
-                quantise(s16(k), k, s_codes, s_planes, MOVING_ROW)
-            if k in quantise_at and ws_now < KG:
-                ws_quantise(quantise_at[k], ws_now, KG)
+                quantise(s16(k), k, s_codes, s_planes)
             if has_x and not has_r:
                 x_quantise(x_gm, x_t + 1, x_t + 2)
             if has_s:

@@ -39,9 +39,9 @@ WS_LOADS = [(0, 512), (512, 256), (768, 256)]
 X_LOAD = [1, 1, 1]
 RATIO_RUN = 2
 COPY_RUN = 4
-ROOT_SCALAR = {1: 64, 2: 256}
+ROOT_SCALAR = {1: 64, 2: 224}
 ROOT_SCALAR_LONG = 128
-ROUND_SCALAR = 112
+ROUND_SCALAR = 96
 ROUND_SCALAR_NARROW = 64
 WIDEN_VECTOR = 3
 WS_AHEAD = 3
@@ -337,38 +337,39 @@ def tile_monopulse_ratio_matrix_s11_kernel(tc, x, ws_bytes, ws_scale, wd_words, 
         plan = plan + [(FIRST[NB - 1], 1, c0, LAST_WIDTH) for c0 in range(0, B, LAST_WIDTH)]
         plan = sorted(plan, key=ready)
 
-        quantise_at = {step_of[j, 0] - WS_AHEAD: j for j in range(SHARED, NB)}
+        quantise_at = {step_of[j, 0] - WS_AHEAD: j for j in range(SHARED + 1, NB)}
         interleave_at = {k - (j < NB - 1): j for k, j in quantise_at.items()}
-        widen_at = {k - 1: j for k, j in interleave_at.items() if j > SHARED}
+        widen_at = {k - 1: j for k, j in interleave_at.items()}
 
         ws_widen(0, 0, 2)
         ws_widen(1, 0, 2)
-        ws_widen(0, 1, 2)
+        ws_widen(0, 1, 3)
+        ws_widen(1, 1, 0)
         ws_interleave(0, 0)
         ws_interleave(0, 1)
-        ws_widen(1, 1, 2)
         warm_tensor(WARM_UPS)
         for t in range(PACK):
             x_transpose(0, t)
         x_copy(0, 0, False)
         x_copy(0, 1, False)
+        ws_interleave(1, 0)
         ws_quantise(0)
         x_copy(0, 2, False)
+        ws_interleave(1, 1)
         x_quantise(0, 0, 2)
         x_copy(0, 3, False)
         for t in range(3):
             x_transpose(1, t)
-        ws_interleave(1, 0)
+        x_copy(1, 0, False)
         x_quantise(0, 2, PACK)
-        project_s(0)
-        for t in range(3):
-            x_copy(1, t, False)
-        ws_widen(SHARED, 0, 0)
-        ws_interleave(1, 1)
-        x_quantise(1, 0, 2)
-        ws_quantise(1)
+        ws_widen(SHARED, 0, 1)
         ws_widen(SHARED, 1, PACK)
+        project_s(0)
+        x_copy(1, 1, False)
+        x_copy(1, 2, False)
+        ws_quantise(1)
         ws_interleave(SHARED, 0)
+        x_quantise(1, 0, 2)
         ws_interleave(SHARED, 1, True)
 
         closed = []
@@ -431,7 +432,7 @@ def tile_monopulse_ratio_matrix_s11_kernel(tc, x, ws_bytes, ws_scale, wd_words, 
             for g in range(KG):
                 if k in widen_at:
                     ws_widen(widen_at[k], g, WIDEN_VECTOR)
-                if k in interleave_at and interleave_at[k] != SHARED:
+                if k in interleave_at:
                     ws_interleave(interleave_at[k], g)
             if has_x and not has_r:
                 x_quantise(x_gm, x_t, x_t + 1)
@@ -443,6 +444,8 @@ def tile_monopulse_ratio_matrix_s11_kernel(tc, x, ws_bytes, ws_scale, wd_words, 
                 quantise(s16(k), k, s_codes, s_planes)
             if has_x and not has_r:
                 x_quantise(x_gm, x_t + 1, x_t + 2)
+            if k == 0:
+                ws_quantise(SHARED)
             if has_s:
                 long_read = k + 1 == LAG or len(closed) == 2
                 root_scalar[k] = ROOT_SCALAR_LONG if wide and long_read else ROOT_SCALAR[len(beam_tiles(k))]

@@ -27,24 +27,21 @@ ALIGN = 256
 KG = K // PASS
 MG = M // PASS
 
-WIDTHS = [2, 2, 2, 1, 1]
-NB = len(WIDTHS)
-FIRST = [sum(WIDTHS[:j]) for j in range(NB + 1)]
-WIDE = P * max(WIDTHS)
+NB = 4
+WIDE = B // NB
+HALVES = range(WIDE // P)
+VALUES = PACK * WIDE
 SHARED = 2
 ORDER = [(j, gm) for gm in range(MG) for j in range(SHARED)] + [(j, gm) for j in range(SHARED, NB) for gm in range(MG)]
 UNITS = len(ORDER)
+PAIRED = UNITS - MG
 LAG = 2
 WS_LOADS = [(0, 512), (512, 256), (768, 256)]
-X_LOAD = [1, 1, 1]
 RATIO_RUN = 2
 COPY_RUN = 4
-ROOT_SCALAR = {1: 64, 2: 224}
+ROOT_SCALAR = 288
 ROOT_SCALAR_LONG = 128
-ROUND_SCALAR = 96
-ROUND_SCALAR_NARROW = 64
-WIDEN_VECTOR = 3
-WS_AHEAD = 3
+ROUND_SCALAR = 112
 WARM_UPS = 4
 LAST_WIDTH = 256
 RESULTS = 8
@@ -60,7 +57,7 @@ def tile_monopulse_ratio_matrix_s11_kernel(tc, x, ws_bytes, ws_scale, wd_words, 
         def tiles(name, n, shape, dtype):
             return [keep.tile(shape, dtype, name="%s%d" % (name, i), align_bytes=ALIGN) for i in range(n)]
 
-        x_raw = [tiles("x_raw%d_" % gm, PACK // n, [P, n * K], BF16) for gm, n in enumerate(X_LOAD)]
+        x_raw = [tiles("x_raw%d_" % gm, PACK, [P, K], BF16) for gm in range(MG)]
         x_grouped = tiles("x_grouped", 2, [P, PACK, KG * P * PACK], BF16)
         x_codes = tiles("x_codes", MG, [P, PACK, KG, P], U32)
         x_planes = tiles("x_planes", MG, [P, PACK, KG, P], U8)
@@ -81,6 +78,8 @@ def tile_monopulse_ratio_matrix_s11_kernel(tc, x, ws_bytes, ws_scale, wd_words, 
         root = tiles("root", 2, [P, PACK * WIDE], F32)
         ring = tiles("ring", LAG + 1, [P, 2 * WIDE * PACK], BF16)
         s_rounded = tiles("s_rounded", 3, [P, WIDE * PACK], BF16)
+        s_pairs = tiles("s_pairs", 2, [P, VALUES], BF16)
+        r_pairs = tiles("r_pairs", 2, [P, VALUES], BF16)
         result = tiles("result", RESULTS, [P, BANK], F32)
         ident = keep.tile([P, P], F32, name="ident")
         one = keep.tile([P, 1], F32, name="one")
@@ -104,9 +103,8 @@ def tile_monopulse_ratio_matrix_s11_kernel(tc, x, ws_bytes, ws_scale, wd_words, 
                 nc.sync.dma_start(out=ws_raw[part][g][:], in_=ws_rows[g][:, :, c0 : c0 + n])
 
         def x_load(gm, first=0, last=PACK):
-            n = X_LOAD[gm]
-            for i, dst in list(enumerate(x_raw[gm]))[first:last]:
-                nc.sync.dma_start(out=dst[:], in_=x_rows[gm][:, n * i : n * (i + 1), :].rearrange("p t k -> p (t k)"))
+            for t in range(first, last):
+                nc.sync.dma_start(out=x_raw[gm][t][:], in_=x_rows[gm][:, t, :])
 
         def wd_load(half):
             cols = slice(half * B // 2, (half + 1) * B // 2)
@@ -137,37 +135,31 @@ def tile_monopulse_ratio_matrix_s11_kernel(tc, x, ws_bytes, ws_scale, wd_words, 
         nc.scalar.activation(out=warm[:], in_=one[:], func=ACT.Abs_reciprocal_sqrt)
 
         def ws_widen(j, g, vector_slots):
-            n = P * WIDTHS[j]
-            part = max(i for i, (first, beams) in enumerate(WS_LOADS) if first <= P * FIRST[j])
-            c0 = P * FIRST[j] - WS_LOADS[part][0]
+            part = max(i for i, (first, beams) in enumerate(WS_LOADS) if first <= WIDE * j)
+            c0 = WIDE * j - WS_LOADS[part][0]
             for t in range(PACK):
-                dst = ws_wide[KG * (j % 2) + g][:, t * n : (t + 1) * n]
-                src = ws_raw[part][g][:, t, c0 : c0 + n].bitcast(FP8)
+                dst = ws_wide[KG * (j % 2) + g][:, t * WIDE : (t + 1) * WIDE]
+                src = ws_raw[part][g][:, t, c0 : c0 + WIDE].bitcast(FP8)
                 if t < vector_slots:
                     nc.vector.tensor_scalar(out=dst, in0=src, scalar1=ws_factor[:, g, t : t + 1], scalar2=None, op0=MULT)
                 else:
                     nc.scalar.activation(out=dst, in_=src, func=ACT.Copy, scale=ws_factor[:, g, t : t + 1])
 
         def ws_interleave(j, g, on_gpsimd=False):
-            n = PACK * P * WIDTHS[j]
-            dst = ws_grouped[j % 2][:, g * n : (g + 1) * n].rearrange("p (c i t) -> p c t i", i=COPY_RUN, t=PACK)
-            src = ws_wide[KG * (j % 2) + g][:, :n].rearrange("p (t c i) -> p c t i", i=COPY_RUN, t=PACK)
+            dst = ws_grouped[j % 2][:, g * VALUES : (g + 1) * VALUES].rearrange("p (c i t) -> p c t i", i=COPY_RUN, t=PACK)
+            src = ws_wide[KG * (j % 2) + g][:].rearrange("p (t c i) -> p c t i", i=COPY_RUN, t=PACK)
             if on_gpsimd:
                 nc.gpsimd.tensor_scalar(out=dst, in0=src, scalar1=1.0, scalar2=0.0, op0=MULT, op1=ADD)
             else:
                 nc.vector.tensor_copy(out=dst, in_=src)
 
         def ws_quantise(j):
-            n = KG * P * WIDTHS[j]
-            nc.vector.quantize_mx(
-                out=ws_codes[j][:, :n].bitcast(FP8X4), scales=ws_planes[j][:, :n], in_=ws_grouped[j % 2][:, : n * PACK]
-            )
+            nc.vector.quantize_mx(out=ws_codes[j][:].bitcast(FP8X4), scales=ws_planes[j][:], in_=ws_grouped[j % 2][:])
 
         def x_transpose(gm, t):
             take(("x", gm, t))
             bank = held["x", gm, t][:].rearrange("p (g u r) -> p g u r", g=KG, u=2)
-            n = X_LOAD[gm]
-            words = x_raw[gm][t // n][:, t % n * K : (t % n + 1) * K].bitcast(F32)
+            words = x_raw[gm][t][:].bitcast(F32)
             for g in range(KG):
                 for u in range(2):
                     nc.tensor.transpose(bank[:, g, u, :], words[:, 2 * P * g + u : 2 * P * (g + 1) : 2], ident[:])
@@ -194,93 +186,99 @@ def tile_monopulse_ratio_matrix_s11_kernel(tc, x, ws_bytes, ws_scale, wd_words, 
                 nc.tensor.matmul(out=held["warm"][:, :P], lhsT=ident[:], rhs=ident[:], start=True, stop=True)
             give("warm")
 
-        def beam_tiles(u):
-            return range(WIDTHS[ORDER[u][0]])
+        def slots(u, h):
+            return range(2 * h, 2 * h + 2) if u >= PAIRED else range(PACK)
 
-        def values(u):
-            return PACK * P * WIDTHS[ORDER[u][0]]
+        def beams(u, h):
+            return range(WIDE) if u >= PAIRED else range(h * P, (h + 1) * P)
 
-        def by_slot(ap):
-            return ap.rearrange("p (t b) -> p t b", t=PACK)
+        def by_slot(ap, n=PACK):
+            return ap.rearrange("p (t b) -> p t b", t=n)
 
-        def by_beam(ap):
-            return ap.rearrange("p (b t) -> p b t", t=PACK)
+        def bank_of(kind, u, h):
+            return by_slot(held[kind, u, h][:], len(slots(u, h)))
 
-        def project(key, gm, codes, planes, c0, per_beam, dtype):
-            take(key)
-            for t in range(PACK):
-                for g in range(KG):
-                    nc.tensor.matmul_mx(
-                        out=by_slot(held[key][:])[:, t, :],
-                        lhsT=x_codes[gm][:, t, g].bitcast(FP8X4), lhsT_scale=x_planes[gm][:, t, g],
-                        rhs=codes[:, g, per_beam * c0 : per_beam * (c0 + P)].bitcast(dtype), rhs_scale=planes[:, g, c0 : c0 + P],
-                        start=(g == 0), stop=(g == KG - 1),
-                    )
+        def part_of(tile, u, h):
+            t, b = slots(u, h), beams(u, h)
+            return by_slot(tile)[:, t.start : t.stop, b.start : b.stop]
+
+        def side_by_side(whole, pairs, u, h):
+            if u >= PAIRED:
+                return pairs[u % 2][:, h * BANK : (h + 1) * BANK].rearrange("p (b t) -> p b t", t=2)
+            return whole.rearrange("p (b t) -> p b t", t=PACK)[:, h * P : (h + 1) * P, :]
+
+        def join(whole, pairs, u):
+            dst = whole.bitcast(F32).rearrange("p (b h) -> p b h", h=2)
+            nc.vector.tensor_copy(out=dst, in_=pairs[u % 2][:].bitcast(F32).rearrange("p (h b) -> p b h", h=2))
+
+        def project(kind, u, codes, planes, c0, per_beam, dtype):
+            for h in HALVES:
+                take((kind, u, h))
+                first, last = c0 + beams(u, h).start, c0 + beams(u, h).stop
+                for i, t in enumerate(slots(u, h)):
+                    for g in range(KG):
+                        nc.tensor.matmul_mx(
+                            out=bank_of(kind, u, h)[:, i, :],
+                            lhsT=x_codes[ORDER[u][1]][:, t, g].bitcast(FP8X4), lhsT_scale=x_planes[ORDER[u][1]][:, t, g],
+                            rhs=codes[:, g, per_beam * first : per_beam * last].bitcast(dtype), rhs_scale=planes[:, g, first:last],
+                            start=(g == 0), stop=(g == KG - 1),
+                        )
 
         def project_s(u):
-            j, gm = ORDER[u]
-            n = KG * P * WIDTHS[j]
-            codes = ws_codes[j][:, :n].rearrange("p (g n) -> p g n", g=KG)
-            planes = ws_planes[j][:, :n].rearrange("p (g n) -> p g n", g=KG)
-            for h in beam_tiles(u):
-                project(("s", u, h), gm, codes, planes, h * P, 1, FP8X4)
+            j = ORDER[u][0]
+            codes = ws_codes[j][:].rearrange("p (g n) -> p g n", g=KG)
+            project("s", u, codes, ws_planes[j][:].rearrange("p (g n) -> p g n", g=KG), 0, 1, FP8X4)
 
         def project_d(u):
-            j, gm = ORDER[u]
-            for h in beam_tiles(u):
-                half, c0 = divmod((FIRST[j] + h) * P, B // 2)
-                project(("d", u, h), gm, wd_codes[half], wd_planes[half], c0, 2, FP4X4)
+            half, c0 = divmod(ORDER[u][0] * WIDE, B // 2)
+            project("d", u, wd_codes[half], wd_planes[half], c0, 2, FP4X4)
 
         def s16(u):
-            return (ring[u] if u < LAG else s_rounded[u % len(s_rounded)])[:, : values(u)]
+            return (ring[u] if u < LAG else s_rounded[u % len(s_rounded)])[:, :VALUES]
 
         def r16(u):
-            return ring[(u + LAG) % len(ring)][:, : values(u)]
+            return ring[(u + LAG) % len(ring)][:, :VALUES]
 
         def reciprocal(u):
-            return ring[u % len(ring)][:].bitcast(F32)[:, : values(u)]
+            return ring[u % len(ring)][:].bitcast(F32)
 
         def s_round(u, h, b0, b1, on_vector):
-            dst = by_beam(s16(u))[:, h * P + b0 : h * P + b1, :]
-            src = by_slot(held["s", u, h][:]).rearrange("p t b -> p b t")[:, b0:b1, :]
+            dst = side_by_side(s16(u), s_pairs, u, h)[:, b0:b1, :]
+            src = bank_of("s", u, h).rearrange("p t b -> p b t")[:, b0:b1, :]
             if on_vector:
                 nc.vector.tensor_copy(out=dst, in_=src)
             else:
                 nc.scalar.copy(out=dst, in_=src)
 
         def s_square(u, h):
-            dst = by_slot(square[u % 2][:, : values(u)])[:, :, h * P : (h + 1) * P]
-            nc.scalar.activation(out=dst, in_=by_slot(held["s", u, h][:]), func=ACT.Square)
+            nc.scalar.activation(out=part_of(square[u % 2][:], u, h), in_=bank_of("s", u, h), func=ACT.Square)
 
         def inverse_root(u, t0, t1):
             for t in range(t0, t1):
                 nc.scalar.activation(
-                    out=by_slot(root[u % 2][:, : values(u)])[:, t, :], in_=by_slot(square[u % 2][:, : values(u)])[:, t, :],
+                    out=by_slot(root[u % 2][:])[:, t, :], in_=by_slot(square[u % 2][:])[:, t, :],
                     func=ACT.Abs_reciprocal_sqrt, bias=noise_col[:, ORDER[u][1], t : t + 1],
                 )
 
-        root_scalar = {}
-
         def root_square(u, on_scalar):
-            n = values(u) - root_scalar[u]
+            n = VALUES - (ROOT_SCALAR_LONG if u + 1 == LAG else VALUES // 2 if u + 1 == UNITS else ROOT_SCALAR)
             if on_scalar:
-                nc.scalar.activation(out=reciprocal(u)[:, n:], in_=root[u % 2][:, n : values(u)], func=ACT.Square)
+                nc.scalar.activation(out=reciprocal(u)[:, n:], in_=root[u % 2][:, n:], func=ACT.Square)
             else:
                 nc.gpsimd.tensor_tensor(out=reciprocal(u)[:, :n], in0=root[u % 2][:, :n], in1=root[u % 2][:, :n], op=MULT)
 
         def ratio(u, h):
-            cols = slice(h * P, (h + 1) * P)
             nc.vector.tensor_tensor(
-                out=by_beam(r16(u))[:, cols, :].rearrange("p (c i) t -> p c t i", i=RATIO_RUN),
-                in0=by_slot(held["d", u, h][:]).rearrange("p t (c i) -> p c t i", i=RATIO_RUN),
-                in1=by_slot(reciprocal(u))[:, :, cols].rearrange("p t (c i) -> p c t i", i=RATIO_RUN),
+                out=side_by_side(r16(u), r_pairs, u, h).rearrange("p (c i) t -> p c t i", i=RATIO_RUN),
+                in0=bank_of("d", u, h).rearrange("p t (c i) -> p c t i", i=RATIO_RUN),
+                in1=part_of(reciprocal(u), u, h).rearrange("p t (c i) -> p c t i", i=RATIO_RUN),
                 op=MULT,
             )
             give(("d", u, h))
 
         def quantise(src, u, codes, planes):
             j, gm = ORDER[u]
-            cols = slice(FIRST[j] * P, FIRST[j + 1] * P)
+            cols = slice(j * WIDE, (j + 1) * WIDE)
             nc.vector.quantize_mx(out=codes[gm][:, cols].bitcast(FP8X4), scales=planes[gm][:, cols], in_=src)
 
         def out_passes(piece):
@@ -321,25 +319,23 @@ def tile_monopulse_ratio_matrix_s11_kernel(tc, x, ws_bytes, ws_scale, wd_words, 
             return found
 
         step_of = {unit: u for u, unit in enumerate(ORDER)}
-        block_of = [j for j in range(NB) for h in range(WIDTHS[j])]
+
+        def deferred(u):
+            return PAIRED - LAG <= u <= PAIRED
 
         def ready(piece):
             row, rows, c0, width = piece
-            r_step = max(step_of[block_of[r], MG - 1] + LAG for r in range(row, row + rows))
-            s_step = max(step_of[block_of[c], MG - 1] for c in range(c0 // P, (c0 + width) // P))
-            return max(r_step, s_step)
+            r_step = step_of[(row + rows - 1) * P // WIDE, MG - 1] + LAG
+            s_step = step_of[(c0 + width - 1) // WIDE, MG - 1]
+            return max(r_step, s_step + deferred(s_step))
 
-        wide_tiles = FIRST[NB - 2]
-        plan = pieces(0, FIRST[SHARED], 0, FIRST[SHARED])
-        for j in range(SHARED, NB - 2):
-            plan = plan + pieces(0, FIRST[j], FIRST[j], FIRST[j + 1]) + pieces(FIRST[j], FIRST[j + 1], 0, FIRST[j + 1])
-        plan = plan + pieces(0, wide_tiles, wide_tiles, FIRST[NB]) + pieces(wide_tiles, FIRST[NB - 1], 0, FIRST[NB])
-        plan = plan + [(FIRST[NB - 1], 1, c0, LAST_WIDTH) for c0 in range(0, B, LAST_WIDTH)]
+        tiles_to = [j * len(HALVES) for j in range(NB + 1)]
+        plan = pieces(0, tiles_to[SHARED], 0, tiles_to[SHARED])
+        for j in range(SHARED, NB):
+            t0, t1 = tiles_to[j], tiles_to[j + 1]
+            plan = plan + pieces(0, t0, t0, t1) + pieces(t0, t1 - (j == NB - 1), 0, t1)
+        plan = plan + [(tiles_to[NB] - 1, 1, c0, LAST_WIDTH) for c0 in range(0, B, LAST_WIDTH)]
         plan = sorted(plan, key=ready)
-
-        quantise_at = {step_of[j, 0] - WS_AHEAD: j for j in range(SHARED + 1, NB)}
-        interleave_at = {k - (j < NB - 1): j for k, j in quantise_at.items()}
-        widen_at = {k - 1: j for k, j in interleave_at.items()}
 
         ws_widen(0, 0, 2)
         ws_widen(1, 0, 2)
@@ -375,21 +371,19 @@ def tile_monopulse_ratio_matrix_s11_kernel(tc, x, ws_bytes, ws_scale, wd_words, 
         closed = []
         for k in range(UNITS + LAG + 1):
             has_s, has_r = k < UNITS, LAG <= k < UNITS + LAG
-            wide = has_s and len(beam_tiles(k)) == 2
             x_gm, x_t = divmod(PACK + 2 + 2 * k, PACK)
             has_x = x_gm < MG
-            split = 0
-            if has_s and not has_x:
-                split = ROUND_SCALAR if wide else ROUND_SCALAR_NARROW * (len(beam_tiles(k - LAG)) - 1)
-            s_order = list(beam_tiles(k))[:: 1 if k == 0 else -1] if has_s else []
+            split = 0 if has_x else WIDE if k >= PAIRED else ROUND_SCALAR
+            s_order = list(HALVES)[:: 1 if k == 0 else -1] if has_s else []
             emptying = closed
-            closed = [piece for piece in plan if ready(piece) < k][: 2 if wide else 1]
+            s_leads = k + 1 < UNITS and k + 1 != PAIRED
+            closed = [piece for piece in plan if ready(piece) < k][: 1 if s_leads else 2 if has_s else None]
             plan = [piece for piece in plan if piece not in closed]
 
-            s_work = [(len(beam_tiles(k + 1)), project_s, k + 1)] if k + 1 < UNITS else []
-            d_work = [(len(beam_tiles(k + 1 - LAG)), project_d, k + 1 - LAG)] if 0 <= k + 1 - LAG < UNITS else []
+            s_work = [(len(HALVES), project_s, k + 1)] if k + 1 < UNITS else []
+            d_work = [(len(HALVES), project_d, k + 1 - LAG)] if 0 <= k + 1 - LAG < UNITS else []
             o_work = [(1, out_passes, piece) for piece in closed]
-            todo = s_work + o_work + d_work if wide else s_work + d_work + o_work
+            todo = s_work + o_work + d_work if s_leads else o_work + d_work + s_work if has_s else d_work + o_work
 
             def multiply():
                 while todo and todo[0][0] <= len(free):
@@ -403,18 +397,22 @@ def tile_monopulse_ratio_matrix_s11_kernel(tc, x, ws_bytes, ws_scale, wd_words, 
             for h in s_order:
                 s_square(k, h)
             if has_r:
-                for h in reversed(beam_tiles(k - LAG)):
+                for h in reversed(HALVES):
                     ratio(k - LAG, h)
             multiply()
-            if split:
+            if has_s and split:
                 s_round(k, 0, 0, split, False)
-            for i, piece in enumerate(emptying):
-                store(piece, i % 2 == 1)
+                if split == len(beams(k, 0)):
+                    give(("s", k, 0))
+                    multiply()
+            for piece in emptying:
+                store(piece, PAIRED <= k < UNITS - 1)
                 multiply()
             for h in s_order:
-                s_round(k, h, split if h == 0 else 0, P, True)
-                give(("s", k, h))
-                multiply()
+                if ("s", k, h) in held:
+                    s_round(k, h, split if h == 0 else 0, len(beams(k, h)), True)
+                    give(("s", k, h))
+                    multiply()
             for slot in turned[1:]:
                 x_copy(*slot, True)
             for slot in turned[:1]:
@@ -430,30 +428,34 @@ def tile_monopulse_ratio_matrix_s11_kernel(tc, x, ws_bytes, ws_scale, wd_words, 
             if has_x and has_r:
                 x_quantise(x_gm, x_t, x_t + 2)
             for g in range(KG):
-                if k in widen_at:
-                    ws_widen(widen_at[k], g, WIDEN_VECTOR)
-                if k in interleave_at:
-                    ws_interleave(interleave_at[k], g)
+                if k == PAIRED - 5 + g:
+                    ws_widen(NB - 1, g, PACK)
+                if k == PAIRED - 3 + g:
+                    ws_interleave(NB - 1, g)
             if has_x and not has_r:
                 x_quantise(x_gm, x_t, x_t + 1)
+            if has_r and k - LAG >= PAIRED:
+                join(r16(k - LAG), r_pairs, k - LAG)
+            if 1 <= k <= UNITS and deferred(k - 1):
+                quantise(s16(k - 1), k - 1, s_codes, s_planes)
+            if has_s and k >= PAIRED:
+                join(s16(k), s_pairs, k)
             if has_r:
                 quantise(r16(k - LAG), k - LAG, r_codes, r_planes)
-            if k in quantise_at:
-                ws_quantise(quantise_at[k])
-            if has_s:
+            if k == PAIRED - 2:
+                ws_quantise(NB - 1)
+            if has_s and not deferred(k):
                 quantise(s16(k), k, s_codes, s_planes)
             if has_x and not has_r:
                 x_quantise(x_gm, x_t + 1, x_t + 2)
             if k == 0:
                 ws_quantise(SHARED)
             if has_s:
-                long_read = k + 1 == LAG or len(closed) == 2
-                root_scalar[k] = ROOT_SCALAR_LONG if wide and long_read else ROOT_SCALAR[len(beam_tiles(k))]
                 root_square(k, False)
             assert not todo
         for piece in closed:
-            store(piece, len(stored) % 2 == 0)
+            store(piece, False)
         for piece in plan:
             out_passes(piece)
-            store(piece, len(stored) % 2 == 0)
+            store(piece, len(stored) % 2 == 1)
         assert sum(rows * width for row, rows, c0, width in stored) * P == B * B

from contextlib import ExitStack

import concourse.mybir as mybir
from concourse.masks import make_identity

M, K, B = 1536, 1024, 1024
FLOPS = 3 * 2 * M * K * B

F32 = mybir.dt.float32
BF16 = mybir.dt.bfloat16
I32 = mybir.dt.int32
U32 = mybir.dt.uint32
U8 = mybir.dt.uint8
FP8 = mybir.dt.float8_e4m3fn
FP8X4 = mybir.dt.float8_e4m3fn_x4
FP4X4 = mybir.dt.float4_e2m1fn_x4
ACT = mybir.ActivationFunctionType
MULT = mybir.AluOpType.mult
ADD = mybir.AluOpType.add

P = 128
PACK = 4
PASS = P * PACK
BANK = 512
BANKS = 8
ALIGN = 256
KG = K // PASS
MG = M // PASS

NB = 4
WIDE = B // NB
HALVES = range(WIDE // P)
VALUES = PACK * WIDE
SHARED = 2
ORDER = [(j, gm) for gm in range(MG) for j in range(SHARED)] + [(j, gm) for j in range(SHARED, NB) for gm in range(MG)]
UNITS = len(ORDER)
PAIRED = UNITS - MG
LAG = 2
WS_LOADS = [(0, 512), (512, 256), (768, 256)]
RATIO_RUN = 2
COPY_RUN = 4
ROOT_SCALAR = 288
ROOT_SCALAR_LONG = 128
ROUND_SCALAR = 112
WARM_UPS = 4
LAST_WIDTH = 256
RESULTS = 8


def tile_monopulse_ratio_matrix_s11_kernel(tc, x, ws_bytes, ws_scale, wd_words, wd_scales, noise, out):
    nc = tc.nc
    with ExitStack() as ctx:
        keep = ctx.enter_context(tc.tile_pool(name="keep", bufs=1))
        psum = ctx.enter_context(tc.psum_pool(name="psum", bufs=1))
        ctx.enter_context(tc.manual_schedule())

        def tiles(name, n, shape, dtype):
            return [keep.tile(shape, dtype, name="%s%d" % (name, i), align_bytes=ALIGN) for i in range(n)]

        x_raw = [tiles("x_raw%d_" % gm, PACK, [P, K], BF16) for gm in range(MG)]
        x_grouped = tiles("x_grouped", 2, [P, PACK, KG * P * PACK], BF16)
        x_codes = tiles("x_codes", MG, [P, PACK, KG, P], U32)
        x_planes = tiles("x_planes", MG, [P, PACK, KG, P], U8)
        ws_raw = [tiles("ws_raw%d_" % i, KG, [P, PACK, n], U8) for i, (c0, n) in enumerate(WS_LOADS)]
        ws_factor = keep.tile([P, KG, PACK], F32, name="ws_factor")
        ws_wide = tiles("ws_wide", 2 * KG, [P, PACK * WIDE], BF16)
        ws_grouped = tiles("ws_grouped", 2, [P, KG * WIDE * PACK], BF16)
        ws_codes = tiles("ws_codes", NB, [P, KG * WIDE], U32)
        ws_planes = tiles("ws_planes", NB, [P, KG * WIDE], U8)
        wd_codes = tiles("wd_codes", 2, [P, KG, B], U8)
        wd_planes = tiles("wd_planes", 2, [P, KG, B // 2], U8)
        noise_col = keep.tile([P, MG, PACK], BF16, name="noise_col")
        s_codes = tiles("s_codes", MG, [P, B], U32)
        s_planes = tiles("s_planes", MG, [P, B], U8)
        r_codes = tiles("r_codes", MG, [P, B], U32)
        r_planes = tiles("r_planes", MG, [P, B], U8)
        square = tiles("square", 2, [P, PACK * WIDE], F32)
        root = tiles("root", 2, [P, PACK * WIDE], F32)
        ring = tiles("ring", LAG + 1, [P, 2 * WIDE * PACK], BF16)
        s_rounded = tiles("s_rounded", 3, [P, WIDE * PACK], BF16)
        s_pairs = tiles("s_pairs", 2, [P, VALUES], BF16)
        r_pairs = tiles("r_pairs", 2, [P, VALUES], BF16)
        result = tiles("result", RESULTS, [P, BANK], F32)
        ident = keep.tile([P, P], F32, name="ident")
        one = keep.tile([P, 1], F32, name="one")
        warm = keep.tile([P, 1], F32, name="warm")

        free = [psum.tile([P, BANK], F32, name="bank%d" % i) for i in range(BANKS)]
        held = {}

        def take(key):
            held[key] = free.pop(0)

        def give(key):
            free.append(held.pop(key))

        ws_rows = ws_bytes.rearrange("(g p t) n -> g p t n", p=P, t=PACK)
        x_rows = x.rearrange("(g p t) k -> g p t k", p=P, t=PACK)

        def ws_load(part):
            c0, n = WS_LOADS[part]
            for g in range(KG):
                nc.sync.dma_start(out=ws_raw[part][g][:], in_=ws_rows[g][:, :, c0 : c0 + n])

        def x_load(gm, first=0, last=PACK):
            for t in range(first, last):
                nc.sync.dma_start(out=x_raw[gm][t][:], in_=x_rows[gm][:, t, :])

        def wd_load(half):
            cols = slice(half * B // 2, (half + 1) * B // 2)
            for q in range(4):
                nc.sync.dma_start(
                    out=wd_planes[half][32 * q : 32 * q + 4, :, :].bitcast(I32),
                    in_=wd_scales[:, 4 * q : 4 * q + 4, cols].rearrange("g r n -> r g n").bitcast(I32),
                )
            words = wd_words.rearrange("g p n -> p g n")
            nc.sync.dma_start(out=wd_codes[half][:], in_=words[:, :, half * B : (half + 1) * B])

        nc.scalar.dma_start(out=ws_factor[:], in_=ws_scale.rearrange("(g p t) o -> p g (t o)", p=P, t=PACK))
        nc.vector.memset(one[:], 1.0)
        for plane in wd_planes:
            nc.vector.memset(plane[:].rearrange("p g n -> p (g n)").bitcast(I32), 0)
        ws_load(0)
        x_load(0)
        x_load(1, 0, 3)
        ws_load(1)
        x_load(1, 3, 4)
        nc.sync.dma_start(out=noise_col[:], in_=noise.rearrange("(g p t) -> p g t", p=P, t=PACK))
        x_load(2, 0, 3)
        wd_load(0)
        x_load(2, 3, 4)
        ws_load(2)
        wd_load(1)
        make_identity(nc, ident[:])
        nc.scalar.activation(out=warm[:], in_=one[:], func=ACT.Abs_reciprocal_sqrt)

        def ws_widen(j, g, vector_slots):
            part = max(i for i, (first, beams) in enumerate(WS_LOADS) if first <= WIDE * j)
            c0 = WIDE * j - WS_LOADS[part][0]
            for t in range(PACK):
                dst = ws_wide[KG * (j % 2) + g][:, t * WIDE : (t + 1) * WIDE]
                src = ws_raw[part][g][:, t, c0 : c0 + WIDE].bitcast(FP8)
                if t < vector_slots:
                    nc.vector.tensor_scalar(out=dst, in0=src, scalar1=ws_factor[:, g, t : t + 1], scalar2=None, op0=MULT)
                else:
                    nc.scalar.activation(out=dst, in_=src, func=ACT.Copy, scale=ws_factor[:, g, t : t + 1])

        def ws_interleave(j, g, on_gpsimd=False):
            dst = ws_grouped[j % 2][:, g * VALUES : (g + 1) * VALUES].rearrange("p (c i t) -> p c t i", i=COPY_RUN, t=PACK)
            src = ws_wide[KG * (j % 2) + g][:].rearrange("p (t c i) -> p c t i", i=COPY_RUN, t=PACK)
            if on_gpsimd:
                nc.gpsimd.tensor_scalar(out=dst, in0=src, scalar1=1.0, scalar2=0.0, op0=MULT, op1=ADD)
            else:
                nc.vector.tensor_copy(out=dst, in_=src)

        def ws_quantise(j):
            nc.vector.quantize_mx(out=ws_codes[j][:].bitcast(FP8X4), scales=ws_planes[j][:], in_=ws_grouped[j % 2][:])

        def x_transpose(gm, t):
            take(("x", gm, t))
            bank = held["x", gm, t][:].rearrange("p (g u r) -> p g u r", g=KG, u=2)
            words = x_raw[gm][t][:].bitcast(F32)
            for g in range(KG):
                for u in range(2):
                    nc.tensor.transpose(bank[:, g, u, :], words[:, 2 * P * g + u : 2 * P * (g + 1) : 2], ident[:])

        def x_copy(gm, t, on_vector):
            dst = x_grouped[gm % 2][:, t, :].bitcast(F32).rearrange("p (g r u) -> p g r u", g=KG, u=2)
            src = held["x", gm, t][:].rearrange("p (g u r) -> p g r u", g=KG, u=2)
            if on_vector:
                nc.vector.tensor_copy(out=dst, in_=src)
            else:
                nc.scalar.copy(out=dst, in_=src)
            give(("x", gm, t))

        def x_quantise(gm, t0, t1):
            nc.vector.quantize_mx(
                out=x_codes[gm][:, t0:t1].rearrange("p t g r -> p (t g r)").bitcast(FP8X4),
                scales=x_planes[gm][:, t0:t1].rearrange("p t g r -> p (t g r)"),
                in_=x_grouped[gm % 2][:, t0:t1].rearrange("p t n -> p (t n)"),
            )

        def warm_tensor(n):
            take("warm")
            for i in range(n):
                nc.tensor.matmul(out=held["warm"][:, :P], lhsT=ident[:], rhs=ident[:], start=True, stop=True)
            give("warm")

        def slots(u, h):
            return range(2 * h, 2 * h + 2) if u >= PAIRED else range(PACK)

        def beams(u, h):
            return range(WIDE) if u >= PAIRED else range(h * P, (h + 1) * P)

        def by_slot(ap, n=PACK):
            return ap.rearrange("p (t b) -> p t b", t=n)

        def bank_of(kind, u, h):
            return by_slot(held[kind, u, h][:], len(slots(u, h)))

        def part_of(tile, u, h):
            t, b = slots(u, h), beams(u, h)
            return by_slot(tile)[:, t.start : t.stop, b.start : b.stop]

        def side_by_side(whole, pairs, u, h):
            if u >= PAIRED:
                return pairs[u % 2][:, h * BANK : (h + 1) * BANK].rearrange("p (b t) -> p b t", t=2)
            return whole.rearrange("p (b t) -> p b t", t=PACK)[:, h * P : (h + 1) * P, :]

        def join(whole, pairs, u):
            dst = whole.bitcast(F32).rearrange("p (b h) -> p b h", h=2)
            nc.vector.tensor_copy(out=dst, in_=pairs[u % 2][:].bitcast(F32).rearrange("p (h b) -> p b h", h=2))

        def project(kind, u, codes, planes, c0, per_beam, dtype):
            for h in HALVES:
                take((kind, u, h))
                first, last = c0 + beams(u, h).start, c0 + beams(u, h).stop
                for i, t in enumerate(slots(u, h)):
                    for g in range(KG):
                        nc.tensor.matmul_mx(
                            out=bank_of(kind, u, h)[:, i, :],
                            lhsT=x_codes[ORDER[u][1]][:, t, g].bitcast(FP8X4), lhsT_scale=x_planes[ORDER[u][1]][:, t, g],
                            rhs=codes[:, g, per_beam * first : per_beam * last].bitcast(dtype), rhs_scale=planes[:, g, first:last],
                            start=(g == 0), stop=(g == KG - 1),
                        )

        def project_s(u):
            j = ORDER[u][0]
            codes = ws_codes[j][:].rearrange("p (g n) -> p g n", g=KG)
            project("s", u, codes, ws_planes[j][:].rearrange("p (g n) -> p g n", g=KG), 0, 1, FP8X4)

        def project_d(u):
            half, c0 = divmod(ORDER[u][0] * WIDE, B // 2)
            project("d", u, wd_codes[half], wd_planes[half], c0, 2, FP4X4)

        def s16(u):
            return (ring[u] if u < LAG else s_rounded[u % len(s_rounded)])[:, :VALUES]

        def r16(u):
            return ring[(u + LAG) % len(ring)][:, :VALUES]

        def reciprocal(u):
            return ring[u % len(ring)][:].bitcast(F32)

        def s_round(u, h, b0, b1, on_vector):
            dst = side_by_side(s16(u), s_pairs, u, h)[:, b0:b1, :]
            src = bank_of("s", u, h).rearrange("p t b -> p b t")[:, b0:b1, :]
            if on_vector:
                nc.vector.tensor_copy(out=dst, in_=src)
            else:
                nc.scalar.copy(out=dst, in_=src)

        def s_square(u, h):
            nc.scalar.activation(out=part_of(square[u % 2][:], u, h), in_=bank_of("s", u, h), func=ACT.Square)

        def inverse_root(u, t0, t1):
            for t in range(t0, t1):
                nc.scalar.activation(
                    out=by_slot(root[u % 2][:])[:, t, :], in_=by_slot(square[u % 2][:])[:, t, :],
                    func=ACT.Abs_reciprocal_sqrt, bias=noise_col[:, ORDER[u][1], t : t + 1],
                )

        def root_square(u, on_scalar):
            n = VALUES - (ROOT_SCALAR_LONG if u + 1 == LAG else VALUES // 2 if u + 1 == UNITS else ROOT_SCALAR)
            if on_scalar:
                nc.scalar.activation(out=reciprocal(u)[:, n:], in_=root[u % 2][:, n:], func=ACT.Square)
            else:
                nc.gpsimd.tensor_tensor(out=reciprocal(u)[:, :n], in0=root[u % 2][:, :n], in1=root[u % 2][:, :n], op=MULT)

        def ratio(u, h):
            nc.vector.tensor_tensor(
                out=side_by_side(r16(u), r_pairs, u, h).rearrange("p (c i) t -> p c t i", i=RATIO_RUN),
                in0=bank_of("d", u, h).rearrange("p t (c i) -> p c t i", i=RATIO_RUN),
                in1=part_of(reciprocal(u), u, h).rearrange("p t (c i) -> p c t i", i=RATIO_RUN),
                op=MULT,
            )
            give(("d", u, h))

        def quantise(src, u, codes, planes):
            j, gm = ORDER[u]
            cols = slice(j * WIDE, (j + 1) * WIDE)
            nc.vector.quantize_mx(out=codes[gm][:, cols].bitcast(FP8X4), scales=planes[gm][:, cols], in_=src)

        def out_passes(piece):
            row, rows, c0, width = piece
            take(piece)
            for i in range(rows):
                r = slice((row + i) * P, (row + i + 1) * P)
                for gm in range(MG):
                    nc.tensor.matmul_mx(
                        out=held[piece][:, i * width : (i + 1) * width],
                        lhsT=r_codes[gm][:, r].bitcast(FP8X4), lhsT_scale=r_planes[gm][:, r],
                        rhs=s_codes[gm][:, c0 : c0 + width].bitcast(FP8X4), rhs_scale=s_planes[gm][:, c0 : c0 + width],
                        start=(gm == 0), stop=(gm == MG - 1),
                    )

        stored = []

        def store(piece, on_vector):
            row, rows, c0, width = piece
            res = result[len(stored) % RESULTS][:, : rows * width]
            stored.append(piece)
            if on_vector:
                nc.vector.tensor_copy(out=res, in_=held[piece][:, : rows * width])
            else:
                nc.scalar.copy(out=res, in_=held[piece][:, : rows * width])
            give(piece)
            nc.sync.dma_start(
                out=out[row * P : (row + rows) * P, c0 : c0 + width].rearrange("(i p) c -> p i c", p=P),
                in_=res.rearrange("p (i c) -> p i c", i=rows),
            )

        def pieces(r0, r1, c0, c1):
            found = []
            while c0 < c1:
                w = max(n for n in (1, 2, 4) if n <= c1 - c0)
                found = found + [(r, min(4 // w, r1 - r), c0 * P, w * P) for r in range(r0, r1, 4 // w)]
                c0 = c0 + w
            return found

        step_of = {unit: u for u, unit in enumerate(ORDER)}

        def deferred(u):
            return PAIRED - LAG <= u <= PAIRED

        def ready(piece):
            row, rows, c0, width = piece
            r_step = step_of[(row + rows - 1) * P // WIDE, MG - 1] + LAG
            s_step = step_of[(c0 + width - 1) // WIDE, MG - 1]
            return max(r_step, s_step + deferred(s_step))

        tiles_to = [j * len(HALVES) for j in range(NB + 1)]
        plan = pieces(0, tiles_to[SHARED], 0, tiles_to[SHARED])
        for j in range(SHARED, NB):
            t0, t1 = tiles_to[j], tiles_to[j + 1]
            plan = plan + pieces(0, t0, t0, t1) + pieces(t0, t1 - (j == NB - 1), 0, t1)
        plan = plan + [(tiles_to[NB] - 1, 1, c0, LAST_WIDTH) for c0 in range(0, B, LAST_WIDTH)]
        plan = sorted(plan, key=ready)

        ws_widen(0, 0, 2)
        ws_widen(1, 0, 2)
        ws_widen(0, 1, 3)
        ws_widen(1, 1, 0)
        ws_interleave(0, 0)
        ws_interleave(0, 1)
        warm_tensor(WARM_UPS)
        for t in range(PACK):
            x_transpose(0, t)
        x_copy(0, 0, False)
        x_copy(0, 1, False)
        ws_interleave(1, 0)
        ws_quantise(0)
        x_copy(0, 2, False)
        ws_interleave(1, 1)
        x_quantise(0, 0, 2)
        x_copy(0, 3, False)
        for t in range(3):
            x_transpose(1, t)
        x_copy(1, 0, False)
        x_quantise(0, 2, PACK)
        ws_widen(SHARED, 0, 1)
        ws_widen(SHARED, 1, PACK)
        project_s(0)
        x_copy(1, 1, False)
        x_copy(1, 2, False)
        ws_quantise(1)
        ws_interleave(SHARED, 0)
        x_quantise(1, 0, 2)
        ws_interleave(SHARED, 1, True)

        closed = []
        for k in range(UNITS + LAG + 1):
            has_s, has_r = k < UNITS, LAG <= k < UNITS + LAG
            x_gm, x_t = divmod(PACK + 2 + 2 * k, PACK)
            has_x = x_gm < MG
            split = 0 if has_x else WIDE if k >= PAIRED else ROUND_SCALAR
            s_order = list(HALVES)[:: 1 if k == 0 else -1] if has_s else []
            emptying = closed
            s_leads = k + 1 < UNITS and k + 1 != PAIRED
            closed = [piece for piece in plan if ready(piece) < k][: 1 if s_leads else 2 if has_s else None]
            plan = [piece for piece in plan if piece not in closed]

            s_work = [(len(HALVES), project_s, k + 1)] if k + 1 < UNITS else []
            d_work = [(len(HALVES), project_d, k + 1 - LAG)] if 0 <= k + 1 - LAG < UNITS else []
            o_work = [(1, out_passes, piece) for piece in closed]
            todo = s_work + o_work + d_work if s_leads else o_work + d_work + s_work if has_s else d_work + o_work

            def multiply():
                while todo and todo[0][0] <= len(free):
                    banks, call, argument = todo.pop(0)
                    call(argument)

            turned = [divmod(n, PACK) for n in (PACK + 3 + 2 * k, PACK + 4 + 2 * k) if n < MG * PACK]
            for slot in turned:
                x_transpose(*slot)
            multiply()
            for h in s_order:
                s_square(k, h)
            if has_r:
                for h in reversed(HALVES):
                    ratio(k - LAG, h)
            multiply()
            if has_s and split:
                s_round(k, 0, 0, split, False)
                if split == len(beams(k, 0)):
                    give(("s", k, 0))
                    multiply()
            for piece in emptying:
                store(piece, PAIRED <= k < UNITS - 1)
                multiply()
            for h in s_order:
                if ("s", k, h) in held:
                    s_round(k, h, split if h == 0 else 0, len(beams(k, h)), True)
                    give(("s", k, h))
                    multiply()
            for slot in turned[1:]:
                x_copy(*slot, True)
            for slot in turned[:1]:
                x_copy(*slot, False)
            multiply()
            if has_s:
                inverse_root(k, 0, 1)
            if 1 <= k <= UNITS:
                root_square(k - 1, True)
            if has_s:
                inverse_root(k, 1, PACK)

            if has_x and has_r:
                x_quantise(x_gm, x_t, x_t + 2)
            for g in range(KG):
                if k == PAIRED - 5 + g:
                    ws_widen(NB - 1, g, PACK)
                if k == PAIRED - 3 + g:
                    ws_interleave(NB - 1, g)
            if has_x and not has_r:
                x_quantise(x_gm, x_t, x_t + 1)
            if has_r and k - LAG >= PAIRED:
                join(r16(k - LAG), r_pairs, k - LAG)
            if 1 <= k <= UNITS and deferred(k - 1):
                quantise(s16(k - 1), k - 1, s_codes, s_planes)
            if has_s and k >= PAIRED:
                join(s16(k), s_pairs, k)
            if has_r:
                quantise(r16(k - LAG), k - LAG, r_codes, r_planes)
            if k == PAIRED - 2:
                ws_quantise(NB - 1)
            if has_s and not deferred(k):
                quantise(s16(k), k, s_codes, s_planes)
            if has_x and not has_r:
                x_quantise(x_gm, x_t + 1, x_t + 2)
            if k == 0:
                ws_quantise(SHARED)
            if has_s:
                root_square(k, False)
            assert not todo
        for piece in closed:
            store(piece, False)
        for piece in plan:
            out_passes(piece)
            store(piece, len(stored) % 2 == 1)
        assert sum(rows * width for row, rows, c0, width in stored) * P == B * B
